import numpy as np
import ml_dtypes


def mxq(x, axis, fmt="e4m3"):
    dtype, down = {"e4m3": (ml_dtypes.float8_e4m3fn, 7), "e5m2": (ml_dtypes.float8_e5m2, 14)}[fmt]
    v = np.moveaxis(np.asarray(x, np.float32).astype(ml_dtypes.bfloat16).astype(np.float64), axis, -1)
    blocks = v.reshape(v.shape[:-1] + (-1, 32))
    amax = np.abs(blocks).max(-1, keepdims=True)
    byte = np.maximum(np.where(amax > 0, np.frexp(amax)[1] - 1 + 127, 0) - down, 1)
    scale = np.exp2(byte - 127.0)
    codes = (blocks / scale).astype(np.float32).astype(dtype).astype(np.float64)
    return np.moveaxis((codes * scale).reshape(v.shape), -1, axis)


WIDE = False


def mx_kscale(k):
    if not WIDE:
        return np.ones(k)
    levels = np.array([10, -10, 5, -5, 0])
    if k % 512:
        return np.exp2(np.random.permutation(np.resize(levels, k // 32))).repeat(32)
    a = np.empty((k // 512, 16))
    for p in range(k // 512):
        a[p, :8] = np.random.permutation(np.resize(levels, 8))
        for g in range(8):
            far = levels[np.abs(levels - a[p, g]) >= 10]
            a[p, g + 8] = far[np.random.randint(len(far))]
    return np.exp2(a.ravel()).repeat(32)


def f64(x):
    return np.asarray(x).astype(np.float64)


def striped(idx):
    return np.tile(idx.reshape(-1, 16).T, (8, 1)).astype(np.uint16)


def unstriped(offs):
    return offs[:16].T.reshape(-1).astype(np.int64)


E2M1 = np.array([0.0, 0.5, 1.0, 1.5, 2.0, 3.0, 4.0, 6.0, -0.0, -0.5, -1.0, -1.5, -2.0, -3.0, -4.0, -6.0])


def pack_weight(w, fmt):
    k, n = w.shape
    w = f64(np.asarray(w, np.float32).astype(ml_dtypes.bfloat16)).reshape(k // 32, 32, n)
    amax = np.abs(w).max(1)
    if fmt == "e4m3":
        byte = np.frexp(amax)[1] - 1 + 127 - 7
    else:
        mant, ex = np.frexp(amax / 6.0)
        byte = np.where(mant > 0.5, ex, ex - 1) + 127
    byte = np.clip(np.where(amax > 0, byte, 1), 1, 254)
    scaled = (w * np.exp2(127.0 - byte)[:, None, :]).reshape(k, n).astype(np.float32)
    by_word = np.ascontiguousarray(scaled.reshape(k // 512, 128, 4, n).transpose(0, 1, 3, 2))
    if fmt == "e4m3":
        words = by_word.astype(ml_dtypes.float8_e4m3fn).view(np.uint8)
    else:
        c = by_word.astype(ml_dtypes.float4_e2m1fn).view(np.uint8) & 0xF
        words = (c[..., 0::2] | (c[..., 1::2] << 4)).reshape(k // 512, 128, 2 * n)
    return np.ascontiguousarray(words), np.ascontiguousarray(byte.astype(np.uint8).reshape(k // 512, 16, n))


def unpack_weight(words, scales, fmt):
    g, _, n = scales.shape
    words = np.ascontiguousarray(words).reshape(g, 128, n, -1)
    if fmt == "e4m3":
        vals = words.view(ml_dtypes.float8_e4m3fn).astype(np.float64)
    else:
        nib = np.empty((g, 128, n, 4), np.uint8)
        nib[..., 0::2] = words & 0xF
        nib[..., 1::2] = words >> 4
        vals = E2M1[nib]
    vals = vals * np.repeat(np.exp2(scales.astype(np.float64) - 127.0), 8, axis=1)[..., None]
    return vals.transpose(0, 1, 3, 2).reshape(g * 512, n)


def gelu(v):
    return 0.5 * v * (1.0 + np.tanh(np.sqrt(2.0 / np.pi) * (v + 0.044715 * v**3)))


K, T, S, P, H, N = 1536, 2048, 1024, 512, 1024, 512

def setup_inputs():
    n = np.random.standard_normal
    s = mx_kscale(K)[:, None]
    u = mx_kscale(H)[:, None]
    tab_words, tab_scales = pack_weight(n((K, T)) * s, "e4m3")
    w1 = n((K, H)) / np.sqrt(K) / s * u.T
    knee = np.exp(0.3 * n(H)) * u[:, 0]
    w2_words, w2_scales = pack_weight(2.0 * n((H, N)) / np.sqrt(H) / u, "e2m1")
    return {
        "tab_words": tab_words, "tab_scales": tab_scales,
        "offs": striped(np.random.permutation(T)[:S]),
        "w1": w1.astype(np.float32),
        "pos1": striped(np.random.permutation(S)[:P]),
        "pos2": striped(np.random.permutation(S)[:P]),
        "knee": knee.astype(np.float32),
        "w2_words": w2_words, "w2_scales": w2_scales,
    }

def reference(tab_words, tab_scales, offs, w1, pos1, pos2, knee, w2_words, w2_scales):
    v = unpack_weight(tab_words, tab_scales, "e4m3")[:, unstriped(offs)]
    h = mxq(f64(w1), 0, "e4m3").T @ v
    a = h[:, unstriped(pos1)]
    b = h[:, unstriped(pos2)]
    z = a * b / (f64(knee)[:, None] + np.abs(a))
    w2 = unpack_weight(w2_words, w2_scales, "e2m1")
    y = w2.T @ mxq(z, 0, "e4m3")
    return np.square(y)

@@ -1,0 +1,274 @@
+from contextlib import ExitStack
+
+import concourse.mybir as mybir
+
+K, T, S, P, H, N = 1536, 2048, 1024, 512, 1024, 512
+FLOPS = 2 * K * H * S + 2 * H * N * P
+
+F32 = mybir.dt.float32
+BF16 = mybir.dt.bfloat16
+I32 = mybir.dt.int32
+U32 = mybir.dt.uint32
+U16 = mybir.dt.uint16
+U8 = mybir.dt.uint8
+FP8X4 = mybir.dt.float8_e4m3fn_x4
+FP4X4 = mybir.dt.float4_e2m1fn_x4
+ACT = mybir.ActivationFunctionType
+MULT = mybir.AluOpType.mult
+
+PARTS = 128
+PACK = 4
+K_PASS = PARTS * PACK
+PASSES = K // K_PASS
+BLOCKS = H // K_PASS
+BANK = 512
+
+VECTOR_SHARE = {(0, 0): 0, (0, 1): 64, (0, 2): 84, (1, 0): 0, (1, 1): 0, (1, 2): 128}
+
+
+def tile_list_hit_segment_energy_kernel(
+    tc, tab_words, tab_scales, offs, w1, pos1, pos2, knee, w2_words, w2_scales, out
+):
+    nc = tc.nc
+    with ExitStack() as ctx:
+        keep = ctx.enter_context(tc.tile_pool(name="keep", bufs=1))
+        ring3 = ctx.enter_context(tc.tile_pool(name="ring3", bufs=3))
+        ring4 = ctx.enter_context(tc.tile_pool(name="ring4", bufs=4))
+        ring2 = ctx.enter_context(tc.tile_pool(name="ring2", bufs=2))
+        psum = ctx.enter_context(tc.psum_pool(name="psum", bufs=1))
+
+        offs_t = keep.tile([PARTS, S // 16], U16, name="offs_t")
+        pos1_t = keep.tile([PARTS, P // 16], U16, name="pos1_t")
+        pos2_t = keep.tile([PARTS, P // 16], U16, name="pos2_t")
+        knee_t = keep.tile([PARTS, BLOCKS, PACK], F32, name="knee_t")
+        tab = [keep.tile([PARTS, T], I32, name="tab%d" % a, align_bytes=64) for a in range(PASSES)]
+        tab_sc = keep.tile([PARTS, T], U8, name="tab_sc", align_bytes=64)
+        hit = [keep.tile([PARTS, S], U32, name="hit%d" % a, align_bytes=64) for a in range(PASSES)]
+        hit_sc = keep.tile([PARTS, S], U8, name="hit_sc", align_bytes=64)
+        raw = {}
+        w1_codes = {}
+        w1_sc = {}
+        for b in range(BLOCKS):
+            for a in range(PASSES):
+                raw[b, a] = keep.tile([PARTS, PACK, K_PASS], F32, name="raw%d%d" % (b, a), align_bytes=64)
+                w1_codes[b, a] = keep.tile([PARTS, K_PASS], U32, name="w1c%d%d" % (b, a), align_bytes=64)
+                w1_sc[b, a] = keep.tile([PARTS, K_PASS], U8, name="w1s%d%d" % (b, a), align_bytes=64)
+        w2_w = keep.tile([PARTS, BLOCKS, 2 * N], U8, name="w2_w", align_bytes=64)
+        w2_sc = keep.tile([PARTS, BLOCKS, N], U8, name="w2_sc", align_bytes=64)
+
+        def load_tab(a, pieces):
+            words = tab_words[a].rearrange("p t i -> p (t i)").bitcast(I32)
+            for c in range(pieces):
+                cols = slice(c * T // pieces, (c + 1) * T // pieces)
+                nc.sync.dma_start(out=tab[a][:, cols], in_=words[:, cols])
+
+        def load_w1(b, a, pieces=1):
+            rows = w1[a * K_PASS : (a + 1) * K_PASS, b * K_PASS : (b + 1) * K_PASS].rearrange("(p j) c -> p j c", j=PACK)
+            for c in range(pieces):
+                js = slice(c * PACK // pieces, (c + 1) * PACK // pieces)
+                nc.sync.dma_start(out=raw[b, a][:, js, :], in_=rows[:, js, :])
+
+        nc.vector.memset(tab_sc[:].bitcast(I32), 0)
+        nc.sync.dma_start(offs_t[:], offs)
+        load_tab(0, 1)
+        load_w1(0, 0)
+        nc.sync.dma_start(pos1_t[:], pos1)
+        for q in range(4):
+            nc.sync.dma_start(
+                out=tab_sc[32 * q : 32 * q + 4 * PASSES, :].bitcast(I32),
+                in_=tab_scales[:, 4 * q : 4 * q + 4, :].bitcast(I32),
+            )
+        for a in range(1, PASSES):
+            load_tab(a, 1)
+            load_w1(0, a)
+        nc.sync.dma_start(pos2_t[:], pos2)
+        nc.sync.dma_start(out=knee_t[:], in_=knee.rearrange("(b p t) -> p b t", b=BLOCKS, t=PACK))
+        for a in range(PASSES):
+            load_w1(1, a)
+        nc.vector.memset(w2_sc[:].rearrange("p b n -> p (b n)").bitcast(I32), 0)
+        nc.sync.dma_start(out=w2_w[:].bitcast(I32), in_=w2_words.rearrange("b p n -> p b n").bitcast(I32))
+        for q in range(4):
+            nc.sync.dma_start(
+                out=w2_sc[32 * q : 32 * q + 4, :, :].bitcast(I32),
+                in_=w2_scales[:, 4 * q : 4 * q + 4, :].rearrange("b r n -> r b n").bitcast(I32),
+            )
+
+        def gather_hits(a):
+            nc.vector.tensor_copy(hit[a][:], tab[a][:].bitcast(U32).indirect(offs_t[:]))
+
+        grouped = {}
+
+        def cast_w1(b, a):
+            g = ring3.tile([PARTS, PACK, PARTS, PACK], BF16, name="grouped", align_bytes=64)
+            grouped[b, a] = g
+            dst = g[:].rearrange("p t m j -> p m j t")
+            src = raw[b, a][:].rearrange("p j (m t) -> p m j t", t=PACK)
+            share = VECTOR_SHARE[b, a]
+            if share < PARTS:
+                nc.scalar.activation(dst[:, share:], src[:, share:], ACT.Copy)
+            if share > 0:
+                nc.vector.tensor_copy(dst[:, :share], src[:, :share])
+
+        def quantize_w1(b, a, t0=0, t1=PACK):
+            cols = slice(t0 * PARTS, t1 * PARTS)
+            nc.vector.quantize_mx(
+                out=w1_codes[b, a][:, cols].bitcast(FP8X4),
+                scales=w1_sc[b, a][:, cols],
+                in_=grouped[b, a][:, t0:t1].rearrange("p t m j -> p (t m j)"),
+            )
+
+        banks = {}
+
+        def h_pass(b, t, a):
+            for half in range(2):
+                if a == 0:
+                    banks[b, t, half] = psum.tile([PARTS, BANK], F32, name="bank%d" % (2 * t + half))
+                cols = slice(half * BANK, (half + 1) * BANK)
+                wcols = slice(t * PARTS, (t + 1) * PARTS)
+                nc.tensor.matmul_mx(
+                    out=banks[b, t, half][:],
+                    lhsT=w1_codes[b, a][:, wcols].bitcast(FP8X4),
+                    lhsT_scale=w1_sc[b, a][:, wcols],
+                    rhs=hit[a][:, cols].bitcast(FP8X4),
+                    rhs_scale=hit_sc[4 * a :, cols],
+                    start=(a == 0),
+                    stop=(a == PASSES - 1),
+                )
+
+        h_t = {}
+        a_t = {}
+        prod = {}
+        recip = {}
+        z_codes = {}
+        z_sc = {}
+
+        def evacuate(b, t):
+            h_t[b, t] = ring4.tile([PARTS, S], F32, name="h_t", align_bytes=64)
+            for half in range(2):
+                dst = h_t[b, t][:, half * BANK : (half + 1) * BANK]
+                if (b, t, half) == (0, 0, 1):
+                    nc.vector.tensor_copy(dst, banks[b, t, half][:])
+                else:
+                    nc.scalar.activation(dst, banks[b, t, half][:], ACT.Copy)
+
+        def gather_first(b, t):
+            a_t[b, t] = keep.tile([PARTS, P], F32, name="a_t%d%d" % (b, t), align_bytes=64)
+            nc.vector.tensor_copy(a_t[b, t][:], h_t[b, t][:].indirect(pos1_t[:]))
+
+        def gather_second(b, t):
+            if t == 0:
+                prod[b] = ring2.tile([PARTS, PACK, P], F32, name="prod", align_bytes=64)
+            nc.vector.tensor_tensor(prod[b][:, t, :], h_t[b, t][:].indirect(pos2_t[:]), a_t[b, t][:], MULT)
+
+        def saturate(b, t, j0=0, j1=P):
+            if t == 0:
+                recip[b] = ring2.tile([PARTS, PACK, P], F32, name="recip", align_bytes=64)
+            mag = ring2.tile([PARTS, P], F32, name="mag", align_bytes=64)
+            root = ring2.tile([PARTS, P], F32, name="root", align_bytes=64)
+            nc.scalar.activation(mag[:, j0:j1], a_t[b, t][:, j0:j1], ACT.Abs)
+            nc.scalar.activation(root[:, j0:j1], mag[:, j0:j1], ACT.Abs_reciprocal_sqrt, bias=knee_t[:, b, t : t + 1])
+            nc.scalar.activation(recip[b][:, t, j0:j1], root[:, j0:j1], ACT.Square)
+
+        z_bf = {}
+
+        def form_z(b, j0, j1):
+            if j0 == 0:
+                z_bf[b] = ring2.tile([PARTS, P, PACK], BF16, name="z_bf", align_bytes=64)
+            nc.vector.tensor_tensor(
+                z_bf[b][:, j0:j1, :].rearrange("p (c i) t -> p c t i", i=4),
+                prod[b][:, :, j0:j1].rearrange("p t (c i) -> p c t i", i=4),
+                recip[b][:, :, j0:j1].rearrange("p t (c i) -> p c t i", i=4),
+                MULT,
+            )
+
+        def quantize_z(b, j0, j1):
+            if j0 == 0:
+                z_codes[b] = ring2.tile([PARTS, P], U32, name="z_codes", align_bytes=64)
+                z_sc[b] = ring2.tile([PARTS, P], U8, name="z_sc", align_bytes=64)
+            nc.vector.quantize_mx(
+                out=z_codes[b][:, j0:j1].bitcast(FP8X4),
+                scales=z_sc[b][:, j0:j1],
+                in_=z_bf[b][:, j0:j1, :].rearrange("p j t -> p (j t)"),
+            )
+
+        y_bank = {}
+
+        def y_pass(b, c):
+            if b == 0:
+                y_bank[c] = psum.tile([PARTS, N // PARTS, PARTS], F32, name="bank%d" % c)
+            cols = slice(c * PARTS, (c + 1) * PARTS)
+            for n in range(N // PARTS):
+                nc.tensor.matmul_mx(
+                    out=y_bank[c][:, n, :],
+                    lhsT=w2_w[:, b, 2 * n * PARTS : 2 * (n + 1) * PARTS].bitcast(FP4X4),
+                    lhsT_scale=w2_sc[:, b, n * PARTS : (n + 1) * PARTS],
+                    rhs=z_codes[b][:, cols].bitcast(FP8X4),
+                    rhs_scale=z_sc[b][:, cols],
+                    start=(b == 0 and n == 0),
+                    stop=(b == BLOCKS - 1 and n == N // PARTS - 1),
+                )
+
+        def store(c):
+            energy = ring4.tile([PARTS, N // PARTS, PARTS], F32, name="energy", align_bytes=64)
+            nc.scalar.activation(energy[:], y_bank[c][:], ACT.Square)
+            nc.sync.dma_start(
+                out=out[:, c * PARTS : (c + 1) * PARTS].rearrange("(n p) j -> p n j", p=PARTS), in_=energy[:]
+            )
+
+        gather_hits(0)
+        nc.vector.tensor_copy(hit_sc[:], tab_sc[:].indirect(offs_t[:]))
+        for a in range(PASSES):
+            if a > 0:
+                gather_hits(a)
+            cast_w1(0, a)
+            if a < PASSES - 1:
+                quantize_w1(0, a)
+            else:
+                quantize_w1(0, a, 0, 1)
+                quantize_w1(0, a, 1, 2)
+                quantize_w1(0, a, 2, 4)
+            for t in range(PACK):
+                h_pass(0, t, a)
+
+        evacuate(0, 0)
+        for t in range(PACK - 1):
+            gather_first(0, t)
+            evacuate(0, t + 1)
+            cast_w1(1, t)
+            gather_second(0, t)
+            if t > 0:
+                quantize_w1(1, t - 1)
+        quantize_w1(1, PASSES - 1)
+        for t in range(PACK):
+            for a in range(PASSES):
+                h_pass(1, t, a)
+        gather_first(0, PACK - 1)
+        gather_second(0, PACK - 1)
+
+        saturate(0, 0)
+        saturate(0, 1)
+        evacuate(1, 0)
+        for t in range(PACK):
+            gather_first(1, t)
+            if t + 1 < PACK:
+                evacuate(1, t + 1)
+            if t + 2 < PACK:
+                saturate(0, t + 2)
+            gather_second(1, t)
+        form_z(0, 0, P)
+        quantize_z(0, 0, P)
+        for c in range(P // PARTS):
+            y_pass(0, c)
+        saturate(1, 0)
+        saturate(1, 1)
+        for half in range(2):
+            for t in range(2, PACK):
+                saturate(1, t, half * P // 2, (half + 1) * P // 2)
+        quarters = P // PARTS
+        for c in range(quarters + 1):
+            if c < quarters:
+                form_z(1, c * PARTS, (c + 1) * PARTS)
+            if c > 0:
+                quantize_z(1, (c - 1) * PARTS, c * PARTS)
+                y_pass(1, c - 1)
+                store(c - 1)

@@ -23,7 +23,8 @@ PASSES = K // K_PASS
 BLOCKS = H // K_PASS
 BANK = 512
 
-VECTOR_SHARE = {(0, 0): 0, (0, 1): 64, (0, 2): 84, (1, 0): 0, (1, 1): 0, (1, 2): 128}
+CAST_ON_VECTOR = {(0, 1, 0), (0, 2, 0), (1, 2, 2)}
+FZ = 1
 
 
 def tile_list_hit_segment_energy_kernel(
@@ -98,16 +99,15 @@ def tile_list_hit_segment_energy_kernel(
 
         grouped = {}
 
-        def cast_w1(b, a):
-            g = ring3.tile([PARTS, PACK, PARTS, PACK], BF16, name="grouped", align_bytes=64)
-            grouped[b, a] = g
-            dst = g[:].rearrange("p t m j -> p m j t")
-            src = raw[b, a][:].rearrange("p j (m t) -> p m j t", t=PACK)
-            share = VECTOR_SHARE[b, a]
-            if share < PARTS:
-                nc.scalar.activation(dst[:, share:], src[:, share:], ACT.Copy)
-            if share > 0:
-                nc.vector.tensor_copy(dst[:, :share], src[:, :share])
+        def cast_w1(b, a, t0=0, t1=PACK):
+            if (b, a) not in grouped:
+                grouped[b, a] = ring3.tile([PARTS, PACK, PARTS, PACK], BF16, name="grouped", align_bytes=64)
+            dst = grouped[b, a][:, t0:t1].rearrange("p t m j -> p m j t")
+            src = raw[b, a][:].rearrange("p j (m t) -> p m j t", t=PACK)[:, :, :, t0:t1]
+            if (b, a, t0) in CAST_ON_VECTOR:
+                nc.vector.tensor_copy(dst, src)
+            else:
+                nc.scalar.activation(dst, src, ACT.Copy)
 
         def quantize_w1(b, a, t0=0, t1=PACK):
             cols = slice(t0 * PARTS, t1 * PARTS)
@@ -160,14 +160,18 @@ def tile_list_hit_segment_energy_kernel(
                 prod[b] = ring2.tile([PARTS, PACK, P], F32, name="prod", align_bytes=64)
             nc.vector.tensor_tensor(prod[b][:, t, :], h_t[b, t][:].indirect(pos2_t[:]), a_t[b, t][:], MULT)
 
-        def saturate(b, t, j0=0, j1=P):
-            if t == 0:
+        def saturate(b, t0):
+            if t0 == 0:
                 recip[b] = ring2.tile([PARTS, PACK, P], F32, name="recip", align_bytes=64)
-            mag = ring2.tile([PARTS, P], F32, name="mag", align_bytes=64)
-            root = ring2.tile([PARTS, P], F32, name="root", align_bytes=64)
-            nc.scalar.activation(mag[:, j0:j1], a_t[b, t][:, j0:j1], ACT.Abs)
-            nc.scalar.activation(root[:, j0:j1], mag[:, j0:j1], ACT.Abs_reciprocal_sqrt, bias=knee_t[:, b, t : t + 1])
-            nc.scalar.activation(recip[b][:, t, j0:j1], root[:, j0:j1], ACT.Square)
+            pair = (t0, t0 + 1)
+            mag = {t: ring2.tile([PARTS, P], F32, name="mag", align_bytes=64) for t in pair}
+            root = {t: ring2.tile([PARTS, P], F32, name="root", align_bytes=64) for t in pair}
+            for t in pair:
+                nc.scalar.activation(mag[t][:], a_t[b, t][:], ACT.Abs)
+            for t in pair:
+                nc.scalar.activation(root[t][:], mag[t][:], ACT.Abs_reciprocal_sqrt, bias=knee_t[:, b, t : t + 1])
+            for t in pair:
+                nc.scalar.activation(recip[b][:, t, :], root[t][:], ACT.Square)
 
         z_bf = {}
 
@@ -194,76 +198,90 @@ def tile_list_hit_segment_energy_kernel(
         y_bank = {}
 
         def y_pass(b, c):
-            if b == 0:
-                y_bank[c] = psum.tile([PARTS, N // PARTS, PARTS], F32, name="bank%d" % c)
             cols = slice(c * PARTS, (c + 1) * PARTS)
-            for n in range(N // PARTS):
-                nc.tensor.matmul_mx(
-                    out=y_bank[c][:, n, :],
-                    lhsT=w2_w[:, b, 2 * n * PARTS : 2 * (n + 1) * PARTS].bitcast(FP4X4),
-                    lhsT_scale=w2_sc[:, b, n * PARTS : (n + 1) * PARTS],
-                    rhs=z_codes[b][:, cols].bitcast(FP8X4),
-                    rhs_scale=z_sc[b][:, cols],
-                    start=(b == 0 and n == 0),
-                    stop=(b == BLOCKS - 1 and n == N // PARTS - 1),
-                )
+            for u in range(2):
+                if b == 0:
+                    y_bank[c, u] = psum.tile([PARTS, 2, PARTS], F32, name="bank%d" % (2 * c + u))
+                for v in range(2):
+                    n = 2 * u + v
+                    nc.tensor.matmul_mx(
+                        out=y_bank[c, u][:, v, :],
+                        lhsT=w2_w[:, b, 2 * n * PARTS : 2 * (n + 1) * PARTS].bitcast(FP4X4),
+                        lhsT_scale=w2_sc[:, b, n * PARTS : (n + 1) * PARTS],
+                        rhs=z_codes[b][:, cols].bitcast(FP8X4),
+                        rhs_scale=z_sc[b][:, cols],
+                        start=(b == 0 and v == 0),
+                        stop=(b == BLOCKS - 1 and v == 1),
+                    )
 
         def store(c):
-            energy = ring4.tile([PARTS, N // PARTS, PARTS], F32, name="energy", align_bytes=64)
-            nc.scalar.activation(energy[:], y_bank[c][:], ACT.Square)
-            nc.sync.dma_start(
-                out=out[:, c * PARTS : (c + 1) * PARTS].rearrange("(n p) j -> p n j", p=PARTS), in_=energy[:]
-            )
+            for u in range(2):
+                energy = keep.tile([PARTS, 2, PARTS], F32, name="energy%d%d" % (c, u), align_bytes=64)
+                nc.scalar.activation(energy[:], y_bank[c, u][:], ACT.Square)
+                rows = out[2 * u * PARTS : 2 * (u + 1) * PARTS, c * PARTS : (c + 1) * PARTS]
+                nc.sync.dma_start(out=rows.rearrange("(n p) j -> p n j", p=PARTS), in_=energy[:])
 
         gather_hits(0)
         nc.vector.tensor_copy(hit_sc[:], tab_sc[:].indirect(offs_t[:]))
-        for a in range(PASSES):
-            if a > 0:
-                gather_hits(a)
-            cast_w1(0, a)
-            if a < PASSES - 1:
-                quantize_w1(0, a)
-            else:
-                quantize_w1(0, a, 0, 1)
-                quantize_w1(0, a, 1, 2)
-                quantize_w1(0, a, 2, 4)
-            for t in range(PACK):
-                h_pass(0, t, a)
+        cast_w1(0, 0)
+        quantize_w1(0, 0)
+        for t in range(PACK):
+            h_pass(0, t, 0)
+        gather_hits(1)
+        cast_w1(0, 1, 0, 2)
+        cast_w1(0, 1, 2, 4)
+        quantize_w1(0, 1)
+        for t in range(PACK):
+            h_pass(0, t, 1)
+        gather_hits(2)
+        cast_w1(0, 2, 0, 2)
+        cast_w1(0, 2, 2, 4)
+        for t in range(2):
+            quantize_w1(0, 2, t, t + 1)
+            h_pass(0, t, 2)
+        quantize_w1(0, 2, 2, 4)
+        for t in range(2, PACK):
+            h_pass(0, t, 2)
 
         evacuate(0, 0)
-        for t in range(PACK - 1):
-            gather_first(0, t)
-            evacuate(0, t + 1)
-            cast_w1(1, t)
-            gather_second(0, t)
-            if t > 0:
-                quantize_w1(1, t - 1)
-        quantize_w1(1, PASSES - 1)
+        gather_first(0, 0)
+        evacuate(0, 1)
+        cast_w1(1, 0)
+        gather_second(0, 0)
+        gather_first(0, 1)
+        evacuate(0, 2)
+        cast_w1(1, 1)
+        gather_second(0, 1)
+        quantize_w1(1, 0)
+        gather_first(0, 2)
+        cast_w1(1, 2, 0, 2)
+        cast_w1(1, 2, 2, 4)
+        evacuate(0, 3)
+        gather_second(0, 2)
+        quantize_w1(1, 1)
+        quantize_w1(1, 2)
         for t in range(PACK):
             for a in range(PASSES):
                 h_pass(1, t, a)
-        gather_first(0, PACK - 1)
-        gather_second(0, PACK - 1)
-
+        gather_first(0, 3)
+        gather_second(0, 3)
         saturate(0, 0)
-        saturate(0, 1)
-        evacuate(1, 0)
-        for t in range(PACK):
+        for t in range(2):
+            evacuate(1, t)
             gather_first(1, t)
-            if t + 1 < PACK:
-                evacuate(1, t + 1)
-            if t + 2 < PACK:
-                saturate(0, t + 2)
             gather_second(1, t)
+        saturate(0, 2)
         form_z(0, 0, P)
+        for t in range(2, PACK):
+            evacuate(1, t)
+            gather_first(1, t)
         quantize_z(0, 0, P)
         for c in range(P // PARTS):
             y_pass(0, c)
+        for t in range(2, PACK):
+            gather_second(1, t)
         saturate(1, 0)
-        saturate(1, 1)
-        for half in range(2):
-            for t in range(2, PACK):
-                saturate(1, t, half * P // 2, (half + 1) * P // 2)
+        saturate(1, 2)
         quarters = P // PARTS
         for c in range(quarters + 1):
             if c < quarters:

@@ -23,9 +23,6 @@ PASSES = K // K_PASS
 BLOCKS = H // K_PASS
 BANK = 512
 
-CAST_ON_VECTOR = {(0, 1, 0), (0, 2, 0), (1, 2, 2)}
-FZ = 1
-
 
 def tile_list_hit_segment_energy_kernel(
     tc, tab_words, tab_scales, offs, w1, pos1, pos2, knee, w2_words, w2_scales, out
@@ -33,9 +30,6 @@ def tile_list_hit_segment_energy_kernel(
     nc = tc.nc
     with ExitStack() as ctx:
         keep = ctx.enter_context(tc.tile_pool(name="keep", bufs=1))
-        ring3 = ctx.enter_context(tc.tile_pool(name="ring3", bufs=3))
-        ring4 = ctx.enter_context(tc.tile_pool(name="ring4", bufs=4))
-        ring2 = ctx.enter_context(tc.tile_pool(name="ring2", bufs=2))
         psum = ctx.enter_context(tc.psum_pool(name="psum", bufs=1))
 
         offs_t = keep.tile([PARTS, S // 16], U16, name="offs_t")
@@ -72,22 +66,24 @@ def tile_list_hit_segment_energy_kernel(
         nc.vector.memset(tab_sc[:].bitcast(I32), 0)
         nc.sync.dma_start(offs_t[:], offs)
         load_tab(0, 1)
+        load_tab(1, 1)
         load_w1(0, 0)
-        nc.sync.dma_start(pos1_t[:], pos1)
         for q in range(4):
             nc.sync.dma_start(
                 out=tab_sc[32 * q : 32 * q + 4 * PASSES, :].bitcast(I32),
                 in_=tab_scales[:, 4 * q : 4 * q + 4, :].bitcast(I32),
             )
-        for a in range(1, PASSES):
-            load_tab(a, 1)
-            load_w1(0, a)
+        load_w1(0, 1)
+        load_tab(2, 1)
+        load_w1(0, 2)
+        nc.sync.dma_start(pos1_t[:], pos1)
         nc.sync.dma_start(pos2_t[:], pos2)
         nc.sync.dma_start(out=knee_t[:], in_=knee.rearrange("(b p t) -> p b t", b=BLOCKS, t=PACK))
-        for a in range(PASSES):
-            load_w1(1, a)
-        nc.vector.memset(w2_sc[:].rearrange("p b n -> p (b n)").bitcast(I32), 0)
         nc.sync.dma_start(out=w2_w[:].bitcast(I32), in_=w2_words.rearrange("b p n -> p b n").bitcast(I32))
+        load_w1(1, 0)
+        load_w1(1, 1)
+        load_w1(1, 2)
+        nc.vector.memset(w2_sc[:].rearrange("p b n -> p (b n)").bitcast(I32), 0)
         for q in range(4):
             nc.sync.dma_start(
                 out=w2_sc[32 * q : 32 * q + 4, :, :].bitcast(I32),
@@ -97,14 +93,23 @@ def tile_list_hit_segment_energy_kernel(
         def gather_hits(a):
             nc.vector.tensor_copy(hit[a][:], tab[a][:].bitcast(U32).indirect(offs_t[:]))
 
+        prod0 = keep.tile([PARTS, PACK * P], F32, name="prod0", align_bytes=64)
+        root0 = keep.tile([PARTS, PACK, P], F32, name="root0", align_bytes=64)
+        prod = {0: prod0[:].rearrange("p (t j) -> p t j", t=PACK), 1: root0[:]}
         grouped = {}
+        for b, a in ((0, 0), (0, 1), (0, 2), (1, 1)):
+            own = keep.tile([PARTS, PACK * K_PASS], BF16, name="grouped%d%d" % (b, a), align_bytes=64)
+            grouped[b, a] = own[:]
+        grouped[1, 0] = prod0[:, 0 : 2 * P].bitcast(BF16)
+        grouped[1, 2] = prod0[:, 2 * P : 4 * P].bitcast(BF16)
+        mag = {0: raw[1, 2][:], 1: raw[0, 1][:]}
+        root = {0: root0[:], 1: raw[1, 0][:]}
+        recip = {0: raw[0, 2][:], 1: raw[1, 1][:]}
 
-        def cast_w1(b, a, t0=0, t1=PACK):
-            if (b, a) not in grouped:
-                grouped[b, a] = ring3.tile([PARTS, PACK, PARTS, PACK], BF16, name="grouped", align_bytes=64)
-            dst = grouped[b, a][:, t0:t1].rearrange("p t m j -> p m j t")
+        def cast_w1(engine, b, a, t0=0, t1=PACK):
+            dst = grouped[b, a].rearrange("p (t m j) -> p m j t", t=PACK, j=PACK)[:, :, :, t0:t1]
             src = raw[b, a][:].rearrange("p j (m t) -> p m j t", t=PACK)[:, :, :, t0:t1]
-            if (b, a, t0) in CAST_ON_VECTOR:
+            if engine == "vector":
                 nc.vector.tensor_copy(dst, src)
             else:
                 nc.scalar.activation(dst, src, ACT.Copy)
@@ -114,15 +119,16 @@ def tile_list_hit_segment_energy_kernel(
             nc.vector.quantize_mx(
                 out=w1_codes[b, a][:, cols].bitcast(FP8X4),
                 scales=w1_sc[b, a][:, cols],
-                in_=grouped[b, a][:, t0:t1].rearrange("p t m j -> p (t m j)"),
+                in_=grouped[b, a][:, t0 * K_PASS : t1 * K_PASS],
             )
 
         banks = {}
+        bank_pair = {(0, 0): 0, (0, 1): 1, (0, 2): 2, (0, 3): 0, (1, 0): 3, (1, 1): 1, (1, 2): 2, (1, 3): 0}
 
         def h_pass(b, t, a):
             for half in range(2):
                 if a == 0:
-                    banks[b, t, half] = psum.tile([PARTS, BANK], F32, name="bank%d" % (2 * t + half))
+                    banks[b, t, half] = psum.tile([PARTS, BANK], F32, name="bank%d" % (2 * bank_pair[b, t] + half))
                 cols = slice(half * BANK, (half + 1) * BANK)
                 wcols = slice(t * PARTS, (t + 1) * PARTS)
                 nc.tensor.matmul_mx(
@@ -136,14 +142,13 @@ def tile_list_hit_segment_energy_kernel(
                 )
 
         h_t = {}
-        a_t = {}
-        prod = {}
-        recip = {}
-        z_codes = {}
-        z_sc = {}
+        first = [keep.tile([PARTS, PACK, P], F32, name="first%d" % b, align_bytes=64) for b in range(BLOCKS)]
+        z_bf = [keep.tile([PARTS, P, PACK], BF16, name="z_bf%d" % b, align_bytes=64) for b in range(BLOCKS)]
+        z_codes = [keep.tile([PARTS, P], U32, name="z_codes%d" % b, align_bytes=64) for b in range(BLOCKS)]
+        z_sc = [keep.tile([PARTS, P], U8, name="z_sc%d" % b, align_bytes=64) for b in range(BLOCKS)]
 
         def evacuate(b, t):
-            h_t[b, t] = ring4.tile([PARTS, S], F32, name="h_t", align_bytes=64)
+            h_t[b, t] = keep.tile([PARTS, S], F32, name="h%d%d" % (b, t), align_bytes=64)
             for half in range(2):
                 dst = h_t[b, t][:, half * BANK : (half + 1) * BANK]
                 if (b, t, half) == (0, 0, 1):
@@ -152,32 +157,21 @@ def tile_list_hit_segment_energy_kernel(
                     nc.scalar.activation(dst, banks[b, t, half][:], ACT.Copy)
 
         def gather_first(b, t):
-            a_t[b, t] = keep.tile([PARTS, P], F32, name="a_t%d%d" % (b, t), align_bytes=64)
-            nc.vector.tensor_copy(a_t[b, t][:], h_t[b, t][:].indirect(pos1_t[:]))
+            nc.vector.tensor_copy(first[b][:, t, :], h_t[b, t][:].indirect(pos1_t[:]))
 
         def gather_second(b, t):
-            if t == 0:
-                prod[b] = ring2.tile([PARTS, PACK, P], F32, name="prod", align_bytes=64)
-            nc.vector.tensor_tensor(prod[b][:, t, :], h_t[b, t][:].indirect(pos2_t[:]), a_t[b, t][:], MULT)
+            nc.vector.tensor_tensor(prod[b][:, t, :], h_t[b, t][:].indirect(pos2_t[:]), first[b][:, t, :], MULT)
 
-        def saturate(b, t0):
-            if t0 == 0:
-                recip[b] = ring2.tile([PARTS, PACK, P], F32, name="recip", align_bytes=64)
-            pair = (t0, t0 + 1)
-            mag = {t: ring2.tile([PARTS, P], F32, name="mag", align_bytes=64) for t in pair}
-            root = {t: ring2.tile([PARTS, P], F32, name="root", align_bytes=64) for t in pair}
-            for t in pair:
-                nc.scalar.activation(mag[t][:], a_t[b, t][:], ACT.Abs)
-            for t in pair:
-                nc.scalar.activation(root[t][:], mag[t][:], ACT.Abs_reciprocal_sqrt, bias=knee_t[:, b, t : t + 1])
-            for t in pair:
-                nc.scalar.activation(recip[b][:, t, :], root[t][:], ACT.Square)
+        def magnitude(b, t0, t1):
+            nc.scalar.activation(mag[b][:, t0:t1, :], first[b][:, t0:t1, :], ACT.Abs)
 
-        z_bf = {}
+        def inverse_root(b, t):
+            nc.scalar.activation(root[b][:, t, :], mag[b][:, t, :], ACT.Abs_reciprocal_sqrt, bias=knee_t[:, b, t : t + 1])
+
+        def reciprocal(b, t0, t1, j0=0, j1=P):
+            nc.scalar.activation(recip[b][:, t0:t1, j0:j1], root[b][:, t0:t1, j0:j1], ACT.Square)
 
         def form_z(b, j0, j1):
-            if j0 == 0:
-                z_bf[b] = ring2.tile([PARTS, P, PACK], BF16, name="z_bf", align_bytes=64)
             nc.vector.tensor_tensor(
                 z_bf[b][:, j0:j1, :].rearrange("p (c i) t -> p c t i", i=4),
                 prod[b][:, :, j0:j1].rearrange("p t (c i) -> p c t i", i=4),
@@ -186,9 +180,6 @@ def tile_list_hit_segment_energy_kernel(
             )
 
         def quantize_z(b, j0, j1):
-            if j0 == 0:
-                z_codes[b] = ring2.tile([PARTS, P], U32, name="z_codes", align_bytes=64)
-                z_sc[b] = ring2.tile([PARTS, P], U8, name="z_sc", align_bytes=64)
             nc.vector.quantize_mx(
                 out=z_codes[b][:, j0:j1].bitcast(FP8X4),
                 scales=z_sc[b][:, j0:j1],
@@ -196,93 +187,111 @@ def tile_list_hit_segment_energy_kernel(
             )
 
         y_bank = {}
+        quarters = P // PARTS
+        y_pair = (3, 1, 2, 0)
+        y_parts = {c: ((2 * y_pair[c], 0, 2), (2 * y_pair[c] + 1, 2, 4)) for c in range(quarters)}
 
         def y_pass(b, c):
             cols = slice(c * PARTS, (c + 1) * PARTS)
-            for u in range(2):
+            for bank, n0, n1 in y_parts[c]:
                 if b == 0:
-                    y_bank[c, u] = psum.tile([PARTS, 2, PARTS], F32, name="bank%d" % (2 * c + u))
-                for v in range(2):
-                    n = 2 * u + v
+                    y_bank[c, n0] = psum.tile([PARTS, n1 - n0, PARTS], F32, name="bank%d" % bank)
+                for n in range(n0, n1):
                     nc.tensor.matmul_mx(
-                        out=y_bank[c, u][:, v, :],
+                        out=y_bank[c, n0][:, n - n0, :],
                         lhsT=w2_w[:, b, 2 * n * PARTS : 2 * (n + 1) * PARTS].bitcast(FP4X4),
                         lhsT_scale=w2_sc[:, b, n * PARTS : (n + 1) * PARTS],
                         rhs=z_codes[b][:, cols].bitcast(FP8X4),
                         rhs_scale=z_sc[b][:, cols],
-                        start=(b == 0 and v == 0),
-                        stop=(b == BLOCKS - 1 and v == 1),
+                        start=(b == 0 and n == n0),
+                        stop=(b == BLOCKS - 1 and n == n1 - 1),
                     )
 
         def store(c):
-            for u in range(2):
-                energy = keep.tile([PARTS, 2, PARTS], F32, name="energy%d%d" % (c, u), align_bytes=64)
-                nc.scalar.activation(energy[:], y_bank[c, u][:], ACT.Square)
-                rows = out[2 * u * PARTS : 2 * (u + 1) * PARTS, c * PARTS : (c + 1) * PARTS]
+            for bank, n0, n1 in y_parts[c]:
+                energy = keep.tile([PARTS, n1 - n0, PARTS], F32, name="energy%d" % bank, align_bytes=64)
+                nc.scalar.activation(energy[:], y_bank[c, n0][:], ACT.Square)
+                rows = out[n0 * PARTS : n1 * PARTS, c * PARTS : (c + 1) * PARTS]
                 nc.sync.dma_start(out=rows.rearrange("(n p) j -> p n j", p=PARTS), in_=energy[:])
 
         gather_hits(0)
-        nc.vector.tensor_copy(hit_sc[:], tab_sc[:].indirect(offs_t[:]))
-        cast_w1(0, 0)
-        quantize_w1(0, 0)
-        for t in range(PACK):
-            h_pass(0, t, 0)
         gather_hits(1)
-        cast_w1(0, 1, 0, 2)
-        cast_w1(0, 1, 2, 4)
+        nc.vector.tensor_copy(hit_sc[:], tab_sc[:].indirect(offs_t[:]))
+        cast_w1("scalar", 0, 0)
+        quantize_w1(0, 0)
+        for t in range(PACK - 1):
+            h_pass(0, t, 0)
+        cast_w1("scalar", 0, 1, 0, 2)
+        cast_w1("vector", 0, 1, 2, 4)
         quantize_w1(0, 1)
-        for t in range(PACK):
+        for t in range(PACK - 1):
             h_pass(0, t, 1)
         gather_hits(2)
-        cast_w1(0, 2, 0, 2)
-        cast_w1(0, 2, 2, 4)
+        cast_w1("vector", 0, 2, 0, 2)
+        cast_w1("scalar", 0, 2, 2, 4)
         for t in range(2):
             quantize_w1(0, 2, t, t + 1)
             h_pass(0, t, 2)
         quantize_w1(0, 2, 2, 4)
-        for t in range(2, PACK):
-            h_pass(0, t, 2)
+        h_pass(0, 2, 2)
 
         evacuate(0, 0)
+        for a in range(PASSES):
+            h_pass(0, 3, a)
         gather_first(0, 0)
         evacuate(0, 1)
-        cast_w1(1, 0)
-        gather_second(0, 0)
         gather_first(0, 1)
-        evacuate(0, 2)
-        cast_w1(1, 1)
-        gather_second(0, 1)
-        quantize_w1(1, 0)
-        gather_first(0, 2)
-        cast_w1(1, 2, 0, 2)
-        cast_w1(1, 2, 2, 4)
-        evacuate(0, 3)
-        gather_second(0, 2)
+        cast_w1("scalar", 1, 0)
+        cast_w1("vector", 1, 1)
         quantize_w1(1, 1)
+        quantize_w1(1, 0)
+        evacuate(0, 2)
+        gather_second(0, 0)
+        gather_first(0, 2)
+        evacuate(0, 3)
+        gather_second(0, 1)
+        gather_first(0, 3)
+        cast_w1("scalar", 1, 2)
+        for t in range(PACK):
+            for a in range(PASSES - 1):
+                h_pass(1, t, a)
         quantize_w1(1, 2)
         for t in range(PACK):
-            for a in range(PASSES):
-                h_pass(1, t, a)
-        gather_first(0, 3)
+            h_pass(1, t, PASSES - 1)
+        gather_second(0, 2)
         gather_second(0, 3)
-        saturate(0, 0)
-        for t in range(2):
+
+        magnitude(0, 0, 1)
+        magnitude(0, 1, 2)
+        inverse_root(0, 0)
+        inverse_root(0, 1)
+        magnitude(0, 2, 4)
+        evacuate(1, 0)
+        gather_first(1, 0)
+        evacuate(1, 1)
+        gather_first(1, 1)
+        reciprocal(0, 0, 1)
+        gather_second(1, 0)
+        inverse_root(0, 2)
+        inverse_root(0, 3)
+        for t in range(2, PACK):
             evacuate(1, t)
             gather_first(1, t)
-            gather_second(1, t)
-        saturate(0, 2)
+        reciprocal(0, 1, 2)
+        gather_second(1, 1)
+        magnitude(1, 0, 2)
+        reciprocal(0, 2, 4)
         form_z(0, 0, P)
-        for t in range(2, PACK):
-            evacuate(1, t)
-            gather_first(1, t)
+        gather_second(1, 2)
         quantize_z(0, 0, P)
-        for c in range(P // PARTS):
+        for c in range(quarters):
             y_pass(0, c)
-        for t in range(2, PACK):
-            gather_second(1, t)
-        saturate(1, 0)
-        saturate(1, 2)
-        quarters = P // PARTS
+        gather_second(1, 3)
+        magnitude(1, 2, 4)
+        for t in range(PACK):
+            inverse_root(1, t)
+        for half in range(2):
+            reciprocal(1, 0, PACK, half * P // 2, (half + 1) * P // 2)
         for c in range(quarters + 1):
             if c < quarters:
                 form_z(1, c * PARTS, (c + 1) * PARTS)

@@ -77,12 +77,12 @@ def tile_list_hit_segment_energy_kernel(
         load_tab(2, 1)
         load_w1(0, 2)
         nc.sync.dma_start(pos1_t[:], pos1)
-        nc.sync.dma_start(pos2_t[:], pos2)
-        nc.sync.dma_start(out=knee_t[:], in_=knee.rearrange("(b p t) -> p b t", b=BLOCKS, t=PACK))
-        nc.sync.dma_start(out=w2_w[:].bitcast(I32), in_=w2_words.rearrange("b p n -> p b n").bitcast(I32))
         load_w1(1, 0)
+        nc.sync.dma_start(pos2_t[:], pos2)
         load_w1(1, 1)
         load_w1(1, 2)
+        nc.sync.dma_start(out=knee_t[:], in_=knee.rearrange("(b p t) -> p b t", b=BLOCKS, t=PACK))
+        nc.sync.dma_start(out=w2_w[:].bitcast(I32), in_=w2_words.rearrange("b p n -> p b n").bitcast(I32))
         nc.vector.memset(w2_sc[:].rearrange("p b n -> p (b n)").bitcast(I32), 0)
         for q in range(4):
             nc.sync.dma_start(
@@ -93,22 +93,21 @@ def tile_list_hit_segment_energy_kernel(
         def gather_hits(a):
             nc.vector.tensor_copy(hit[a][:], tab[a][:].bitcast(U32).indirect(offs_t[:]))
 
-        prod0 = keep.tile([PARTS, PACK * P], F32, name="prod0", align_bytes=64)
         root0 = keep.tile([PARTS, PACK, P], F32, name="root0", align_bytes=64)
-        prod = {0: prod0[:].rearrange("p (t j) -> p t j", t=PACK), 1: root0[:]}
+        prod = {0: raw[1, 2][:], 1: root0[:]}
         grouped = {}
-        for b, a in ((0, 0), (0, 1), (0, 2), (1, 1)):
-            own = keep.tile([PARTS, PACK * K_PASS], BF16, name="grouped%d%d" % (b, a), align_bytes=64)
-            grouped[b, a] = own[:]
-        grouped[1, 0] = prod0[:, 0 : 2 * P].bitcast(BF16)
-        grouped[1, 2] = prod0[:, 2 * P : 4 * P].bitcast(BF16)
-        mag = {0: raw[1, 2][:], 1: raw[0, 1][:]}
+        for b in range(BLOCKS):
+            for a in range(PASSES):
+                own = keep.tile([PARTS, PACK * K_PASS], BF16, name="grouped%d%d" % (b, a), align_bytes=64)
+                grouped[b, a] = own[:]
+        mag = {(0, t): raw[1, 2][:, t : t + 1, :] for t in range(PACK)}
+        mag[1, 0] = raw[0, 1][:, :, :]
         root = {0: root0[:], 1: raw[1, 0][:]}
         recip = {0: raw[0, 2][:], 1: raw[1, 1][:]}
 
         def cast_w1(engine, b, a, t0=0, t1=PACK):
             dst = grouped[b, a].rearrange("p (t m j) -> p m j t", t=PACK, j=PACK)[:, :, :, t0:t1]
-            src = raw[b, a][:].rearrange("p j (m t) -> p m j t", t=PACK)[:, :, :, t0:t1]
+            src = raw[b, a][:, :, :].rearrange("p j (m t) -> p m j t", t=PACK)[:, :, :, t0:t1]
             if engine == "vector":
                 nc.vector.tensor_copy(dst, src)
             else:
@@ -123,7 +122,7 @@ def tile_list_hit_segment_energy_kernel(
             )
 
         banks = {}
-        bank_pair = {(0, 0): 0, (0, 1): 1, (0, 2): 2, (0, 3): 0, (1, 0): 3, (1, 1): 1, (1, 2): 2, (1, 3): 0}
+        bank_pair = {(0, 0): 0, (0, 1): 1, (0, 2): 2, (0, 3): 0, (1, 0): 3, (1, 1): 1, (1, 2): 3, (1, 3): 1}
 
         def h_pass(b, t, a):
             for half in range(2):
@@ -151,10 +150,7 @@ def tile_list_hit_segment_energy_kernel(
             h_t[b, t] = keep.tile([PARTS, S], F32, name="h%d%d" % (b, t), align_bytes=64)
             for half in range(2):
                 dst = h_t[b, t][:, half * BANK : (half + 1) * BANK]
-                if (b, t, half) == (0, 0, 1):
-                    nc.vector.tensor_copy(dst, banks[b, t, half][:])
-                else:
-                    nc.scalar.activation(dst, banks[b, t, half][:], ACT.Copy)
+                nc.scalar.activation(dst, banks[b, t, half][:], ACT.Copy)
 
         def gather_first(b, t):
             nc.vector.tensor_copy(first[b][:, t, :], h_t[b, t][:].indirect(pos1_t[:]))
@@ -163,10 +159,12 @@ def tile_list_hit_segment_energy_kernel(
             nc.vector.tensor_tensor(prod[b][:, t, :], h_t[b, t][:].indirect(pos2_t[:]), first[b][:, t, :], MULT)
 
         def magnitude(b, t0, t1):
-            nc.scalar.activation(mag[b][:, t0:t1, :], first[b][:, t0:t1, :], ACT.Abs)
+            dst = mag[0, t0] if b == 0 else mag[1, 0][:, t0:t1, :]
+            nc.scalar.activation(dst, first[b][:, t0:t1, :], ACT.Abs)
 
         def inverse_root(b, t):
-            nc.scalar.activation(root[b][:, t, :], mag[b][:, t, :], ACT.Abs_reciprocal_sqrt, bias=knee_t[:, b, t : t + 1])
+            src = mag[0, t][:, 0, :] if b == 0 else mag[1, 0][:, t, :]
+            nc.scalar.activation(root[b][:, t, :], src, ACT.Abs_reciprocal_sqrt, bias=knee_t[:, b, t : t + 1])
 
         def reciprocal(b, t0, t1, j0=0, j1=P):
             nc.scalar.activation(recip[b][:, t0:t1, j0:j1], root[b][:, t0:t1, j0:j1], ACT.Square)
@@ -188,7 +186,7 @@ def tile_list_hit_segment_energy_kernel(
 
         y_bank = {}
         quarters = P // PARTS
-        y_pair = (3, 1, 2, 0)
+        y_pair = (2, 0, 3, 1)
         y_parts = {c: ((2 * y_pair[c], 0, 2), (2 * y_pair[c] + 1, 2, 4)) for c in range(quarters)}
 
         def y_pass(b, c):
@@ -214,6 +212,9 @@ def tile_list_hit_segment_energy_kernel(
                 rows = out[n0 * PARTS : n1 * PARTS, c * PARTS : (c + 1) * PARTS]
                 nc.sync.dma_start(out=rows.rearrange("(n p) j -> p n j", p=PARTS), in_=energy[:])
 
+        unused = keep.tile([PARTS, 1], F32, name="unused")
+        nc.scalar.activation(unused[:], raw[0, 0][:, 0, 0:1], ACT.Abs_reciprocal_sqrt, scale=0.0, bias=1.0)
+
         gather_hits(0)
         gather_hits(1)
         nc.vector.tensor_copy(hit_sc[:], tab_sc[:].indirect(offs_t[:]))
@@ -235,52 +236,56 @@ def tile_list_hit_segment_energy_kernel(
         quantize_w1(0, 2, 2, 4)
         h_pass(0, 2, 2)
 
+        cast_w1("vector", 1, 0)
         evacuate(0, 0)
         for a in range(PASSES):
             h_pass(0, 3, a)
         gather_first(0, 0)
+        quantize_w1(1, 0)
         evacuate(0, 1)
         gather_first(0, 1)
-        cast_w1("scalar", 1, 0)
-        cast_w1("vector", 1, 1)
-        quantize_w1(1, 1)
-        quantize_w1(1, 0)
         evacuate(0, 2)
-        gather_second(0, 0)
         gather_first(0, 2)
         evacuate(0, 3)
-        gather_second(0, 1)
         gather_first(0, 3)
+        cast_w1("vector", 1, 1, 0, 2)
+        cast_w1("scalar", 1, 1, 2, 4)
+        quantize_w1(1, 1)
         cast_w1("scalar", 1, 2)
-        for t in range(PACK):
+        for t in range(2):
             for a in range(PASSES - 1):
                 h_pass(1, t, a)
         quantize_w1(1, 2)
-        for t in range(PACK):
+        for t in range(2):
             h_pass(1, t, PASSES - 1)
-        gather_second(0, 2)
-        gather_second(0, 3)
 
         magnitude(0, 0, 1)
         magnitude(0, 1, 2)
-        inverse_root(0, 0)
-        inverse_root(0, 1)
-        magnitude(0, 2, 4)
+        for t in range(2):
+            inverse_root(0, t)
+            gather_second(0, t)
+        magnitude(0, 2, 3)
+        magnitude(0, 3, 4)
+        for t in range(2, PACK):
+            inverse_root(0, t)
+            gather_second(0, t)
         evacuate(1, 0)
+        for a in range(PASSES):
+            h_pass(1, 2, a)
         gather_first(1, 0)
         evacuate(1, 1)
+        for a in range(PASSES):
+            h_pass(1, 3, a)
         gather_first(1, 1)
         reciprocal(0, 0, 1)
         gather_second(1, 0)
-        inverse_root(0, 2)
-        inverse_root(0, 3)
         for t in range(2, PACK):
             evacuate(1, t)
             gather_first(1, t)
         reciprocal(0, 1, 2)
         gather_second(1, 1)
-        magnitude(1, 0, 2)
         reciprocal(0, 2, 4)
+        magnitude(1, 0, 2)
         form_z(0, 0, P)
         gather_second(1, 2)
         quantize_z(0, 0, P)

@@ -45,9 +45,13 @@ def tile_list_hit_segment_energy_kernel(
         w1_sc = {}
         for b in range(BLOCKS):
             for a in range(PASSES):
-                raw[b, a] = keep.tile([PARTS, PACK, K_PASS], F32, name="raw%d%d" % (b, a), align_bytes=64)
+                if (b, a) != (1, 0):
+                    own = keep.tile([PARTS, PACK, K_PASS], F32, name="raw%d%d" % (b, a), align_bytes=64)
+                    raw[b, a] = own[:]
                 w1_codes[b, a] = keep.tile([PARTS, K_PASS], U32, name="w1c%d%d" % (b, a), align_bytes=64)
                 w1_sc[b, a] = keep.tile([PARTS, K_PASS], U8, name="w1s%d%d" % (b, a), align_bytes=64)
+        early = keep.tile([PARTS, P // 2 + PACK * K_PASS], F32, name="early", align_bytes=64)
+        raw[1, 0] = early[:, P // 2 :].rearrange("p (j c) -> p j c", j=PACK)
         w2_w = keep.tile([PARTS, BLOCKS, 2 * N], U8, name="w2_w", align_bytes=64)
         w2_sc = keep.tile([PARTS, BLOCKS, N], U8, name="w2_sc", align_bytes=64)
 
@@ -94,20 +98,23 @@ def tile_list_hit_segment_energy_kernel(
             nc.vector.tensor_copy(hit[a][:], tab[a][:].bitcast(U32).indirect(offs_t[:]))
 
         root0 = keep.tile([PARTS, PACK, P], F32, name="root0", align_bytes=64)
-        prod = {0: raw[1, 2][:], 1: root0[:]}
+        prod = {0: raw[1, 2], 1: root0[:]}
         grouped = {}
         for b in range(BLOCKS):
             for a in range(PASSES):
                 own = keep.tile([PARTS, PACK * K_PASS], BF16, name="grouped%d%d" % (b, a), align_bytes=64)
                 grouped[b, a] = own[:]
-        mag = {(0, t): raw[1, 2][:, t : t + 1, :] for t in range(PACK)}
+        mag = {(0, t): raw[1, 2][:, t + 2 : t + 3, :] for t in range(2)}
+        late = grouped[1, 2].bitcast(F32).rearrange("p (r j) -> p r j", j=P)
+        mag[0, 2] = late[:, 0:1, :]
+        mag[0, 3] = late[:, 1:2, :]
         mag[1, 0] = raw[0, 1][:, :, :]
-        root = {0: root0[:], 1: raw[1, 0][:]}
-        recip = {0: raw[0, 2][:], 1: raw[1, 1][:]}
+        root = {0: root0[:], 1: raw[1, 0]}
+        recip = {0: raw[0, 2], 1: raw[1, 1]}
 
-        def cast_w1(engine, b, a, t0=0, t1=PACK):
-            dst = grouped[b, a].rearrange("p (t m j) -> p m j t", t=PACK, j=PACK)[:, :, :, t0:t1]
-            src = raw[b, a][:, :, :].rearrange("p j (m t) -> p m j t", t=PACK)[:, :, :, t0:t1]
+        def cast_w1(engine, b, a, t0=0, t1=PACK, m0=0, m1=PARTS):
+            dst = grouped[b, a].rearrange("p (t m j) -> p m j t", t=PACK, j=PACK)[:, m0:m1, :, t0:t1]
+            src = raw[b, a].rearrange("p j (m t) -> p m j t", t=PACK)[:, m0:m1, :, t0:t1]
             if engine == "vector":
                 nc.vector.tensor_copy(dst, src)
             else:
@@ -122,7 +129,7 @@ def tile_list_hit_segment_energy_kernel(
             )
 
         banks = {}
-        bank_pair = {(0, 0): 0, (0, 1): 1, (0, 2): 2, (0, 3): 0, (1, 0): 3, (1, 1): 1, (1, 2): 3, (1, 3): 1}
+        bank_pair = {(0, 0): 0, (0, 1): 1, (0, 2): 2, (0, 3): 0, (1, 0): 1, (1, 1): 2, (1, 2): 1, (1, 3): 2}
 
         def h_pass(b, t, a):
             for half in range(2):
@@ -142,6 +149,8 @@ def tile_list_hit_segment_energy_kernel(
 
         h_t = {}
         first = [keep.tile([PARTS, PACK, P], F32, name="first%d" % b, align_bytes=64) for b in range(BLOCKS)]
+        picked = {(b, t): first[b][:, t, :] for b in range(BLOCKS) for t in range(PACK)}
+        picked[0, 0] = early[:, 0:P]
         z_bf = [keep.tile([PARTS, P, PACK], BF16, name="z_bf%d" % b, align_bytes=64) for b in range(BLOCKS)]
         z_codes = [keep.tile([PARTS, P], U32, name="z_codes%d" % b, align_bytes=64) for b in range(BLOCKS)]
         z_sc = [keep.tile([PARTS, P], U8, name="z_sc%d" % b, align_bytes=64) for b in range(BLOCKS)]
@@ -153,14 +162,16 @@ def tile_list_hit_segment_energy_kernel(
                 nc.scalar.activation(dst, banks[b, t, half][:], ACT.Copy)
 
         def gather_first(b, t):
-            nc.vector.tensor_copy(first[b][:, t, :], h_t[b, t][:].indirect(pos1_t[:]))
+            nc.vector.tensor_copy(picked[b, t], h_t[b, t][:].indirect(pos1_t[:]))
 
         def gather_second(b, t):
-            nc.vector.tensor_tensor(prod[b][:, t, :], h_t[b, t][:].indirect(pos2_t[:]), first[b][:, t, :], MULT)
+            nc.vector.tensor_tensor(prod[b][:, t, :], h_t[b, t][:].indirect(pos2_t[:]), picked[b, t], MULT)
 
         def magnitude(b, t0, t1):
-            dst = mag[0, t0] if b == 0 else mag[1, 0][:, t0:t1, :]
-            nc.scalar.activation(dst, first[b][:, t0:t1, :], ACT.Abs)
+            if b == 0:
+                nc.scalar.activation(mag[0, t0][:, 0, :], picked[0, t0], ACT.Abs)
+            else:
+                nc.scalar.activation(mag[1, 0][:, t0:t1, :], first[1][:, t0:t1, :], ACT.Abs)
 
         def inverse_root(b, t):
             src = mag[0, t][:, 0, :] if b == 0 else mag[1, 0][:, t, :]
@@ -186,7 +197,7 @@ def tile_list_hit_segment_energy_kernel(
 
         y_bank = {}
         quarters = P // PARTS
-        y_pair = (2, 0, 3, 1)
+        y_pair = (3, 0, 1, 2)
         y_parts = {c: ((2 * y_pair[c], 0, 2), (2 * y_pair[c] + 1, 2, 4)) for c in range(quarters)}
 
         def y_pass(b, c):
@@ -236,7 +247,8 @@ def tile_list_hit_segment_energy_kernel(
         quantize_w1(0, 2, 2, 4)
         h_pass(0, 2, 2)
 
-        cast_w1("vector", 1, 0)
+        for half in range(2):
+            cast_w1("vector", 1, 0, 0, PACK, half * PARTS // 2, (half + 1) * PARTS // 2)
         evacuate(0, 0)
         for a in range(PASSES):
             h_pass(0, 3, a)
@@ -259,11 +271,11 @@ def tile_list_hit_segment_energy_kernel(
         for t in range(2):
             h_pass(1, t, PASSES - 1)
 
-        magnitude(0, 0, 1)
-        magnitude(0, 1, 2)
+        for t in range(2):
+            gather_second(0, t)
+            magnitude(0, t, t + 1)
         for t in range(2):
             inverse_root(0, t)
-            gather_second(0, t)
         magnitude(0, 2, 3)
         magnitude(0, 3, 4)
         for t in range(2, PACK):

@@ -101,9 +101,12 @@ def tile_list_hit_segment_energy_kernel(
         prod = {0: raw[1, 2], 1: root0[:]}
         grouped = {}
         for b in range(BLOCKS):
-            for a in range(PASSES):
+            for a in range(PASSES) if b == 0 else (2,):
                 own = keep.tile([PARTS, PACK * K_PASS], BF16, name="grouped%d%d" % (b, a), align_bytes=64)
                 grouped[b, a] = own[:]
+        pair = keep.tile([PARTS, 6 * K_PASS], BF16, name="pair", align_bytes=64)
+        grouped[1, 0] = pair[:, 0 : PACK * K_PASS]
+        grouped[1, 1] = pair[:, 2 * K_PASS :]
         mag = {(0, t): raw[1, 2][:, t + 2 : t + 3, :] for t in range(2)}
         late = grouped[1, 2].bitcast(F32).rearrange("p (r j) -> p r j", j=P)
         mag[0, 2] = late[:, 0:1, :]
@@ -117,6 +120,10 @@ def tile_list_hit_segment_energy_kernel(
             src = raw[b, a].rearrange("p j (m t) -> p m j t", t=PACK)[:, m0:m1, :, t0:t1]
             if engine == "vector":
                 nc.vector.tensor_copy(dst, src)
+            elif engine == "gpsimd":
+                dst = grouped[b, a].rearrange("p (t m j) -> p t m j", t=PACK, j=PACK)
+                src = raw[b, a].rearrange("p j (m t) -> p t m j", t=PACK)
+                nc.gpsimd.tensor_scalar(dst, src, 1.0, 0.0, MULT, mybir.AluOpType.add)
             else:
                 nc.scalar.activation(dst, src, ACT.Copy)
 
@@ -173,9 +180,9 @@ def tile_list_hit_segment_energy_kernel(
             else:
                 nc.scalar.activation(mag[1, 0][:, t0:t1, :], first[1][:, t0:t1, :], ACT.Abs)
 
-        def inverse_root(b, t):
-            src = mag[0, t][:, 0, :] if b == 0 else mag[1, 0][:, t, :]
-            nc.scalar.activation(root[b][:, t, :], src, ACT.Abs_reciprocal_sqrt, bias=knee_t[:, b, t : t + 1])
+        def inverse_root(b, t, j0=0, j1=P):
+            src = mag[0, t][:, 0, j0:j1] if b == 0 else mag[1, 0][:, t, j0:j1]
+            nc.scalar.activation(root[b][:, t, j0:j1], src, ACT.Abs_reciprocal_sqrt, bias=knee_t[:, b, t : t + 1])
 
         def reciprocal(b, t0, t1, j0=0, j1=P):
             nc.scalar.activation(recip[b][:, t0:t1, j0:j1], root[b][:, t0:t1, j0:j1], ACT.Square)
@@ -203,7 +210,8 @@ def tile_list_hit_segment_energy_kernel(
         def y_pass(b, c):
             cols = slice(c * PARTS, (c + 1) * PARTS)
             for bank, n0, n1 in y_parts[c]:
-                if b == 0:
+                opens = b == 0
+                if opens:
                     y_bank[c, n0] = psum.tile([PARTS, n1 - n0, PARTS], F32, name="bank%d" % bank)
                 for n in range(n0, n1):
                     nc.tensor.matmul_mx(
@@ -212,8 +220,8 @@ def tile_list_hit_segment_energy_kernel(
                         lhsT_scale=w2_sc[:, b, n * PARTS : (n + 1) * PARTS],
                         rhs=z_codes[b][:, cols].bitcast(FP8X4),
                         rhs_scale=z_sc[b][:, cols],
-                        start=(b == 0 and n == n0),
-                        stop=(b == BLOCKS - 1 and n == n1 - 1),
+                        start=(opens and n == n0),
+                        stop=(not opens and n == n1 - 1),
                     )
 
         def store(c):
@@ -260,8 +268,7 @@ def tile_list_hit_segment_energy_kernel(
         gather_first(0, 2)
         evacuate(0, 3)
         gather_first(0, 3)
-        cast_w1("vector", 1, 1, 0, 2)
-        cast_w1("scalar", 1, 1, 2, 4)
+        cast_w1("gpsimd", 1, 1)
         quantize_w1(1, 1)
         cast_w1("scalar", 1, 2)
         for t in range(2):
@@ -279,12 +286,13 @@ def tile_list_hit_segment_energy_kernel(
         magnitude(0, 2, 3)
         magnitude(0, 3, 4)
         for t in range(2, PACK):
-            inverse_root(0, t)
             gather_second(0, t)
+        inverse_root(0, 2)
         evacuate(1, 0)
         for a in range(PASSES):
             h_pass(1, 2, a)
         gather_first(1, 0)
+        inverse_root(0, 3)
         evacuate(1, 1)
         for a in range(PASSES):
             h_pass(1, 3, a)

@@ -22,6 +22,7 @@ K_PASS = PARTS * PACK
 PASSES = K // K_PASS
 BLOCKS = H // K_PASS
 BANK = 512
+SHARE = 80
 
 
 def tile_list_hit_segment_energy_kernel(
@@ -121,8 +122,8 @@ def tile_list_hit_segment_energy_kernel(
             if engine == "vector":
                 nc.vector.tensor_copy(dst, src)
             elif engine == "gpsimd":
-                dst = grouped[b, a].rearrange("p (t m j) -> p t m j", t=PACK, j=PACK)
-                src = raw[b, a].rearrange("p j (m t) -> p t m j", t=PACK)
+                dst = grouped[b, a].rearrange("p (t m j) -> p t m j", t=PACK, j=PACK)[:, :, m0:m1, :]
+                src = raw[b, a].rearrange("p j (m t) -> p t m j", t=PACK)[:, :, m0:m1, :]
                 nc.gpsimd.tensor_scalar(dst, src, 1.0, 0.0, MULT, mybir.AluOpType.add)
             else:
                 nc.scalar.activation(dst, src, ACT.Copy)
@@ -268,7 +269,8 @@ def tile_list_hit_segment_energy_kernel(
         gather_first(0, 2)
         evacuate(0, 3)
         gather_first(0, 3)
-        cast_w1("gpsimd", 1, 1)
+        cast_w1("gpsimd", 1, 1, 0, PACK, 0, SHARE)
+        cast_w1("scalar", 1, 1, 0, PACK, SHARE, PARTS)
         quantize_w1(1, 1)
         cast_w1("scalar", 1, 2)
         for t in range(2):
@@ -287,18 +289,18 @@ def tile_list_hit_segment_energy_kernel(
         magnitude(0, 3, 4)
         for t in range(2, PACK):
             gather_second(0, t)
-        inverse_root(0, 2)
         evacuate(1, 0)
         for a in range(PASSES):
             h_pass(1, 2, a)
         gather_first(1, 0)
-        inverse_root(0, 3)
+        inverse_root(0, 2)
         evacuate(1, 1)
         for a in range(PASSES):
             h_pass(1, 3, a)
         gather_first(1, 1)
         reciprocal(0, 0, 1)
         gather_second(1, 0)
+        inverse_root(0, 3)
         for t in range(2, PACK):
             evacuate(1, t)
             gather_first(1, t)
@@ -313,10 +315,14 @@ def tile_list_hit_segment_energy_kernel(
             y_pass(0, c)
         gather_second(1, 3)
         magnitude(1, 2, 4)
-        for t in range(PACK):
+        for t in range(2):
             inverse_root(1, t)
-        for half in range(2):
-            reciprocal(1, 0, PACK, half * P // 2, (half + 1) * P // 2)
+        for t in range(2, PACK):
+            inverse_root(1, t, 0, P // 2)
+        for c in range(quarters):
+            if c < 2:
+                inverse_root(1, 2 + c, P // 2, P)
+            reciprocal(1, 0, PACK, c * PARTS, (c + 1) * PARTS)
         for c in range(quarters + 1):
             if c < quarters:
                 form_z(1, c * PARTS, (c + 1) * PARTS)

@@ -15,14 +15,19 @@ FP8X4 = mybir.dt.float8_e4m3fn_x4
 FP4X4 = mybir.dt.float4_e2m1fn_x4
 ACT = mybir.ActivationFunctionType
 MULT = mybir.AluOpType.mult
+ADD = mybir.AluOpType.add
 
 PARTS = 128
 PACK = 4
 K_PASS = PARTS * PACK
 PASSES = K // K_PASS
-BLOCKS = H // K_PASS
+BANDS = H // K_PASS
 BANK = 512
-SHARE = 80
+QUADRANTS = 4
+QUARTERS = P // PARTS
+GROUP = 16
+CAST_SHARE = 80
+Z_SHARE = 160
 
 
 def tile_list_hit_segment_energy_kernel(
@@ -33,10 +38,10 @@ def tile_list_hit_segment_energy_kernel(
         keep = ctx.enter_context(tc.tile_pool(name="keep", bufs=1))
         psum = ctx.enter_context(tc.psum_pool(name="psum", bufs=1))
 
-        offs_t = keep.tile([PARTS, S // 16], U16, name="offs_t")
-        pos1_t = keep.tile([PARTS, P // 16], U16, name="pos1_t")
-        pos2_t = keep.tile([PARTS, P // 16], U16, name="pos2_t")
-        knee_t = keep.tile([PARTS, BLOCKS, PACK], F32, name="knee_t")
+        offs_t = keep.tile([PARTS, S // GROUP], U16, name="offs_t")
+        pos1_t = keep.tile([PARTS, P // GROUP], U16, name="pos1_t")
+        pos2_t = keep.tile([PARTS, P // GROUP], U16, name="pos2_t")
+        knee_t = keep.tile([PARTS, BANDS, PACK], F32, name="knee_t")
         tab = [keep.tile([PARTS, T], I32, name="tab%d" % a, align_bytes=64) for a in range(PASSES)]
         tab_sc = keep.tile([PARTS, T], U8, name="tab_sc", align_bytes=64)
         hit = [keep.tile([PARTS, S], U32, name="hit%d" % a, align_bytes=64) for a in range(PASSES)]
@@ -44,52 +49,47 @@ def tile_list_hit_segment_energy_kernel(
         raw = {}
         w1_codes = {}
         w1_sc = {}
-        for b in range(BLOCKS):
+        for b in range(BANDS):
             for a in range(PASSES):
                 if (b, a) != (1, 0):
-                    own = keep.tile([PARTS, PACK, K_PASS], F32, name="raw%d%d" % (b, a), align_bytes=64)
-                    raw[b, a] = own[:]
+                    piece = keep.tile([PARTS, PACK, K_PASS], F32, name="raw%d%d" % (b, a), align_bytes=64)
+                    raw[b, a] = piece[:]
                 w1_codes[b, a] = keep.tile([PARTS, K_PASS], U32, name="w1c%d%d" % (b, a), align_bytes=64)
                 w1_sc[b, a] = keep.tile([PARTS, K_PASS], U8, name="w1s%d%d" % (b, a), align_bytes=64)
         early = keep.tile([PARTS, P // 2 + PACK * K_PASS], F32, name="early", align_bytes=64)
         raw[1, 0] = early[:, P // 2 :].rearrange("p (j c) -> p j c", j=PACK)
-        w2_w = keep.tile([PARTS, BLOCKS, 2 * N], U8, name="w2_w", align_bytes=64)
-        w2_sc = keep.tile([PARTS, BLOCKS, N], U8, name="w2_sc", align_bytes=64)
+        w2_w = keep.tile([PARTS, BANDS, 2 * N], U8, name="w2_w", align_bytes=64)
+        w2_sc = keep.tile([PARTS, BANDS, N], U8, name="w2_sc", align_bytes=64)
 
-        def load_tab(a, pieces):
-            words = tab_words[a].rearrange("p t i -> p (t i)").bitcast(I32)
-            for c in range(pieces):
-                cols = slice(c * T // pieces, (c + 1) * T // pieces)
-                nc.sync.dma_start(out=tab[a][:, cols], in_=words[:, cols])
+        def load_tab(a):
+            nc.sync.dma_start(out=tab[a][:], in_=tab_words[a].rearrange("p t i -> p (t i)").bitcast(I32))
 
-        def load_w1(b, a, pieces=1):
-            rows = w1[a * K_PASS : (a + 1) * K_PASS, b * K_PASS : (b + 1) * K_PASS].rearrange("(p j) c -> p j c", j=PACK)
-            for c in range(pieces):
-                js = slice(c * PACK // pieces, (c + 1) * PACK // pieces)
-                nc.sync.dma_start(out=raw[b, a][:, js, :], in_=rows[:, js, :])
+        def load_w1(b, a):
+            rows = w1[a * K_PASS : (a + 1) * K_PASS, b * K_PASS : (b + 1) * K_PASS]
+            nc.sync.dma_start(out=raw[b, a], in_=rows.rearrange("(p j) c -> p j c", j=PACK))
 
         nc.vector.memset(tab_sc[:].bitcast(I32), 0)
         nc.sync.dma_start(offs_t[:], offs)
-        load_tab(0, 1)
-        load_tab(1, 1)
+        load_tab(0)
+        load_tab(1)
         load_w1(0, 0)
-        for q in range(4):
+        for q in range(QUADRANTS):
             nc.sync.dma_start(
                 out=tab_sc[32 * q : 32 * q + 4 * PASSES, :].bitcast(I32),
                 in_=tab_scales[:, 4 * q : 4 * q + 4, :].bitcast(I32),
             )
         load_w1(0, 1)
-        load_tab(2, 1)
+        load_tab(2)
         load_w1(0, 2)
         nc.sync.dma_start(pos1_t[:], pos1)
         load_w1(1, 0)
         nc.sync.dma_start(pos2_t[:], pos2)
         load_w1(1, 1)
         load_w1(1, 2)
-        nc.sync.dma_start(out=knee_t[:], in_=knee.rearrange("(b p t) -> p b t", b=BLOCKS, t=PACK))
+        nc.sync.dma_start(out=knee_t[:], in_=knee.rearrange("(b p t) -> p b t", b=BANDS, t=PACK))
         nc.sync.dma_start(out=w2_w[:].bitcast(I32), in_=w2_words.rearrange("b p n -> p b n").bitcast(I32))
         nc.vector.memset(w2_sc[:].rearrange("p b n -> p (b n)").bitcast(I32), 0)
-        for q in range(4):
+        for q in range(QUADRANTS):
             nc.sync.dma_start(
                 out=w2_sc[32 * q : 32 * q + 4, :, :].bitcast(I32),
                 in_=w2_scales[:, 4 * q : 4 * q + 4, :].rearrange("b r n -> r b n").bitcast(I32),
@@ -98,35 +98,37 @@ def tile_list_hit_segment_energy_kernel(
         def gather_hits(a):
             nc.vector.tensor_copy(hit[a][:], tab[a][:].bitcast(U32).indirect(offs_t[:]))
 
-        root0 = keep.tile([PARTS, PACK, P], F32, name="root0", align_bytes=64)
-        prod = {0: raw[1, 2], 1: root0[:]}
+        late = keep.tile([PARTS, (PACK + 2) * P], F32, name="late", align_bytes=64)
+        late_rows = late[:].rearrange("p (r j) -> p r j", j=P)
+        prod = {0: raw[1, 2], 1: late_rows[:, 1 : PACK + 1, :]}
         grouped = {}
-        for b in range(BLOCKS):
-            for a in range(PASSES) if b == 0 else (2,):
-                own = keep.tile([PARTS, PACK * K_PASS], BF16, name="grouped%d%d" % (b, a), align_bytes=64)
-                grouped[b, a] = own[:]
-        pair = keep.tile([PARTS, 6 * K_PASS], BF16, name="pair", align_bytes=64)
-        grouped[1, 0] = pair[:, 0 : PACK * K_PASS]
-        grouped[1, 1] = pair[:, 2 * K_PASS :]
-        mag = {(0, t): raw[1, 2][:, t + 2 : t + 3, :] for t in range(2)}
-        late = grouped[1, 2].bitcast(F32).rearrange("p (r j) -> p r j", j=P)
-        mag[0, 2] = late[:, 0:1, :]
-        mag[0, 3] = late[:, 1:2, :]
-        mag[1, 0] = raw[0, 1][:, :, :]
-        root = {0: root0[:], 1: raw[1, 0]}
+        for a in range(PASSES):
+            rounded = keep.tile([PARTS, PACK * K_PASS], BF16, name="grouped%d" % a, align_bytes=64)
+            grouped[0, a] = rounded[:]
+        grouped[1, 2] = late[:, 0 : 2 * P].bitcast(BF16)
+        overlap = keep.tile([PARTS, (PACK + PACK // 2) * K_PASS], BF16, name="overlap", align_bytes=64)
+        grouped[1, 0] = overlap[:, 0 : PACK * K_PASS]
+        grouped[1, 1] = overlap[:, PACK // 2 * K_PASS :]
+        mag0 = [raw[1, 2][:, 2, :], raw[1, 2][:, 3, :], late_rows[:, 0, :], late_rows[:, 1, :]]
+        mag1 = raw[0, 1]
+        root = {0: late_rows[:, 2:, :], 1: raw[1, 0]}
         recip = {0: raw[0, 2], 1: raw[1, 1]}
 
-        def cast_w1(engine, b, a, t0=0, t1=PACK, m0=0, m1=PARTS):
-            dst = grouped[b, a].rearrange("p (t m j) -> p m j t", t=PACK, j=PACK)[:, m0:m1, :, t0:t1]
-            src = raw[b, a].rearrange("p j (m t) -> p m j t", t=PACK)[:, m0:m1, :, t0:t1]
-            if engine == "vector":
-                nc.vector.tensor_copy(dst, src)
-            elif engine == "gpsimd":
-                dst = grouped[b, a].rearrange("p (t m j) -> p t m j", t=PACK, j=PACK)[:, :, m0:m1, :]
-                src = raw[b, a].rearrange("p j (m t) -> p t m j", t=PACK)[:, :, m0:m1, :]
-                nc.gpsimd.tensor_scalar(dst, src, 1.0, 0.0, MULT, mybir.AluOpType.add)
-            else:
-                nc.scalar.activation(dst, src, ACT.Copy)
+        def cast_views(b, a, ts, ms):
+            dst = grouped[b, a].rearrange("p (t m j) -> p m j t", t=PACK, j=PACK)[:, ms, :, ts]
+            src = raw[b, a].rearrange("p j (m t) -> p m j t", t=PACK)[:, ms, :, ts]
+            return dst, src
+
+        def cast_vector(b, a, ts=slice(0, PACK), ms=slice(0, PARTS)):
+            nc.vector.tensor_copy(*cast_views(b, a, ts, ms))
+
+        def cast_scalar(b, a, ts=slice(0, PACK), ms=slice(0, PARTS)):
+            nc.scalar.activation(*cast_views(b, a, ts, ms), ACT.Copy)
+
+        def cast_gpsimd(b, a, ms):
+            dst = grouped[b, a].rearrange("p (t m j) -> p t m j", t=PACK, j=PACK)[:, :, ms, :]
+            src = raw[b, a].rearrange("p j (m t) -> p t m j", t=PACK)[:, :, ms, :]
+            nc.gpsimd.tensor_scalar(dst, src, 1.0, 0.0, MULT, ADD)
 
         def quantize_w1(b, a, t0=0, t1=PACK):
             cols = slice(t0 * PARTS, t1 * PARTS)
@@ -136,17 +138,19 @@ def tile_list_hit_segment_energy_kernel(
                 in_=grouped[b, a][:, t0 * K_PASS : t1 * K_PASS],
             )
 
-        banks = {}
-        bank_pair = {(0, 0): 0, (0, 1): 1, (0, 2): 2, (0, 3): 0, (1, 0): 1, (1, 1): 2, (1, 2): 1, (1, 3): 2}
+        h_bank = {}
+        h_pair = {(0, t): t % 3 for t in range(PACK)}
+        for t in range(PACK):
+            h_pair[1, t] = 1 + t % 2
 
         def h_pass(b, t, a):
             for half in range(2):
                 if a == 0:
-                    banks[b, t, half] = psum.tile([PARTS, BANK], F32, name="bank%d" % (2 * bank_pair[b, t] + half))
+                    h_bank[b, t, half] = psum.tile([PARTS, BANK], F32, name="bank%d" % (2 * h_pair[b, t] + half))
                 cols = slice(half * BANK, (half + 1) * BANK)
                 wcols = slice(t * PARTS, (t + 1) * PARTS)
                 nc.tensor.matmul_mx(
-                    out=banks[b, t, half][:],
+                    out=h_bank[b, t, half][:],
                     lhsT=w1_codes[b, a][:, wcols].bitcast(FP8X4),
                     lhsT_scale=w1_sc[b, a][:, wcols],
                     rhs=hit[a][:, cols].bitcast(FP8X4),
@@ -155,19 +159,23 @@ def tile_list_hit_segment_energy_kernel(
                     stop=(a == PASSES - 1),
                 )
 
+        def h_slice(b, t):
+            for a in range(PASSES):
+                h_pass(b, t, a)
+
         h_t = {}
-        first = [keep.tile([PARTS, PACK, P], F32, name="first%d" % b, align_bytes=64) for b in range(BLOCKS)]
-        picked = {(b, t): first[b][:, t, :] for b in range(BLOCKS) for t in range(PACK)}
+        first = [keep.tile([PARTS, PACK, P], F32, name="first%d" % b, align_bytes=64) for b in range(BANDS)]
+        picked = {(b, t): first[b][:, t, :] for b in range(BANDS) for t in range(PACK)}
         picked[0, 0] = early[:, 0:P]
-        z_bf = [keep.tile([PARTS, P, PACK], BF16, name="z_bf%d" % b, align_bytes=64) for b in range(BLOCKS)]
-        z_codes = [keep.tile([PARTS, P], U32, name="z_codes%d" % b, align_bytes=64) for b in range(BLOCKS)]
-        z_sc = [keep.tile([PARTS, P], U8, name="z_sc%d" % b, align_bytes=64) for b in range(BLOCKS)]
+        z_bf = [keep.tile([PARTS, P, PACK], BF16, name="z_bf%d" % b, align_bytes=64) for b in range(BANDS)]
+        z_codes = [keep.tile([PARTS, P], U32, name="z_codes%d" % b, align_bytes=64) for b in range(BANDS)]
+        z_sc = [keep.tile([PARTS, P], U8, name="z_sc%d" % b, align_bytes=64) for b in range(BANDS)]
 
         def evacuate(b, t):
             h_t[b, t] = keep.tile([PARTS, S], F32, name="h%d%d" % (b, t), align_bytes=64)
             for half in range(2):
                 dst = h_t[b, t][:, half * BANK : (half + 1) * BANK]
-                nc.scalar.activation(dst, banks[b, t, half][:], ACT.Copy)
+                nc.scalar.activation(dst, h_bank[b, t, half][:], ACT.Copy)
 
         def gather_first(b, t):
             nc.vector.tensor_copy(picked[b, t], h_t[b, t][:].indirect(pos1_t[:]))
@@ -175,24 +183,32 @@ def tile_list_hit_segment_energy_kernel(
         def gather_second(b, t):
             nc.vector.tensor_tensor(prod[b][:, t, :], h_t[b, t][:].indirect(pos2_t[:]), picked[b, t], MULT)
 
-        def magnitude(b, t0, t1):
-            if b == 0:
-                nc.scalar.activation(mag[0, t0][:, 0, :], picked[0, t0], ACT.Abs)
-            else:
-                nc.scalar.activation(mag[1, 0][:, t0:t1, :], first[1][:, t0:t1, :], ACT.Abs)
+        def magnitude0(t):
+            nc.scalar.activation(mag0[t], picked[0, t], ACT.Abs)
+
+        def magnitude1(t0, t1):
+            nc.scalar.activation(mag1[:, t0:t1, :], first[1][:, t0:t1, :], ACT.Abs)
 
         def inverse_root(b, t, j0=0, j1=P):
-            src = mag[0, t][:, 0, j0:j1] if b == 0 else mag[1, 0][:, t, j0:j1]
+            src = mag0[t][:, j0:j1] if b == 0 else mag1[:, t, j0:j1]
             nc.scalar.activation(root[b][:, t, j0:j1], src, ACT.Abs_reciprocal_sqrt, bias=knee_t[:, b, t : t + 1])
 
-        def reciprocal(b, t0, t1, j0=0, j1=P):
-            nc.scalar.activation(recip[b][:, t0:t1, j0:j1], root[b][:, t0:t1, j0:j1], ACT.Square)
+        def reciprocal(b, j0, j1):
+            nc.scalar.activation(recip[b][:, :, j0:j1], root[b][:, :, j0:j1], ACT.Square)
 
         def form_z(b, j0, j1):
             nc.vector.tensor_tensor(
                 z_bf[b][:, j0:j1, :].rearrange("p (c i) t -> p c t i", i=4),
                 prod[b][:, :, j0:j1].rearrange("p t (c i) -> p c t i", i=4),
                 recip[b][:, :, j0:j1].rearrange("p t (c i) -> p c t i", i=4),
+                MULT,
+            )
+
+        def form_z_gpsimd(b, j0, j1):
+            nc.gpsimd.tensor_tensor(
+                z_bf[b][:, j0:j1, :],
+                prod[b][:, :, j0:j1].rearrange("p t j -> p j t"),
+                recip[b][:, :, j0:j1].rearrange("p t j -> p j t"),
                 MULT,
             )
 
@@ -204,75 +220,70 @@ def tile_list_hit_segment_energy_kernel(
             )
 
         y_bank = {}
-        quarters = P // PARTS
-        y_pair = (3, 0, 1, 2)
-        y_parts = {c: ((2 * y_pair[c], 0, 2), (2 * y_pair[c] + 1, 2, 4)) for c in range(quarters)}
 
         def y_pass(b, c):
             cols = slice(c * PARTS, (c + 1) * PARTS)
-            for bank, n0, n1 in y_parts[c]:
-                opens = b == 0
-                if opens:
-                    y_bank[c, n0] = psum.tile([PARTS, n1 - n0, PARTS], F32, name="bank%d" % bank)
-                for n in range(n0, n1):
+            for u in range(2):
+                if b == 0:
+                    y_bank[c, u] = psum.tile([PARTS, 2, PARTS], F32, name="bank%d" % (2 * ((c + 3) % QUARTERS) + u))
+                for v in range(2):
+                    n = 2 * u + v
                     nc.tensor.matmul_mx(
-                        out=y_bank[c, n0][:, n - n0, :],
+                        out=y_bank[c, u][:, v, :],
                         lhsT=w2_w[:, b, 2 * n * PARTS : 2 * (n + 1) * PARTS].bitcast(FP4X4),
                         lhsT_scale=w2_sc[:, b, n * PARTS : (n + 1) * PARTS],
                         rhs=z_codes[b][:, cols].bitcast(FP8X4),
                         rhs_scale=z_sc[b][:, cols],
-                        start=(opens and n == n0),
-                        stop=(not opens and n == n1 - 1),
+                        start=(b == 0 and v == 0),
+                        stop=(b == BANDS - 1 and v == 1),
                     )
 
         def store(c):
-            for bank, n0, n1 in y_parts[c]:
-                energy = keep.tile([PARTS, n1 - n0, PARTS], F32, name="energy%d" % bank, align_bytes=64)
-                nc.scalar.activation(energy[:], y_bank[c, n0][:], ACT.Square)
-                rows = out[n0 * PARTS : n1 * PARTS, c * PARTS : (c + 1) * PARTS]
+            for u in range(2):
+                energy = keep.tile([PARTS, 2, PARTS], F32, name="energy%d%d" % (c, u), align_bytes=64)
+                nc.scalar.activation(energy[:], y_bank[c, u][:], ACT.Square)
+                rows = out[2 * u * PARTS : 2 * (u + 1) * PARTS, c * PARTS : (c + 1) * PARTS]
                 nc.sync.dma_start(out=rows.rearrange("(n p) j -> p n j", p=PARTS), in_=energy[:])
 
         unused = keep.tile([PARTS, 1], F32, name="unused")
         nc.scalar.activation(unused[:], raw[0, 0][:, 0, 0:1], ACT.Abs_reciprocal_sqrt, scale=0.0, bias=1.0)
 
+        low, high = slice(0, PACK // 2), slice(PACK // 2, PACK)
+
         gather_hits(0)
         gather_hits(1)
         nc.vector.tensor_copy(hit_sc[:], tab_sc[:].indirect(offs_t[:]))
-        cast_w1("scalar", 0, 0)
+        cast_scalar(0, 0)
         quantize_w1(0, 0)
         for t in range(PACK - 1):
             h_pass(0, t, 0)
-        cast_w1("scalar", 0, 1, 0, 2)
-        cast_w1("vector", 0, 1, 2, 4)
+        cast_scalar(0, 1, low)
+        cast_vector(0, 1, high)
         quantize_w1(0, 1)
         for t in range(PACK - 1):
             h_pass(0, t, 1)
         gather_hits(2)
-        cast_w1("vector", 0, 2, 0, 2)
-        cast_w1("scalar", 0, 2, 2, 4)
+        cast_vector(0, 2, low)
+        cast_scalar(0, 2, high)
         for t in range(2):
             quantize_w1(0, 2, t, t + 1)
             h_pass(0, t, 2)
-        quantize_w1(0, 2, 2, 4)
+        quantize_w1(0, 2, 2, PACK)
         h_pass(0, 2, 2)
 
         for half in range(2):
-            cast_w1("vector", 1, 0, 0, PACK, half * PARTS // 2, (half + 1) * PARTS // 2)
+            cast_vector(1, 0, ms=slice(half * PARTS // 2, (half + 1) * PARTS // 2))
         evacuate(0, 0)
-        for a in range(PASSES):
-            h_pass(0, 3, a)
+        h_slice(0, 3)
         gather_first(0, 0)
         quantize_w1(1, 0)
-        evacuate(0, 1)
-        gather_first(0, 1)
-        evacuate(0, 2)
-        gather_first(0, 2)
-        evacuate(0, 3)
-        gather_first(0, 3)
-        cast_w1("gpsimd", 1, 1, 0, PACK, 0, SHARE)
-        cast_w1("scalar", 1, 1, 0, PACK, SHARE, PARTS)
+        for t in range(1, PACK):
+            evacuate(0, t)
+            gather_first(0, t)
+        cast_gpsimd(1, 1, slice(0, CAST_SHARE))
+        cast_scalar(1, 1, ms=slice(CAST_SHARE, PARTS))
         quantize_w1(1, 1)
-        cast_w1("scalar", 1, 2)
+        cast_scalar(1, 2)
         for t in range(2):
             for a in range(PASSES - 1):
                 h_pass(1, t, a)
@@ -282,49 +293,48 @@ def tile_list_hit_segment_energy_kernel(
 
         for t in range(2):
             gather_second(0, t)
-            magnitude(0, t, t + 1)
+            magnitude0(t)
         for t in range(2):
             inverse_root(0, t)
-        magnitude(0, 2, 3)
-        magnitude(0, 3, 4)
+        for t in range(2, PACK):
+            magnitude0(t)
         for t in range(2, PACK):
             gather_second(0, t)
-        evacuate(1, 0)
-        for a in range(PASSES):
-            h_pass(1, 2, a)
-        gather_first(1, 0)
         inverse_root(0, 2)
-        evacuate(1, 1)
-        for a in range(PASSES):
-            h_pass(1, 3, a)
-        gather_first(1, 1)
-        reciprocal(0, 0, 1)
-        gather_second(1, 0)
-        inverse_root(0, 3)
-        for t in range(2, PACK):
+
+        for t in range(2):
             evacuate(1, t)
+            h_slice(1, t + 2)
             gather_first(1, t)
-        reciprocal(0, 1, 2)
+        inverse_root(0, 3)
+        gather_second(1, 0)
+        evacuate(1, 2)
+        gather_first(1, 2)
+        reciprocal(0, 0, Z_SHARE)
+        form_z_gpsimd(0, 0, Z_SHARE)
+        evacuate(1, 3)
+        gather_first(1, 3)
+        reciprocal(0, Z_SHARE, P)
         gather_second(1, 1)
-        reciprocal(0, 2, 4)
-        magnitude(1, 0, 2)
-        form_z(0, 0, P)
+        magnitude1(0, 2)
+        form_z(0, Z_SHARE, P)
         gather_second(1, 2)
         quantize_z(0, 0, P)
-        for c in range(quarters):
+        for c in range(QUARTERS):
             y_pass(0, c)
         gather_second(1, 3)
-        magnitude(1, 2, 4)
+
+        magnitude1(2, PACK)
         for t in range(2):
             inverse_root(1, t)
         for t in range(2, PACK):
             inverse_root(1, t, 0, P // 2)
-        for c in range(quarters):
+        for c in range(QUARTERS):
             if c < 2:
                 inverse_root(1, 2 + c, P // 2, P)
-            reciprocal(1, 0, PACK, c * PARTS, (c + 1) * PARTS)
-        for c in range(quarters + 1):
-            if c < quarters:
+            reciprocal(1, c * PARTS, (c + 1) * PARTS)
+        for c in range(QUARTERS + 1):
+            if c < QUARTERS:
                 form_z(1, c * PARTS, (c + 1) * PARTS)
             if c > 0:
                 quantize_z(1, (c - 1) * PARTS, c * PARTS)

@@ -18,6 +18,7 @@ MULT = mybir.AluOpType.mult
 ADD = mybir.AluOpType.add
 
 PARTS = 128
+HALF = PARTS // 2
 PACK = 4
 K_PASS = PARTS * PACK
 PASSES = K // K_PASS
@@ -26,8 +27,7 @@ BANK = 512
 QUADRANTS = 4
 QUARTERS = P // PARTS
 GROUP = 16
-CAST_SHARE = 80
-Z_SHARE = 160
+GROUPS = ((0, K_PASS // 2), (K_PASS // 2, K_PASS // 2), (K_PASS, K_PASS))
 
 
 def tile_list_hit_segment_energy_kernel(
@@ -36,57 +36,91 @@ def tile_list_hit_segment_energy_kernel(
     nc = tc.nc
     with ExitStack() as ctx:
         keep = ctx.enter_context(tc.tile_pool(name="keep", bufs=1))
+        placed = ctx.enter_context(tc.tile_pool(name="placed", bufs=1))
         psum = ctx.enter_context(tc.psum_pool(name="psum", bufs=1))
+
+        def tile(shape, dtype, name):
+            return keep.tile(shape, dtype, name=name, align_bytes=64)
 
         offs_t = keep.tile([PARTS, S // GROUP], U16, name="offs_t")
         pos1_t = keep.tile([PARTS, P // GROUP], U16, name="pos1_t")
         pos2_t = keep.tile([PARTS, P // GROUP], U16, name="pos2_t")
-        knee_t = keep.tile([PARTS, BANDS, PACK], F32, name="knee_t")
-        tab = [keep.tile([PARTS, T], I32, name="tab%d" % a, align_bytes=64) for a in range(PASSES)]
-        tab_sc = keep.tile([PARTS, T], U8, name="tab_sc", align_bytes=64)
-        hit = [keep.tile([PARTS, S], U32, name="hit%d" % a, align_bytes=64) for a in range(PASSES)]
-        hit_sc = keep.tile([PARTS, S], U8, name="hit_sc", align_bytes=64)
-        raw = {}
+        knee_half = keep.tile([PARTS, 2, 2], F32, name="knee_half")
+        knee_band = keep.tile([PARTS, PACK], F32, name="knee_band")
+        tab = [tile([PARTS, T], I32, "tab%d" % a) for a in range(PASSES)]
+        tab_sc = tile([PARTS, T], U8, "tab_sc")
+        hit = [tile([PARTS, S], U32, "hit%d" % a) for a in range(PASSES)]
+        hit_sc = tile([PARTS, S], U8, "hit_sc")
+        w2_w = tile([PARTS, BANDS, 2 * N], U8, "w2_w")
+        w2_sc = tile([PARTS, BANDS, N], U8, "w2_sc")
+
+        late = tile([PARTS, PACK * P], F32, "late")
+        late_rows = late[:].rearrange("p (r j) -> p r j", j=P)
+        pair_bf = placed.tile([PARTS, PACK * K_PASS], BF16, name="pair_bf", align_bytes=64, offset=0)
+        last_codes = tile([PARTS, 2 * K_PASS], U32, "last_codes")
+        last_sc = tile([PARTS, 2 * K_PASS], U8, "last_sc")
+        pair_codes = tile([PARTS, K_PASS], U32, "pair_codes")
+        pair_sc = tile([PARTS, K_PASS], U8, "pair_sc")
+        flat = {}
+        grouped = {}
         w1_codes = {}
         w1_sc = {}
-        for b in range(BANDS):
+        for g, (c0, width) in enumerate(GROUPS):
             for a in range(PASSES):
-                if (b, a) != (1, 0):
-                    piece = keep.tile([PARTS, PACK, K_PASS], F32, name="raw%d%d" % (b, a), align_bytes=64)
-                    raw[b, a] = piece[:]
-                w1_codes[b, a] = keep.tile([PARTS, K_PASS], U32, name="w1c%d%d" % (b, a), align_bytes=64)
-                w1_sc[b, a] = keep.tile([PARTS, K_PASS], U8, name="w1s%d%d" % (b, a), align_bytes=64)
-        early = keep.tile([PARTS, P // 2 + PACK * K_PASS], F32, name="early", align_bytes=64)
-        raw[1, 0] = early[:, P // 2 :].rearrange("p (j c) -> p j c", j=PACK)
-        w2_w = keep.tile([PARTS, BANDS, 2 * N], U8, name="w2_w", align_bytes=64)
-        w2_sc = keep.tile([PARTS, BANDS, N], U8, name="w2_sc", align_bytes=64)
+                if (g, a) == (2, 2):
+                    flat[g, a] = late[:, 0 : PACK * P]
+                elif (g, a) == (2, 0):
+                    flat[g, a] = placed.tile([PARTS, PACK * width], F32, name="raw20", align_bytes=64, offset=16 * P)[:]
+                else:
+                    flat[g, a] = tile([PARTS, PACK * width], F32, "raw%d%d" % (g, a))[:]
+                if g == 1 and a < 2:
+                    grouped[g, a] = pair_bf[:, a * PACK * width : (a + 1) * PACK * width]
+                    w1_codes[g, a] = pair_codes[:, a * width : (a + 1) * width]
+                    w1_sc[g, a] = pair_sc[:, a * width : (a + 1) * width]
+                elif g == 2 and a > 0:
+                    w1_codes[g, a] = last_codes[:, (a - 1) * width : a * width]
+                    w1_sc[g, a] = last_sc[:, (a - 1) * width : a * width]
+                else:
+                    if g != 1:
+                        grouped[g, a] = tile([PARTS, PACK * width], BF16, "grouped%d%d" % (g, a))[:]
+                    w1_codes[g, a] = tile([PARTS, width], U32, "w1c%d%d" % (g, a))[:]
+                    w1_sc[g, a] = tile([PARTS, width], U8, "w1s%d%d" % (g, a))[:]
+
+        def rows(ap):
+            return ap.rearrange("p (r j) -> p r j", j=P)
 
         def load_tab(a):
             nc.sync.dma_start(out=tab[a][:], in_=tab_words[a].rearrange("p t i -> p (t i)").bitcast(I32))
 
-        def load_w1(b, a):
-            rows = w1[a * K_PASS : (a + 1) * K_PASS, b * K_PASS : (b + 1) * K_PASS]
-            nc.sync.dma_start(out=raw[b, a], in_=rows.rearrange("(p j) c -> p j c", j=PACK))
+        def load_w1(g, a):
+            c0, width = GROUPS[g]
+            src = w1[a * K_PASS : (a + 1) * K_PASS, c0 : c0 + width]
+            nc.sync.dma_start(
+                out=flat[g, a].rearrange("p (j c) -> p j c", j=PACK), in_=src.rearrange("(p j) c -> p j c", j=PACK)
+            )
 
         nc.vector.memset(tab_sc[:].bitcast(I32), 0)
         nc.sync.dma_start(offs_t[:], offs)
         load_tab(0)
-        load_tab(1)
         load_w1(0, 0)
         for q in range(QUADRANTS):
             nc.sync.dma_start(
                 out=tab_sc[32 * q : 32 * q + 4 * PASSES, :].bitcast(I32),
                 in_=tab_scales[:, 4 * q : 4 * q + 4, :].bitcast(I32),
             )
+        load_tab(1)
         load_w1(0, 1)
         load_tab(2)
         load_w1(0, 2)
-        nc.sync.dma_start(pos1_t[:], pos1)
         load_w1(1, 0)
-        nc.sync.dma_start(pos2_t[:], pos2)
+        nc.sync.dma_start(pos1_t[:], pos1)
         load_w1(1, 1)
         load_w1(1, 2)
-        nc.sync.dma_start(out=knee_t[:], in_=knee.rearrange("(b p t) -> p b t", b=BANDS, t=PACK))
+        nc.sync.dma_start(pos2_t[:], pos2)
+        nc.sync.dma_start(out=knee_half[:], in_=knee[0:K_PASS].rearrange("(g q s) -> q g s", g=2, s=2))
+        for a in range(PASSES):
+            load_w1(2, a)
+        nc.sync.dma_start(out=knee_band[:], in_=knee[K_PASS:].rearrange("(p t) -> p t", t=PACK))
         nc.sync.dma_start(out=w2_w[:].bitcast(I32), in_=w2_words.rearrange("b p n -> p b n").bitcast(I32))
         nc.vector.memset(w2_sc[:].rearrange("p b n -> p (b n)").bitcast(I32), 0)
         for q in range(QUADRANTS):
@@ -95,120 +129,131 @@ def tile_list_hit_segment_energy_kernel(
                 in_=w2_scales[:, 4 * q : 4 * q + 4, :].rearrange("b r n -> r b n").bitcast(I32),
             )
 
-        def gather_hits(a):
-            nc.vector.tensor_copy(hit[a][:], tab[a][:].bitcast(U32).indirect(offs_t[:]))
-
-        late = keep.tile([PARTS, (PACK + 2) * P], F32, name="late", align_bytes=64)
-        late_rows = late[:].rearrange("p (r j) -> p r j", j=P)
-        prod = {0: raw[1, 2], 1: late_rows[:, 1 : PACK + 1, :]}
-        grouped = {}
-        for a in range(PASSES):
-            rounded = keep.tile([PARTS, PACK * K_PASS], BF16, name="grouped%d" % a, align_bytes=64)
-            grouped[0, a] = rounded[:]
-        grouped[1, 2] = late[:, 0 : 2 * P].bitcast(BF16)
-        overlap = keep.tile([PARTS, (PACK + PACK // 2) * K_PASS], BF16, name="overlap", align_bytes=64)
-        grouped[1, 0] = overlap[:, 0 : PACK * K_PASS]
-        grouped[1, 1] = overlap[:, PACK // 2 * K_PASS :]
-        mag0 = [raw[1, 2][:, 2, :], raw[1, 2][:, 3, :], late_rows[:, 0, :], late_rows[:, 1, :]]
-        mag1 = raw[0, 1]
-        root = {0: late_rows[:, 2:, :], 1: raw[1, 0]}
-        recip = {0: raw[0, 2], 1: raw[1, 1]}
-
-        def cast_views(b, a, ts, ms):
-            dst = grouped[b, a].rearrange("p (t m j) -> p m j t", t=PACK, j=PACK)[:, ms, :, ts]
-            src = raw[b, a].rearrange("p j (m t) -> p m j t", t=PACK)[:, ms, :, ts]
-            return dst, src
-
-        def cast_vector(b, a, ts=slice(0, PACK), ms=slice(0, PARTS)):
-            nc.vector.tensor_copy(*cast_views(b, a, ts, ms))
-
-        def cast_scalar(b, a, ts=slice(0, PACK), ms=slice(0, PARTS)):
-            nc.scalar.activation(*cast_views(b, a, ts, ms), ACT.Copy)
-
-        def cast_gpsimd(b, a, ms):
-            dst = grouped[b, a].rearrange("p (t m j) -> p t m j", t=PACK, j=PACK)[:, :, ms, :]
-            src = raw[b, a].rearrange("p j (m t) -> p t m j", t=PACK)[:, :, ms, :]
-            nc.gpsimd.tensor_scalar(dst, src, 1.0, 0.0, MULT, ADD)
-
-        def quantize_w1(b, a, t0=0, t1=PACK):
-            cols = slice(t0 * PARTS, t1 * PARTS)
-            nc.vector.quantize_mx(
-                out=w1_codes[b, a][:, cols].bitcast(FP8X4),
-                scales=w1_sc[b, a][:, cols],
-                in_=grouped[b, a][:, t0 * K_PASS : t1 * K_PASS],
+        def gather_hits(a, i0=0, i1=S):
+            nc.vector.tensor_copy(
+                hit[a][:, i0:i1], tab[a][:].bitcast(U32).indirect(offs_t[:, i0 // GROUP : i1 // GROUP])
             )
 
-        h_bank = {}
-        h_pair = {(0, t): t % 3 for t in range(PACK)}
-        for t in range(PACK):
-            h_pair[1, t] = 1 + t % 2
+        def cast_views(g, a, ms=slice(0, PARTS)):
+            if g < 2:
+                dst = grouped[g, a].rearrange("p (s m u j) -> p m j u s", s=2, u=2, j=PACK)
+                src = flat[g, a].rearrange("p (j m u s) -> p m j u s", j=PACK, u=2, s=2)
+                return dst, src
+            dst = grouped[g, a].rearrange("p (t m j) -> p m j t", t=PACK, j=PACK)
+            src = flat[g, a].rearrange("p (j m t) -> p m j t", j=PACK, t=PACK)
+            return dst[:, ms], src[:, ms]
 
-        def h_pass(b, t, a):
-            for half in range(2):
+        def cast_gpsimd_half(g, a):
+            dst = grouped[g, a].rearrange("p (s q j) -> p s q j", s=2, j=PACK)
+            src = flat[g, a].rearrange("p (j q s) -> p s q j", j=PACK, s=2)
+            nc.gpsimd.tensor_scalar(dst, src, 1.0, 0.0, MULT, ADD)
+
+        def cast_gpsimd_band(g, a):
+            dst = grouped[g, a].rearrange("p (t m j) -> p m t j", t=PACK, j=PACK)
+            src = flat[g, a].rearrange("p (j m t) -> p m t j", j=PACK, t=PACK)
+            nc.gpsimd.tensor_scalar(dst, src, 1.0, 0.0, MULT, ADD)
+
+        def cast_vector(g, a):
+            nc.vector.tensor_copy(*cast_views(g, a))
+
+        def cast_scalar(g, a, ms=slice(0, PARTS)):
+            nc.scalar.copy(*cast_views(g, a, ms))
+
+        def quantize_w1(g, a):
+            nc.vector.quantize_mx(out=w1_codes[g, a].bitcast(FP8X4), scales=w1_sc[g, a], in_=grouped[g, a])
+
+        h_bank = {}
+
+        def h_pass(g, s, a, halves=(0, 1)):
+            pair = 2 + s if g == 1 else s
+            for half in halves:
                 if a == 0:
-                    h_bank[b, t, half] = psum.tile([PARTS, BANK], F32, name="bank%d" % (2 * h_pair[b, t] + half))
+                    h_bank[g, s, half] = psum.tile([PARTS, BANK], F32, name="bank%d" % (2 * pair + half))
                 cols = slice(half * BANK, (half + 1) * BANK)
-                wcols = slice(t * PARTS, (t + 1) * PARTS)
+                wcols = slice(s * PARTS, (s + 1) * PARTS)
                 nc.tensor.matmul_mx(
-                    out=h_bank[b, t, half][:],
-                    lhsT=w1_codes[b, a][:, wcols].bitcast(FP8X4),
-                    lhsT_scale=w1_sc[b, a][:, wcols],
+                    out=h_bank[g, s, half][:],
+                    lhsT=w1_codes[g, a][:, wcols].bitcast(FP8X4),
+                    lhsT_scale=w1_sc[g, a][:, wcols],
                     rhs=hit[a][:, cols].bitcast(FP8X4),
                     rhs_scale=hit_sc[4 * a :, cols],
                     start=(a == 0),
                     stop=(a == PASSES - 1),
                 )
 
-        def h_slice(b, t):
-            for a in range(PASSES):
-                h_pass(b, t, a)
-
         h_t = {}
-        first = [keep.tile([PARTS, PACK, P], F32, name="first%d" % b, align_bytes=64) for b in range(BANDS)]
-        picked = {(b, t): first[b][:, t, :] for b in range(BANDS) for t in range(PACK)}
-        picked[0, 0] = early[:, 0:P]
-        z_bf = [keep.tile([PARTS, P, PACK], BF16, name="z_bf%d" % b, align_bytes=64) for b in range(BANDS)]
-        z_codes = [keep.tile([PARTS, P], U32, name="z_codes%d" % b, align_bytes=64) for b in range(BANDS)]
-        z_sc = [keep.tile([PARTS, P], U8, name="z_sc%d" % b, align_bytes=64) for b in range(BANDS)]
+        first = [None, tile([PARTS, 2, P], F32, "first1")[:], tile([PARTS, PACK, P], F32, "first2")[:]]
+        prod = [rows(flat[1, 2]), late_rows[:, 2:4, :], late_rows]
+        mag = [late_rows[:, 0:2, :], late_rows[:, 0:2, :], tile([PARTS, PACK, P], F32, "mag2")[:]]
+        root2 = tile([PARTS, PACK, P], F32, "root2")
+        root_half = [rows(flat[1, 1])[:, s, :] for s in range(2)]
+        root = [root_half, root_half, [root2[:, t, :] for t in range(PACK)]]
+        recip = [rows(flat[0, 0]), rows(flat[0, 1]), tile([PARTS, PACK, P], F32, "recip2")[:]]
+        z_words = tile([PARTS, 2, 2 * P], BF16, "z_words")
+        z_bf = [tile([PARTS, P, PACK], BF16, "z_bf%d" % b) for b in range(BANDS)]
+        z_codes = [tile([PARTS, P], U32, "z_codes%d" % b) for b in range(BANDS)]
+        z_sc = [tile([PARTS, P], U8, "z_sc%d" % b) for b in range(BANDS)]
 
-        def evacuate(b, t):
-            h_t[b, t] = keep.tile([PARTS, S], F32, name="h%d%d" % (b, t), align_bytes=64)
+        def evacuate(g, s, shared=False):
+            if g == 1:
+                h_t[g, s] = placed.tile([PARTS, S], F32, name="h1%d" % s, align_bytes=64, offset=(20 + 8 * s) * P)
+            else:
+                h_t[g, s] = tile([PARTS, S], F32, "raw10" if (g, s) == (0, 0) else "h%d%d" % (g, s))
             for half in range(2):
-                dst = h_t[b, t][:, half * BANK : (half + 1) * BANK]
-                nc.scalar.activation(dst, h_bank[b, t, half][:], ACT.Copy)
+                dst = h_t[g, s][:, half * BANK : (half + 1) * BANK]
+                if shared and half == 1:
+                    nc.vector.tensor_copy(dst, h_bank[g, s, half][:])
+                else:
+                    nc.scalar.copy(dst, h_bank[g, s, half][:])
 
-        def gather_first(b, t):
-            nc.vector.tensor_copy(picked[b, t], h_t[b, t][:].indirect(pos1_t[:]))
+        def gather_first(g, s):
+            nc.vector.tensor_copy(first[g][:, s, :], h_t[g, s][:].indirect(pos1_t[:]))
 
-        def gather_second(b, t):
-            nc.vector.tensor_tensor(prod[b][:, t, :], h_t[b, t][:].indirect(pos2_t[:]), picked[b, t], MULT)
+        def gather_second(g, s):
+            nc.vector.tensor_tensor(prod[g][:, s, :], h_t[g, s][:].indirect(pos2_t[:]), first[g][:, s, :], MULT)
 
-        def magnitude0(t):
-            nc.scalar.activation(mag0[t], picked[0, t], ACT.Abs)
+        def magnitude(g, s0, s1):
+            nc.scalar.activation(mag[g][:, s0:s1, :], first[g][:, s0:s1, :], ACT.Abs)
 
-        def magnitude1(t0, t1):
-            nc.scalar.activation(mag1[:, t0:t1, :], first[1][:, t0:t1, :], ACT.Abs)
+        def inverse_root(g, s, j0=0, j1=P):
+            bias = knee_half[:, g, s : s + 1] if g < 2 else knee_band[:, s : s + 1]
+            nc.scalar.activation(root[g][s][:, j0:j1], mag[g][:, s, j0:j1], ACT.Abs_reciprocal_sqrt, bias=bias)
 
-        def inverse_root(b, t, j0=0, j1=P):
-            src = mag0[t][:, j0:j1] if b == 0 else mag1[:, t, j0:j1]
-            nc.scalar.activation(root[b][:, t, j0:j1], src, ACT.Abs_reciprocal_sqrt, bias=knee_t[:, b, t : t + 1])
+        def reciprocal(g, j0, j1):
+            nc.scalar.activation(recip[g][:, :, j0:j1], root2[:, :, j0:j1], ACT.Square)
 
-        def reciprocal(b, j0, j1):
-            nc.scalar.activation(recip[b][:, :, j0:j1], root[b][:, :, j0:j1], ACT.Square)
+        def reciprocal_half(g):
+            for s in range(2):
+                nc.scalar.activation(recip[g][:, s, :], root[g][s], ACT.Square)
 
-        def form_z(b, j0, j1):
-            nc.vector.tensor_tensor(
-                z_bf[b][:, j0:j1, :].rearrange("p (c i) t -> p c t i", i=4),
-                prod[b][:, :, j0:j1].rearrange("p t (c i) -> p c t i", i=4),
-                recip[b][:, :, j0:j1].rearrange("p t (c i) -> p c t i", i=4),
+        def form_z_half(g, after):
+            if g == 0:
+                pairs = placed.tile([PARTS, P, 2], BF16, name="pairs0", align_bytes=64, offset=28 * P)
+            else:
+                pairs = tile([PARTS, P, 2], BF16, "h%d%d" % after)
+            nc.gpsimd.tensor_tensor(
+                pairs[:].rearrange("p (c i) s -> p c s i", i=4),
+                prod[g].rearrange("p s (c i) -> p c s i", i=4),
+                recip[g].rearrange("p s (c i) -> p c s i", i=4),
                 MULT,
             )
+            for u in range(2):
+                nc.sync.dma_start(
+                    out=z_words[g * HALF : (g + 1) * HALF, u, :],
+                    in_=pairs[u:PARTS:2, :, :].rearrange("p j s -> p (j s)"),
+                )
 
-        def form_z_gpsimd(b, j0, j1):
-            nc.gpsimd.tensor_tensor(
-                z_bf[b][:, j0:j1, :],
-                prod[b][:, :, j0:j1].rearrange("p t j -> p j t"),
-                recip[b][:, :, j0:j1].rearrange("p t j -> p j t"),
+        def weave_z():
+            nc.vector.tensor_copy(
+                z_bf[0][:].rearrange("p j t -> p (j t)").bitcast(I32).rearrange("p (c i u) -> p c u i", i=2, u=2),
+                z_words[:].bitcast(I32).rearrange("p u (c i) -> p c u i", i=2),
+            )
+
+        def form_z(j0, j1):
+            nc.vector.tensor_tensor(
+                z_bf[1][:, j0:j1, :].rearrange("p (c i) t -> p c t i", i=4),
+                prod[2][:, :, j0:j1].rearrange("p t (c i) -> p c t i", i=4),
+                recip[2][:, :, j0:j1].rearrange("p t (c i) -> p c t i", i=4),
                 MULT,
             )
 
@@ -225,7 +270,7 @@ def tile_list_hit_segment_energy_kernel(
             cols = slice(c * PARTS, (c + 1) * PARTS)
             for u in range(2):
                 if b == 0:
-                    y_bank[c, u] = psum.tile([PARTS, 2, PARTS], F32, name="bank%d" % (2 * ((c + 3) % QUARTERS) + u))
+                    y_bank[c, u] = psum.tile([PARTS, 2, PARTS], F32, name="bank%d" % (2 * c + u))
                 for v in range(2):
                     n = 2 * u + v
                     nc.tensor.matmul_mx(
@@ -240,103 +285,105 @@ def tile_list_hit_segment_energy_kernel(
 
         def store(c):
             for u in range(2):
-                energy = keep.tile([PARTS, 2, PARTS], F32, name="energy%d%d" % (c, u), align_bytes=64)
+                energy = tile([PARTS, 2, PARTS], F32, "energy%d%d" % (c, u))
                 nc.scalar.activation(energy[:], y_bank[c, u][:], ACT.Square)
-                rows = out[2 * u * PARTS : 2 * (u + 1) * PARTS, c * PARTS : (c + 1) * PARTS]
-                nc.sync.dma_start(out=rows.rearrange("(n p) j -> p n j", p=PARTS), in_=energy[:])
+                dst = out[2 * u * PARTS : 2 * (u + 1) * PARTS, c * PARTS : (c + 1) * PARTS]
+                nc.sync.dma_start(out=dst.rearrange("(n p) j -> p n j", p=PARTS), in_=energy[:])
 
         unused = keep.tile([PARTS, 1], F32, name="unused")
-        nc.scalar.activation(unused[:], raw[0, 0][:, 0, 0:1], ACT.Abs_reciprocal_sqrt, scale=0.0, bias=1.0)
-
-        low, high = slice(0, PACK // 2), slice(PACK // 2, PACK)
+        nc.scalar.activation(unused[:], flat[0, 0][:, 0:1], ACT.Abs_reciprocal_sqrt, scale=0.0, bias=1.0)
 
         gather_hits(0)
-        gather_hits(1)
         nc.vector.tensor_copy(hit_sc[:], tab_sc[:].indirect(offs_t[:]))
-        cast_scalar(0, 0)
-        quantize_w1(0, 0)
-        for t in range(PACK - 1):
-            h_pass(0, t, 0)
-        cast_scalar(0, 1, low)
-        cast_vector(0, 1, high)
-        quantize_w1(0, 1)
-        for t in range(PACK - 1):
-            h_pass(0, t, 1)
-        gather_hits(2)
-        cast_vector(0, 2, low)
-        cast_scalar(0, 2, high)
-        for t in range(2):
-            quantize_w1(0, 2, t, t + 1)
-            h_pass(0, t, 2)
-        quantize_w1(0, 2, 2, PACK)
-        h_pass(0, 2, 2)
-
-        for half in range(2):
-            cast_vector(1, 0, ms=slice(half * PARTS // 2, (half + 1) * PARTS // 2))
-        evacuate(0, 0)
-        h_slice(0, 3)
-        gather_first(0, 0)
-        quantize_w1(1, 0)
-        for t in range(1, PACK):
-            evacuate(0, t)
-            gather_first(0, t)
-        cast_gpsimd(1, 1, slice(0, CAST_SHARE))
-        cast_scalar(1, 1, ms=slice(CAST_SHARE, PARTS))
-        quantize_w1(1, 1)
-        cast_scalar(1, 2)
-        for t in range(2):
-            for a in range(PASSES - 1):
-                h_pass(1, t, a)
+        for a in range(PASSES):
+            if a > 0:
+                gather_hits(a)
+            cast_scalar(0, a)
+            quantize_w1(0, a)
+            for s in range(2):
+                h_pass(0, s, a)
+        cast_scalar(1, 0)
+        cast_vector(1, 1)
+        nc.vector.quantize_mx(
+            out=pair_codes[:].bitcast(FP8X4), scales=pair_sc[:], in_=pair_bf[:]
+        )
+        first[0] = placed.tile([PARTS, 2, P], F32, name="first0", align_bytes=64, offset=4 * P)[:]
+        grouped[1, 2] = placed.tile([PARTS, 2 * P], BF16, name="grouped12", align_bytes=64, offset=0)[:]
+        for a in range(PASSES - 1):
+            for s in range(2):
+                h_pass(1, s, a)
+        for s in range(2):
+            evacuate(0, s)
+            gather_first(0, s)
+        cast_gpsimd_half(1, 2)
         quantize_w1(1, 2)
-        for t in range(2):
-            h_pass(1, t, PASSES - 1)
-
-        for t in range(2):
-            gather_second(0, t)
-            magnitude0(t)
-        for t in range(2):
-            inverse_root(0, t)
-        for t in range(2, PACK):
-            magnitude0(t)
-        for t in range(2, PACK):
-            gather_second(0, t)
-        inverse_root(0, 2)
-
-        for t in range(2):
-            evacuate(1, t)
-            h_slice(1, t + 2)
-            gather_first(1, t)
-        inverse_root(0, 3)
-        gather_second(1, 0)
-        evacuate(1, 2)
-        gather_first(1, 2)
-        reciprocal(0, 0, Z_SHARE)
-        form_z_gpsimd(0, 0, Z_SHARE)
-        evacuate(1, 3)
-        gather_first(1, 3)
-        reciprocal(0, Z_SHARE, P)
-        gather_second(1, 1)
-        magnitude1(0, 2)
-        form_z(0, Z_SHARE, P)
-        gather_second(1, 2)
-        quantize_z(0, 0, P)
-        for c in range(QUARTERS):
+        for s in range(2):
+            h_pass(1, s, PASSES - 1)
+        for s in range(2):
+            gather_second(0, s)
+        cast_scalar(2, 0)
+        quantize_w1(2, 0)
+        for s in range(2):
+            h_pass(2, s, 0)
+        for s in range(2):
+            evacuate(1, s)
+            h_pass(2, s + 2, 0)
+            gather_first(1, s)
+        last_bf = tile([PARTS, 2 * PACK * K_PASS], BF16, "grouped20")
+        for a in range(1, PASSES):
+            grouped[2, a] = last_bf[:, (a - 1) * PACK * K_PASS : a * PACK * K_PASS]
+        cast_gpsimd_band(2, 1)
+        cast_scalar(2, 2)
+        nc.vector.quantize_mx(out=last_codes[:].bitcast(FP8X4), scales=last_sc[:], in_=last_bf[:])
+        for s in range(PACK):
+            for a in range(1, PASSES):
+                h_pass(2, s, a)
+        for s in range(2):
+            gather_second(1, s)
+        for s in range(2):
+            magnitude(0, s, s + 1)
+        for s in range(2):
+            inverse_root(0, s)
+        reciprocal_half(0)
+        form_z_half(0, (1, 1))
+        for s in range(2):
+            evacuate(2, s, shared=(s == 0))
+            gather_first(2, s)
+        for s in range(2):
+            magnitude(1, s, s + 1)
+        for s in range(2):
+            inverse_root(1, s)
+            gather_second(2, s)
+        evacuate(2, 2)
+        reciprocal_half(1)
+        form_z_half(1, (2, 1))
+        gather_first(2, 2)
+        evacuate(2, 3)
+        gather_first(2, 3)
+        for s in range(2, PACK):
+            gather_second(2, s)
+        weave_z()
+        magnitude(2, 0, 2)
+        magnitude(2, 2, PACK)
+        quantize_z(0, 0, P // 2)
+        for c in range(2):
             y_pass(0, c)
-        gather_second(1, 3)
-
-        magnitude1(2, PACK)
         for t in range(2):
-            inverse_root(1, t)
+            inverse_root(2, t)
         for t in range(2, PACK):
-            inverse_root(1, t, 0, P // 2)
+            inverse_root(2, t, 0, P // 2)
         for c in range(QUARTERS):
             if c < 2:
-                inverse_root(1, 2 + c, P // 2, P)
-            reciprocal(1, c * PARTS, (c + 1) * PARTS)
+                inverse_root(2, 2 + c, P // 2, P)
+            reciprocal(2, c * PARTS, (c + 1) * PARTS)
         for c in range(QUARTERS + 1):
             if c < QUARTERS:
-                form_z(1, c * PARTS, (c + 1) * PARTS)
+                form_z(c * PARTS, (c + 1) * PARTS)
             if c > 0:
                 quantize_z(1, (c - 1) * PARTS, c * PARTS)
                 y_pass(1, c - 1)
                 store(c - 1)
+            if c == 1:
+                quantize_z(0, P // 2, P)
+                for d in range(2, QUARTERS):
+                    y_pass(0, d)

@@ -56,11 +56,14 @@ def tile_list_hit_segment_energy_kernel(
 
         late = tile([PARTS, PACK * P], F32, "late")
         late_rows = late[:].rearrange("p (r j) -> p r j", j=P)
-        pair_bf = placed.tile([PARTS, PACK * K_PASS], BF16, name="pair_bf", align_bytes=64, offset=0)
         last_codes = tile([PARTS, 2 * K_PASS], U32, "last_codes")
         last_sc = tile([PARTS, 2 * K_PASS], U8, "last_sc")
         pair_codes = tile([PARTS, K_PASS], U32, "pair_codes")
         pair_sc = tile([PARTS, K_PASS], U8, "pair_sc")
+
+        def place(shape, dtype, name, row):
+            return placed.tile(shape, dtype, name=name, align_bytes=64, offset=row * 4 * P)
+
         flat = {}
         grouped = {}
         w1_codes = {}
@@ -69,19 +72,21 @@ def tile_list_hit_segment_energy_kernel(
             for a in range(PASSES):
                 if (g, a) == (2, 2):
                     flat[g, a] = late[:, 0 : PACK * P]
+                elif (g, a) == (1, 0):
+                    flat[g, a] = place([PARTS, PACK * width], F32, "raw10", 3)[:]
                 elif (g, a) == (2, 0):
-                    flat[g, a] = placed.tile([PARTS, PACK * width], F32, name="raw20", align_bytes=64, offset=16 * P)[:]
+                    flat[g, a] = place([PARTS, PACK * width], F32, "raw20", 7)[:]
                 else:
                     flat[g, a] = tile([PARTS, PACK * width], F32, "raw%d%d" % (g, a))[:]
-                if g == 1 and a < 2:
-                    grouped[g, a] = pair_bf[:, a * PACK * width : (a + 1) * PACK * width]
-                    w1_codes[g, a] = pair_codes[:, a * width : (a + 1) * width]
-                    w1_sc[g, a] = pair_sc[:, a * width : (a + 1) * width]
+                if g == 1 and a > 0:
+                    w1_codes[g, a] = pair_codes[:, (a - 1) * width : a * width]
+                    w1_sc[g, a] = pair_sc[:, (a - 1) * width : a * width]
                 elif g == 2 and a > 0:
-                    w1_codes[g, a] = last_codes[:, (a - 1) * width : a * width]
-                    w1_sc[g, a] = last_sc[:, (a - 1) * width : a * width]
+                    continue
                 else:
-                    if g != 1:
+                    if g == 1:
+                        grouped[g, a] = place([PARTS, PACK * width], BF16, "grouped10", 0)[:]
+                    else:
                         grouped[g, a] = tile([PARTS, PACK * width], BF16, "grouped%d%d" % (g, a))[:]
                     w1_codes[g, a] = tile([PARTS, width], U32, "w1c%d%d" % (g, a))[:]
                     w1_sc[g, a] = tile([PARTS, width], U8, "w1s%d%d" % (g, a))[:]
@@ -134,14 +139,14 @@ def tile_list_hit_segment_energy_kernel(
                 hit[a][:, i0:i1], tab[a][:].bitcast(U32).indirect(offs_t[:, i0 // GROUP : i1 // GROUP])
             )
 
-        def cast_views(g, a, ms=slice(0, PARTS)):
+        def cast_views(g, a, ts=slice(0, PACK)):
             if g < 2:
                 dst = grouped[g, a].rearrange("p (s m u j) -> p m j u s", s=2, u=2, j=PACK)
                 src = flat[g, a].rearrange("p (j m u s) -> p m j u s", j=PACK, u=2, s=2)
                 return dst, src
-            dst = grouped[g, a].rearrange("p (t m j) -> p m j t", t=PACK, j=PACK)
+            dst = grouped[g, a].rearrange("p t (m j) -> p m j t", j=PACK)
             src = flat[g, a].rearrange("p (j m t) -> p m j t", j=PACK, t=PACK)
-            return dst[:, ms], src[:, ms]
+            return dst[:, :, :, ts], src[:, :, :, ts]
 
         def cast_gpsimd_half(g, a):
             dst = grouped[g, a].rearrange("p (s q j) -> p s q j", s=2, j=PACK)
@@ -149,32 +154,40 @@ def tile_list_hit_segment_energy_kernel(
             nc.gpsimd.tensor_scalar(dst, src, 1.0, 0.0, MULT, ADD)
 
         def cast_gpsimd_band(g, a):
-            dst = grouped[g, a].rearrange("p (t m j) -> p m t j", t=PACK, j=PACK)
+            dst = grouped[g, a].rearrange("p t (m j) -> p m t j", j=PACK)
             src = flat[g, a].rearrange("p (j m t) -> p m t j", j=PACK, t=PACK)
             nc.gpsimd.tensor_scalar(dst, src, 1.0, 0.0, MULT, ADD)
 
-        def cast_vector(g, a):
-            nc.vector.tensor_copy(*cast_views(g, a))
+        def cast_scalar(g, a, ts=slice(0, PACK)):
+            nc.scalar.copy(*cast_views(g, a, ts))
 
-        def cast_scalar(g, a, ms=slice(0, PARTS)):
-            nc.scalar.copy(*cast_views(g, a, ms))
+        def quantize(codes, scales, rounded):
+            nc.vector.quantize_mx(out=codes.bitcast(FP8X4), scales=scales, in_=rounded)
 
         def quantize_w1(g, a):
-            nc.vector.quantize_mx(out=w1_codes[g, a].bitcast(FP8X4), scales=w1_sc[g, a], in_=grouped[g, a])
+            quantize(w1_codes[g, a], w1_sc[g, a], grouped[g, a])
+
+        def quantize_last(u0, u1):
+            cols = slice(u0 * PARTS, u1 * PARTS)
+            quantize(last_codes[:, cols], last_sc[:, cols], last_bf[:, u0 * K_PASS : u1 * K_PASS])
 
         h_bank = {}
 
         def h_pass(g, s, a, halves=(0, 1)):
-            pair = 2 + s if g == 1 else s
+            pair = (s + 2) % PACK if g == 2 else s
             for half in halves:
                 if a == 0:
                     h_bank[g, s, half] = psum.tile([PARTS, BANK], F32, name="bank%d" % (2 * pair + half))
                 cols = slice(half * BANK, (half + 1) * BANK)
-                wcols = slice(s * PARTS, (s + 1) * PARTS)
+                if g == 2 and a > 0:
+                    codes, scales, unit = last_codes, last_sc, 2 * s + a - 1
+                else:
+                    codes, scales, unit = w1_codes[g, a], w1_sc[g, a], s
+                wcols = slice(unit * PARTS, (unit + 1) * PARTS)
                 nc.tensor.matmul_mx(
                     out=h_bank[g, s, half][:],
-                    lhsT=w1_codes[g, a][:, wcols].bitcast(FP8X4),
-                    lhsT_scale=w1_sc[g, a][:, wcols],
+                    lhsT=codes[:, wcols].bitcast(FP8X4),
+                    lhsT_scale=scales[:, wcols],
                     rhs=hit[a][:, cols].bitcast(FP8X4),
                     rhs_scale=hit_sc[4 * a :, cols],
                     start=(a == 0),
@@ -182,29 +195,30 @@ def tile_list_hit_segment_energy_kernel(
                 )
 
         h_t = {}
-        first = [None, tile([PARTS, 2, P], F32, "first1")[:], tile([PARTS, PACK, P], F32, "first2")[:]]
-        prod = [rows(flat[1, 2]), late_rows[:, 2:4, :], late_rows]
-        mag = [late_rows[:, 0:2, :], late_rows[:, 0:2, :], tile([PARTS, PACK, P], F32, "mag2")[:]]
+        first = [tile([PARTS, 2, P], F32, "first0")[:], tile([PARTS, 2, P], F32, "first1")[:], tile([PARTS, PACK, P], F32, "first2")[:]]
+        prod = [None, late_rows[:, 2:4, :], late_rows]
+        mag2 = tile([PARTS, PACK, P], F32, "mag2")
+        mag = [
+            [rows(flat[0, 2])[:, 0, :], None],
+            [late_rows[:, s, :] for s in range(2)],
+            [mag2[:, t, :] for t in range(PACK)],
+        ]
         root2 = tile([PARTS, PACK, P], F32, "root2")
         root_half = [rows(flat[1, 1])[:, s, :] for s in range(2)]
-        root = [root_half, root_half, [root2[:, t, :] for t in range(PACK)]]
+        root = [[None, root_half[1]], root_half, [root2[:, t, :] for t in range(PACK)]]
         recip = [rows(flat[0, 0]), rows(flat[0, 1]), tile([PARTS, PACK, P], F32, "recip2")[:]]
         z_words = tile([PARTS, 2, 2 * P], BF16, "z_words")
         z_bf = [tile([PARTS, P, PACK], BF16, "z_bf%d" % b) for b in range(BANDS)]
         z_codes = [tile([PARTS, P], U32, "z_codes%d" % b) for b in range(BANDS)]
         z_sc = [tile([PARTS, P], U8, "z_sc%d" % b) for b in range(BANDS)]
 
-        def evacuate(g, s, shared=False):
-            if g == 1:
-                h_t[g, s] = placed.tile([PARTS, S], F32, name="h1%d" % s, align_bytes=64, offset=(20 + 8 * s) * P)
+        def evacuate(g, s):
+            if g < 2:
+                h_t[g, s] = place([PARTS, S], F32, "h%d%d" % (g, s), 2 + 6 * g + 2 * s)
             else:
-                h_t[g, s] = tile([PARTS, S], F32, "raw10" if (g, s) == (0, 0) else "h%d%d" % (g, s))
+                h_t[g, s] = tile([PARTS, S], F32, "h%d%d" % (g, s))
             for half in range(2):
-                dst = h_t[g, s][:, half * BANK : (half + 1) * BANK]
-                if shared and half == 1:
-                    nc.vector.tensor_copy(dst, h_bank[g, s, half][:])
-                else:
-                    nc.scalar.copy(dst, h_bank[g, s, half][:])
+                nc.scalar.copy(h_t[g, s][:, half * BANK : (half + 1) * BANK], h_bank[g, s, half][:])
 
         def gather_first(g, s):
             nc.vector.tensor_copy(first[g][:, s, :], h_t[g, s][:].indirect(pos1_t[:]))
@@ -212,12 +226,15 @@ def tile_list_hit_segment_energy_kernel(
         def gather_second(g, s):
             nc.vector.tensor_tensor(prod[g][:, s, :], h_t[g, s][:].indirect(pos2_t[:]), first[g][:, s, :], MULT)
 
-        def magnitude(g, s0, s1):
-            nc.scalar.activation(mag[g][:, s0:s1, :], first[g][:, s0:s1, :], ACT.Abs)
+        def magnitude(g, s):
+            nc.scalar.activation(mag[g][s], first[g][:, s, :], ACT.Abs)
+
+        def magnitude_band(t0, t1):
+            nc.scalar.activation(mag2[:, t0:t1, :], first[2][:, t0:t1, :], ACT.Abs)
 
         def inverse_root(g, s, j0=0, j1=P):
             bias = knee_half[:, g, s : s + 1] if g < 2 else knee_band[:, s : s + 1]
-            nc.scalar.activation(root[g][s][:, j0:j1], mag[g][:, s, j0:j1], ACT.Abs_reciprocal_sqrt, bias=bias)
+            nc.scalar.activation(root[g][s][:, j0:j1], mag[g][s][:, j0:j1], ACT.Abs_reciprocal_sqrt, bias=bias)
 
         def reciprocal(g, j0, j1):
             nc.scalar.activation(recip[g][:, :, j0:j1], root2[:, :, j0:j1], ACT.Square)
@@ -228,7 +245,7 @@ def tile_list_hit_segment_energy_kernel(
 
         def form_z_half(g, after):
             if g == 0:
-                pairs = placed.tile([PARTS, P, 2], BF16, name="pairs0", align_bytes=64, offset=28 * P)
+                pairs = place([PARTS, P, 2], BF16, "pairs0", 10)
             else:
                 pairs = tile([PARTS, P, 2], BF16, "h%d%d" % after)
             nc.gpsimd.tensor_tensor(
@@ -265,14 +282,16 @@ def tile_list_hit_segment_energy_kernel(
             )
 
         y_bank = {}
+        y_banks = ((4, 5), (6, 7), (0, 1), (2, 3))
 
         def y_pass(b, c):
             cols = slice(c * PARTS, (c + 1) * PARTS)
-            for u in range(2):
+            per = QUARTERS // len(y_banks[c])
+            for u, bank in enumerate(y_banks[c]):
                 if b == 0:
-                    y_bank[c, u] = psum.tile([PARTS, 2, PARTS], F32, name="bank%d" % (2 * c + u))
-                for v in range(2):
-                    n = 2 * u + v
+                    y_bank[c, u] = psum.tile([PARTS, per, PARTS], F32, name="bank%d" % bank)
+                for v in range(per):
+                    n = per * u + v
                     nc.tensor.matmul_mx(
                         out=y_bank[c, u][:, v, :],
                         lhsT=w2_w[:, b, 2 * n * PARTS : 2 * (n + 1) * PARTS].bitcast(FP4X4),
@@ -280,14 +299,15 @@ def tile_list_hit_segment_energy_kernel(
                         rhs=z_codes[b][:, cols].bitcast(FP8X4),
                         rhs_scale=z_sc[b][:, cols],
                         start=(b == 0 and v == 0),
-                        stop=(b == BANDS - 1 and v == 1),
+                        stop=(b == BANDS - 1 and v == per - 1),
                     )
 
         def store(c):
-            for u in range(2):
-                energy = tile([PARTS, 2, PARTS], F32, "energy%d%d" % (c, u))
+            per = QUARTERS // len(y_banks[c])
+            for u in range(len(y_banks[c])):
+                energy = tile([PARTS, per, PARTS], F32, "energy%d%d" % (c, u))
                 nc.scalar.activation(energy[:], y_bank[c, u][:], ACT.Square)
-                dst = out[2 * u * PARTS : 2 * (u + 1) * PARTS, c * PARTS : (c + 1) * PARTS]
+                dst = out[per * u * PARTS : per * (u + 1) * PARTS, c * PARTS : (c + 1) * PARTS]
                 nc.sync.dma_start(out=dst.rearrange("(n p) j -> p n j", p=PARTS), in_=energy[:])
 
         unused = keep.tile([PARTS, 1], F32, name="unused")
@@ -295,34 +315,42 @@ def tile_list_hit_segment_energy_kernel(
 
         gather_hits(0)
         nc.vector.tensor_copy(hit_sc[:], tab_sc[:].indirect(offs_t[:]))
-        for a in range(PASSES):
+        for a in range(PASSES - 1):
             if a > 0:
                 gather_hits(a)
             cast_scalar(0, a)
             quantize_w1(0, a)
             for s in range(2):
                 h_pass(0, s, a)
-        cast_scalar(1, 0)
-        cast_vector(1, 1)
-        nc.vector.quantize_mx(
-            out=pair_codes[:].bitcast(FP8X4), scales=pair_sc[:], in_=pair_bf[:]
-        )
-        first[0] = placed.tile([PARTS, 2, P], F32, name="first0", align_bytes=64, offset=4 * P)[:]
-        grouped[1, 2] = placed.tile([PARTS, 2 * P], BF16, name="grouped12", align_bytes=64, offset=0)[:]
-        for a in range(PASSES - 1):
+        for half in range(2):
+            gather_hits(PASSES - 1, half * BANK, (half + 1) * BANK)
+            if half == 0:
+                cast_scalar(0, PASSES - 1)
+                quantize_w1(0, PASSES - 1)
             for s in range(2):
-                h_pass(1, s, a)
+                h_pass(0, s, PASSES - 1, (half,))
+        cast_scalar(1, 0)
+        quantize_w1(1, 0)
         for s in range(2):
             evacuate(0, s)
+            h_pass(1, s, 0)
             gather_first(0, s)
-        cast_gpsimd_half(1, 2)
-        quantize_w1(1, 2)
+        pair_bf = place([PARTS, PACK * K_PASS], BF16, "pair_bf", 0)
+        for a in range(1, PASSES):
+            grouped[1, a] = pair_bf[:, (a - 1) * 2 * P : a * 2 * P]
+            cast_gpsimd_half(1, a)
+        nc.vector.quantize_mx(out=pair_codes[:].bitcast(FP8X4), scales=pair_sc[:], in_=pair_bf[:])
+        prod[0] = place([PARTS, 2, P], F32, "prod0", 0)[:]
         for s in range(2):
-            h_pass(1, s, PASSES - 1)
+            for a in range(1, PASSES):
+                h_pass(1, s, a)
         for s in range(2):
             gather_second(0, s)
+        magnitude(0, 0)
+        whole = grouped[2, 0]
+        grouped[2, 0] = whole.rearrange("p (t c) -> p t c", t=PACK)
         cast_scalar(2, 0)
-        quantize_w1(2, 0)
+        quantize(w1_codes[2, 0], w1_sc[2, 0], whole)
         for s in range(2):
             h_pass(2, s, 0)
         for s in range(2):
@@ -331,26 +359,36 @@ def tile_list_hit_segment_energy_kernel(
             gather_first(1, s)
         last_bf = tile([PARTS, 2 * PACK * K_PASS], BF16, "grouped20")
         for a in range(1, PASSES):
-            grouped[2, a] = last_bf[:, (a - 1) * PACK * K_PASS : a * PACK * K_PASS]
+            grouped[2, a] = last_bf[:].rearrange("p (t a c) -> p a t c", t=PACK, a=2)[:, a - 1]
         cast_gpsimd_band(2, 1)
-        cast_scalar(2, 2)
-        nc.vector.quantize_mx(out=last_codes[:].bitcast(FP8X4), scales=last_sc[:], in_=last_bf[:])
-        for s in range(PACK):
-            for a in range(1, PASSES):
-                h_pass(2, s, a)
-        for s in range(2):
-            gather_second(1, s)
-        for s in range(2):
-            magnitude(0, s, s + 1)
+        quantize_last(0, 1)
+        h_pass(2, 0, 1)
+        nc.vector.tensor_copy(*cast_views(2, 2, slice(0, 2)))
+        cast_scalar(2, 2, slice(2, PACK))
+        stage = place([PARTS, 2, P], F32, "stage", 6)
+        mag[0][1] = stage[:, 0, :]
+        root[0][0] = stage[:, 1, :]
+        magnitude(0, 1)
         for s in range(2):
             inverse_root(0, s)
         reciprocal_half(0)
+        quantize_last(1, 2)
+        h_pass(2, 0, 2)
+        quantize_last(2, 4)
+        for a in range(1, PASSES):
+            h_pass(2, 1, a)
+        gather_second(1, 0)
+        quantize_last(4, 8)
+        for s in range(2, PACK):
+            for a in range(1, PASSES):
+                h_pass(2, s, a)
+        gather_second(1, 1)
         form_z_half(0, (1, 1))
         for s in range(2):
-            evacuate(2, s, shared=(s == 0))
+            evacuate(2, s)
             gather_first(2, s)
         for s in range(2):
-            magnitude(1, s, s + 1)
+            magnitude(1, s)
         for s in range(2):
             inverse_root(1, s)
             gather_second(2, s)
@@ -363,8 +401,8 @@ def tile_list_hit_segment_energy_kernel(
         for s in range(2, PACK):
             gather_second(2, s)
         weave_z()
-        magnitude(2, 0, 2)
-        magnitude(2, 2, PACK)
+        magnitude_band(0, 2)
+        magnitude_band(2, PACK)
         quantize_z(0, 0, P // 2)
         for c in range(2):
             y_pass(0, c)

@@ -64,6 +64,7 @@ def tile_list_hit_segment_energy_kernel(
         def place(shape, dtype, name, row):
             return placed.tile(shape, dtype, name=name, align_bytes=64, offset=row * 4 * P)
 
+        pair_bf = place([PARTS, PACK * K_PASS], BF16, "pair_bf", 13)
         flat = {}
         grouped = {}
         w1_codes = {}
@@ -78,15 +79,14 @@ def tile_list_hit_segment_energy_kernel(
                     flat[g, a] = place([PARTS, PACK * width], F32, "raw20", 7)[:]
                 else:
                     flat[g, a] = tile([PARTS, PACK * width], F32, "raw%d%d" % (g, a))[:]
-                if g == 1 and a > 0:
-                    w1_codes[g, a] = pair_codes[:, (a - 1) * width : a * width]
-                    w1_sc[g, a] = pair_sc[:, (a - 1) * width : a * width]
+                if g == 1 and a < 2:
+                    grouped[g, a] = pair_bf[:, a * PACK * width : (a + 1) * PACK * width]
+                    w1_codes[g, a] = pair_codes[:, a * width : (a + 1) * width]
+                    w1_sc[g, a] = pair_sc[:, a * width : (a + 1) * width]
                 elif g == 2 and a > 0:
                     continue
                 else:
-                    if g == 1:
-                        grouped[g, a] = place([PARTS, PACK * width], BF16, "grouped10", 0)[:]
-                    else:
+                    if g != 1:
                         grouped[g, a] = tile([PARTS, PACK * width], BF16, "grouped%d%d" % (g, a))[:]
                     w1_codes[g, a] = tile([PARTS, width], U32, "w1c%d%d" % (g, a))[:]
                     w1_sc[g, a] = tile([PARTS, width], U8, "w1s%d%d" % (g, a))[:]
@@ -144,18 +144,18 @@ def tile_list_hit_segment_energy_kernel(
                 dst = grouped[g, a].rearrange("p (s m u j) -> p m j u s", s=2, u=2, j=PACK)
                 src = flat[g, a].rearrange("p (j m u s) -> p m j u s", j=PACK, u=2, s=2)
                 return dst, src
-            dst = grouped[g, a].rearrange("p t (m j) -> p m j t", j=PACK)
+            dst = grouped[g, a, ts.start].rearrange("p t (m j) -> p m j t", j=PACK)
             src = flat[g, a].rearrange("p (j m t) -> p m j t", j=PACK, t=PACK)
-            return dst[:, :, :, ts], src[:, :, :, ts]
+            return dst, src[:, :, :, ts]
 
         def cast_gpsimd_half(g, a):
-            dst = grouped[g, a].rearrange("p (s q j) -> p s q j", s=2, j=PACK)
-            src = flat[g, a].rearrange("p (j q s) -> p s q j", j=PACK, s=2)
+            dst = grouped[g, a].rearrange("p (s q j) -> p q s j", s=2, j=PACK)
+            src = flat[g, a].rearrange("p (j q s) -> p q s j", j=PACK, s=2)
             nc.gpsimd.tensor_scalar(dst, src, 1.0, 0.0, MULT, ADD)
 
-        def cast_gpsimd_band(g, a):
-            dst = grouped[g, a].rearrange("p t (m j) -> p m t j", j=PACK)
-            src = flat[g, a].rearrange("p (j m t) -> p m t j", j=PACK, t=PACK)
+        def cast_gpsimd_band(g, a, ts):
+            dst = grouped[g, a, ts.start].rearrange("p t (m j) -> p m t j", j=PACK)
+            src = flat[g, a].rearrange("p (j m t) -> p m t j", j=PACK, t=PACK)[:, :, ts, :]
             nc.gpsimd.tensor_scalar(dst, src, 1.0, 0.0, MULT, ADD)
 
         def cast_scalar(g, a, ts=slice(0, PACK)):
@@ -169,7 +169,8 @@ def tile_list_hit_segment_energy_kernel(
 
         def quantize_last(u0, u1):
             cols = slice(u0 * PARTS, u1 * PARTS)
-            quantize(last_codes[:, cols], last_sc[:, cols], last_bf[:, u0 * K_PASS : u1 * K_PASS])
+            rounded = last_bf[u0 // PACK][:, u0 % PACK * K_PASS : ((u1 - 1) % PACK + 1) * K_PASS]
+            quantize(last_codes[:, cols], last_sc[:, cols], rounded)
 
         h_bank = {}
 
@@ -195,7 +196,7 @@ def tile_list_hit_segment_energy_kernel(
                 )
 
         h_t = {}
-        first = [tile([PARTS, 2, P], F32, "first0")[:], tile([PARTS, 2, P], F32, "first1")[:], tile([PARTS, PACK, P], F32, "first2")[:]]
+        first = [None, tile([PARTS, 2, P], F32, "first1")[:], tile([PARTS, PACK, P], F32, "first2")[:]]
         prod = [None, late_rows[:, 2:4, :], late_rows]
         mag2 = tile([PARTS, PACK, P], F32, "mag2")
         mag = [
@@ -330,25 +331,25 @@ def tile_list_hit_segment_energy_kernel(
             for s in range(2):
                 h_pass(0, s, PASSES - 1, (half,))
         cast_scalar(1, 0)
-        quantize_w1(1, 0)
+        nc.vector.tensor_copy(*cast_views(1, 1))
+        quantize(pair_codes[:], pair_sc[:], pair_bf[:])
+        first[0] = place([PARTS, 2, P], F32, "first0", 14)[:]
         for s in range(2):
             evacuate(0, s)
-            h_pass(1, s, 0)
-            gather_first(0, s)
-        pair_bf = place([PARTS, PACK * K_PASS], BF16, "pair_bf", 0)
-        for a in range(1, PASSES):
-            grouped[1, a] = pair_bf[:, (a - 1) * 2 * P : a * 2 * P]
-            cast_gpsimd_half(1, a)
-        nc.vector.quantize_mx(out=pair_codes[:].bitcast(FP8X4), scales=pair_sc[:], in_=pair_bf[:])
-        prod[0] = place([PARTS, 2, P], F32, "prod0", 0)[:]
-        for s in range(2):
-            for a in range(1, PASSES):
+            for a in range(PASSES - 1):
                 h_pass(1, s, a)
+            gather_first(0, s)
+        grouped[1, 2] = place([PARTS, 2 * P], BF16, "grouped12", 13)[:]
+        cast_gpsimd_half(1, 2)
+        quantize_w1(1, 2)
+        prod[0] = place([PARTS, 2, P], F32, "prod0", 12)[:]
+        for s in range(2):
+            h_pass(1, s, PASSES - 1)
         for s in range(2):
             gather_second(0, s)
         magnitude(0, 0)
         whole = grouped[2, 0]
-        grouped[2, 0] = whole.rearrange("p (t c) -> p t c", t=PACK)
+        grouped[2, 0, 0] = whole.rearrange("p (t c) -> p t c", t=PACK)
         cast_scalar(2, 0)
         quantize(w1_codes[2, 0], w1_sc[2, 0], whole)
         for s in range(2):
@@ -357,18 +358,20 @@ def tile_list_hit_segment_energy_kernel(
             evacuate(1, s)
             h_pass(2, s + 2, 0)
             gather_first(1, s)
-        last_bf = tile([PARTS, 2 * PACK * K_PASS], BF16, "grouped20")
-        for a in range(1, PASSES):
-            grouped[2, a] = last_bf[:].rearrange("p (t a c) -> p a t c", t=PACK, a=2)[:, a - 1]
-        cast_gpsimd_band(2, 1)
-        quantize_last(0, 1)
-        h_pass(2, 0, 1)
-        nc.vector.tensor_copy(*cast_views(2, 2, slice(0, 2)))
-        cast_scalar(2, 2, slice(2, PACK))
         stage = place([PARTS, 2, P], F32, "stage", 6)
         mag[0][1] = stage[:, 0, :]
         root[0][0] = stage[:, 1, :]
         magnitude(0, 1)
+        last_bf = [place([PARTS, PACK * K_PASS], BF16, "low_bf", 14), tile([PARTS, PACK * K_PASS], BF16, "grouped20")]
+        for a in range(1, PASSES):
+            for pair in range(2):
+                grouped[2, a, 2 * pair] = last_bf[pair][:].rearrange("p (t a c) -> p a t c", t=2, a=2)[:, a - 1]
+        cast_gpsimd_band(2, 1, slice(2, PACK))
+        for a in range(1, PASSES):
+            nc.vector.tensor_copy(*cast_views(2, a, slice(0, 2)))
+        quantize_last(0, 1)
+        h_pass(2, 0, 1)
+        cast_scalar(2, 2, slice(2, PACK))
         for s in range(2):
             inverse_root(0, s)
         reciprocal_half(0)

@@ -62,9 +62,9 @@ def tile_list_hit_segment_energy_kernel(
         pair_sc = tile([PARTS, K_PASS], U8, "pair_sc")
 
         def place(shape, dtype, name, row):
-            return placed.tile(shape, dtype, name=name, align_bytes=64, offset=row * 4 * P)
+            return placed.tile(shape, dtype, name=name, align_bytes=64, offset=int(row * 4 * P))
 
-        pair_bf = place([PARTS, PACK * K_PASS], BF16, "pair_bf", 13)
+        pair_bf = place([PARTS, PACK * K_PASS], BF16, "pair_bf", 15)
         flat = {}
         grouped = {}
         w1_codes = {}
@@ -86,7 +86,9 @@ def tile_list_hit_segment_energy_kernel(
                 elif g == 2 and a > 0:
                     continue
                 else:
-                    if g != 1:
+                    if g == 2:
+                        grouped[g, a] = place([PARTS, PACK * width], BF16, "grouped20", 12)[:]
+                    elif g == 0:
                         grouped[g, a] = tile([PARTS, PACK * width], BF16, "grouped%d%d" % (g, a))[:]
                     w1_codes[g, a] = tile([PARTS, width], U32, "w1c%d%d" % (g, a))[:]
                     w1_sc[g, a] = tile([PARTS, width], U8, "w1s%d%d" % (g, a))[:]
@@ -105,8 +107,8 @@ def tile_list_hit_segment_energy_kernel(
             )
 
         nc.vector.memset(tab_sc[:].bitcast(I32), 0)
-        nc.sync.dma_start(offs_t[:], offs)
         load_tab(0)
+        nc.sync.dma_start(offs_t[:], offs)
         load_w1(0, 0)
         for q in range(QUADRANTS):
             nc.sync.dma_start(
@@ -215,7 +217,7 @@ def tile_list_hit_segment_energy_kernel(
 
         def evacuate(g, s):
             if g < 2:
-                h_t[g, s] = place([PARTS, S], F32, "h%d%d" % (g, s), 2 + 6 * g + 2 * s)
+                h_t[g, s] = place([PARTS, S], F32, "h%d%d" % (g, s), 2 + 2 * s if g == 0 else 10 - 2 * s)
             else:
                 h_t[g, s] = tile([PARTS, S], F32, "h%d%d" % (g, s))
             for half in range(2):
@@ -246,7 +248,7 @@ def tile_list_hit_segment_energy_kernel(
 
         def form_z_half(g, after):
             if g == 0:
-                pairs = place([PARTS, P, 2], BF16, "pairs0", 10)
+                pairs = place([PARTS, P, 2], BF16, "pairs0", 11.5)
             else:
                 pairs = tile([PARTS, P, 2], BF16, "h%d%d" % after)
             nc.gpsimd.tensor_tensor(
@@ -333,16 +335,16 @@ def tile_list_hit_segment_energy_kernel(
         cast_scalar(1, 0)
         nc.vector.tensor_copy(*cast_views(1, 1))
         quantize(pair_codes[:], pair_sc[:], pair_bf[:])
-        first[0] = place([PARTS, 2, P], F32, "first0", 14)[:]
+        first[0] = place([PARTS, 2, P], F32, "first0", 16)[:]
         for s in range(2):
             evacuate(0, s)
             for a in range(PASSES - 1):
                 h_pass(1, s, a)
             gather_first(0, s)
-        grouped[1, 2] = place([PARTS, 2 * P], BF16, "grouped12", 13)[:]
+        grouped[1, 2] = place([PARTS, 2 * P], BF16, "grouped12", 15)[:]
         cast_gpsimd_half(1, 2)
         quantize_w1(1, 2)
-        prod[0] = place([PARTS, 2, P], F32, "prod0", 12)[:]
+        prod[0] = place([PARTS, 2, P], F32, "prod0", 14)[:]
         for s in range(2):
             h_pass(1, s, PASSES - 1)
         for s in range(2):
@@ -362,7 +364,7 @@ def tile_list_hit_segment_energy_kernel(
         mag[0][1] = stage[:, 0, :]
         root[0][0] = stage[:, 1, :]
         magnitude(0, 1)
-        last_bf = [place([PARTS, PACK * K_PASS], BF16, "low_bf", 14), tile([PARTS, PACK * K_PASS], BF16, "grouped20")]
+        last_bf = [place([PARTS, PACK * K_PASS], BF16, "low_bf", 16), place([PARTS, PACK * K_PASS], BF16, "high_bf", 12)]
         for a in range(1, PASSES):
             for pair in range(2):
                 grouped[2, a, 2 * pair] = last_bf[pair][:].rearrange("p (t a c) -> p a t c", t=2, a=2)[:, a - 1]
@@ -397,7 +399,7 @@ def tile_list_hit_segment_energy_kernel(
             gather_second(2, s)
         evacuate(2, 2)
         reciprocal_half(1)
-        form_z_half(1, (2, 1))
+        form_z_half(1, (2, 0))
         gather_first(2, 2)
         evacuate(2, 3)
         gather_first(2, 3)

@@ -64,7 +64,6 @@ def tile_list_hit_segment_energy_kernel(
         def place(shape, dtype, name, row):
             return placed.tile(shape, dtype, name=name, align_bytes=64, offset=int(row * 4 * P))
 
-        pair_bf = place([PARTS, PACK * K_PASS], BF16, "pair_bf", 15)
         flat = {}
         grouped = {}
         w1_codes = {}
@@ -79,16 +78,17 @@ def tile_list_hit_segment_energy_kernel(
                     flat[g, a] = place([PARTS, PACK * width], F32, "raw20", 7)[:]
                 else:
                     flat[g, a] = tile([PARTS, PACK * width], F32, "raw%d%d" % (g, a))[:]
-                if g == 1 and a < 2:
-                    grouped[g, a] = pair_bf[:, a * PACK * width : (a + 1) * PACK * width]
-                    w1_codes[g, a] = pair_codes[:, a * width : (a + 1) * width]
-                    w1_sc[g, a] = pair_sc[:, a * width : (a + 1) * width]
+                if g == 1 and a > 0:
+                    w1_codes[g, a] = pair_codes[:, (a - 1) * width : a * width]
+                    w1_sc[g, a] = pair_sc[:, (a - 1) * width : a * width]
                 elif g == 2 and a > 0:
                     continue
                 else:
                     if g == 2:
                         grouped[g, a] = place([PARTS, PACK * width], BF16, "grouped20", 12)[:]
-                    elif g == 0:
+                    elif g == 1:
+                        grouped[g, a] = place([PARTS, PACK * width], BF16, "grouped10", 14)[:]
+                    else:
                         grouped[g, a] = tile([PARTS, PACK * width], BF16, "grouped%d%d" % (g, a))[:]
                     w1_codes[g, a] = tile([PARTS, width], U32, "w1c%d%d" % (g, a))[:]
                     w1_sc[g, a] = tile([PARTS, width], U8, "w1s%d%d" % (g, a))[:]
@@ -198,7 +198,7 @@ def tile_list_hit_segment_energy_kernel(
                 )
 
         h_t = {}
-        first = [None, tile([PARTS, 2, P], F32, "first1")[:], tile([PARTS, PACK, P], F32, "first2")[:]]
+        first = [place([PARTS, 2, P], F32, "first0", 16)[:], tile([PARTS, 2, P], F32, "first1")[:], tile([PARTS, PACK, P], F32, "first2")[:]]
         prod = [None, late_rows[:, 2:4, :], late_rows]
         mag2 = tile([PARTS, PACK, P], F32, "mag2")
         mag = [
@@ -231,9 +231,6 @@ def tile_list_hit_segment_energy_kernel(
 
         def magnitude(g, s):
             nc.scalar.activation(mag[g][s], first[g][:, s, :], ACT.Abs)
-
-        def magnitude_band(t0, t1):
-            nc.scalar.activation(mag2[:, t0:t1, :], first[2][:, t0:t1, :], ACT.Abs)
 
         def inverse_root(g, s, j0=0, j1=P):
             bias = knee_half[:, g, s : s + 1] if g < 2 else knee_band[:, s : s + 1]
@@ -333,20 +330,20 @@ def tile_list_hit_segment_energy_kernel(
             for s in range(2):
                 h_pass(0, s, PASSES - 1, (half,))
         cast_scalar(1, 0)
-        nc.vector.tensor_copy(*cast_views(1, 1))
-        quantize(pair_codes[:], pair_sc[:], pair_bf[:])
-        first[0] = place([PARTS, 2, P], F32, "first0", 16)[:]
+        quantize_w1(1, 0)
         for s in range(2):
             evacuate(0, s)
-            for a in range(PASSES - 1):
-                h_pass(1, s, a)
+            h_pass(1, s, 0)
             gather_first(0, s)
-        grouped[1, 2] = place([PARTS, 2 * P], BF16, "grouped12", 15)[:]
-        cast_gpsimd_half(1, 2)
-        quantize_w1(1, 2)
+        pair_bf = place([PARTS, PACK * K_PASS], BF16, "pair_bf", 14)
+        for a in range(1, PASSES):
+            grouped[1, a] = pair_bf[:, (a - 1) * 2 * P : a * 2 * P]
+            cast_gpsimd_half(1, a)
+        quantize(pair_codes[:], pair_sc[:], pair_bf[:])
         prod[0] = place([PARTS, 2, P], F32, "prod0", 14)[:]
         for s in range(2):
-            h_pass(1, s, PASSES - 1)
+            for a in range(1, PASSES):
+                h_pass(1, s, a)
         for s in range(2):
             gather_second(0, s)
         magnitude(0, 0)
@@ -389,11 +386,11 @@ def tile_list_hit_segment_energy_kernel(
                 h_pass(2, s, a)
         gather_second(1, 1)
         form_z_half(0, (1, 1))
+        magnitude(1, 0)
         for s in range(2):
             evacuate(2, s)
             gather_first(2, s)
-        for s in range(2):
-            magnitude(1, s)
+        magnitude(1, 1)
         for s in range(2):
             inverse_root(1, s)
             gather_second(2, s)
@@ -406,13 +403,15 @@ def tile_list_hit_segment_energy_kernel(
         for s in range(2, PACK):
             gather_second(2, s)
         weave_z()
-        magnitude_band(0, 2)
-        magnitude_band(2, PACK)
         quantize_z(0, 0, P // 2)
         for c in range(2):
             y_pass(0, c)
         for t in range(2):
+            magnitude(2, t)
+        for t in range(2):
             inverse_root(2, t)
+        for t in range(2, PACK):
+            magnitude(2, t)
         for t in range(2, PACK):
             inverse_root(2, t, 0, P // 2)
         for c in range(QUARTERS):

@@ -123,10 +123,11 @@ def tile_list_hit_segment_energy_kernel(
         nc.sync.dma_start(pos1_t[:], pos1)
         load_w1(1, 1)
         load_w1(1, 2)
+        load_w1(2, 0)
         nc.sync.dma_start(pos2_t[:], pos2)
-        nc.sync.dma_start(out=knee_half[:], in_=knee[0:K_PASS].rearrange("(g q s) -> q g s", g=2, s=2))
-        for a in range(PASSES):
+        for a in range(1, PASSES):
             load_w1(2, a)
+        nc.sync.dma_start(out=knee_half[:], in_=knee[0:K_PASS].rearrange("(g q s) -> q g s", g=2, s=2))
         nc.sync.dma_start(out=knee_band[:], in_=knee[K_PASS:].rearrange("(p t) -> p t", t=PACK))
         nc.sync.dma_start(out=w2_w[:].bitcast(I32), in_=w2_words.rearrange("b p n -> p b n").bitcast(I32))
         nc.vector.memset(w2_sc[:].rearrange("p b n -> p (b n)").bitcast(I32), 0)

@@ -211,13 +211,15 @@ def tile_list_hit_segment_energy_kernel(
         root_half = [rows(flat[1, 1])[:, s, :] for s in range(2)]
         root = [[None, root_half[1]], root_half, [root2[:, t, :] for t in range(PACK)]]
         recip = [rows(flat[0, 0]), rows(flat[0, 1]), tile([PARTS, PACK, P], F32, "recip2")[:]]
-        z_words = tile([PARTS, 2, 2 * P], BF16, "z_words")
+        z_words = [tile([PARTS, 2, P], BF16, "z_words%d" % half) for half in range(2)]
         z_bf = [tile([PARTS, P, PACK], BF16, "z_bf%d" % b) for b in range(BANDS)]
         z_codes = [tile([PARTS, P], U32, "z_codes%d" % b) for b in range(BANDS)]
         z_sc = [tile([PARTS, P], U8, "z_sc%d" % b) for b in range(BANDS)]
 
         def evacuate(g, s):
-            if g < 2:
+            if (g, s) == (2, 0):
+                h_t[g, s] = place([PARTS, S], F32, "h20", 0)
+            elif g < 2:
                 h_t[g, s] = place([PARTS, S], F32, "h%d%d" % (g, s), 2 + 2 * s if g == 0 else 10 - 2 * s)
             else:
                 h_t[g, s] = tile([PARTS, S], F32, "h%d%d" % (g, s))
@@ -244,27 +246,30 @@ def tile_list_hit_segment_energy_kernel(
             for s in range(2):
                 nc.scalar.activation(recip[g][:, s, :], root[g][s], ACT.Square)
 
-        def form_z_half(g, after):
-            if g == 0:
-                pairs = place([PARTS, P, 2], BF16, "pairs0", 11.5)
-            else:
-                pairs = tile([PARTS, P, 2], BF16, "h%d%d" % after)
-            nc.gpsimd.tensor_tensor(
-                pairs[:].rearrange("p (c i) s -> p c s i", i=4),
-                prod[g].rearrange("p s (c i) -> p c s i", i=4),
-                recip[g].rearrange("p s (c i) -> p c s i", i=4),
-                MULT,
-            )
-            for u in range(2):
-                nc.sync.dma_start(
-                    out=z_words[g * HALF : (g + 1) * HALF, u, :],
-                    in_=pairs[u:PARTS:2, :, :].rearrange("p j s -> p (j s)"),
-                )
+        def form_z_half(g):
+            width = P if g == 0 else P // 2
+            for half in range(2):
+                if half * (P // 2) % width == 0:
+                    part = slice(half * (P // 2), half * (P // 2) + width)
+                    pairs = place([PARTS, width, 2], BF16, "pairs%d%d" % (g, half), 11.5 if g == 0 else half)
+                    nc.gpsimd.tensor_tensor(
+                        pairs[:].rearrange("p (c i) s -> p c s i", i=4),
+                        prod[g][:, :, part].rearrange("p s (c i) -> p c s i", i=4),
+                        recip[g][:, :, part].rearrange("p s (c i) -> p c s i", i=4),
+                        MULT,
+                    )
+                cols = slice(half * (P // 2) % width, half * (P // 2) % width + P // 2)
+                for u in range(2):
+                    nc.sync.dma_start(
+                        out=z_words[half][g * HALF : (g + 1) * HALF, u, :],
+                        in_=pairs[u:PARTS:2, cols, :].rearrange("p j s -> p (j s)"),
+                    )
 
-        def weave_z():
+        def weave_z(half):
+            woven = z_bf[0][:, half * (P // 2) : (half + 1) * (P // 2), :].rearrange("p j t -> p (j t)")
             nc.vector.tensor_copy(
-                z_bf[0][:].rearrange("p j t -> p (j t)").bitcast(I32).rearrange("p (c i u) -> p c u i", i=2, u=2),
-                z_words[:].bitcast(I32).rearrange("p u (c i) -> p c u i", i=2),
+                woven.bitcast(I32).rearrange("p (c i u) -> p c u i", i=2, u=2),
+                z_words[half][:].bitcast(I32).rearrange("p u (c i) -> p c u i", i=2),
             )
 
         def form_z(j0, j1):
@@ -386,7 +391,7 @@ def tile_list_hit_segment_energy_kernel(
             for a in range(1, PASSES):
                 h_pass(2, s, a)
         gather_second(1, 1)
-        form_z_half(0, (1, 1))
+        form_z_half(0)
         magnitude(1, 0)
         for s in range(2):
             evacuate(2, s)
@@ -397,13 +402,13 @@ def tile_list_hit_segment_energy_kernel(
             gather_second(2, s)
         evacuate(2, 2)
         reciprocal_half(1)
-        form_z_half(1, (2, 0))
+        form_z_half(1)
         gather_first(2, 2)
         evacuate(2, 3)
         gather_first(2, 3)
         for s in range(2, PACK):
             gather_second(2, s)
-        weave_z()
+        weave_z(0)
         quantize_z(0, 0, P // 2)
         for c in range(2):
             y_pass(0, c)
@@ -426,6 +431,8 @@ def tile_list_hit_segment_energy_kernel(
                 quantize_z(1, (c - 1) * PARTS, c * PARTS)
                 y_pass(1, c - 1)
                 store(c - 1)
+            if c == 0:
+                weave_z(1)
             if c == 1:
                 quantize_z(0, P // 2, P)
                 for d in range(2, QUARTERS):

@@ -42,12 +42,16 @@ def tile_list_hit_segment_energy_kernel(
         def tile(shape, dtype, name):
             return keep.tile(shape, dtype, name=name, align_bytes=64)
 
+        def place(shape, dtype, name, row):
+            return placed.tile(shape, dtype, name=name, align_bytes=64, offset=int(row * 4 * P))
+
         offs_t = keep.tile([PARTS, S // GROUP], U16, name="offs_t")
         pos1_t = keep.tile([PARTS, P // GROUP], U16, name="pos1_t")
         pos2_t = keep.tile([PARTS, P // GROUP], U16, name="pos2_t")
         knee_half = keep.tile([PARTS, 2, 2], F32, name="knee_half")
         knee_band = keep.tile([PARTS, PACK], F32, name="knee_band")
-        tab = [tile([PARTS, T], I32, "tab%d" % a) for a in range(PASSES)]
+        tab = [tile([PARTS, T], I32, "tab%d" % a) for a in range(PASSES - 1)]
+        tab.append(place([PARTS, T], I32, "tab2", 18))
         tab_sc = tile([PARTS, T], U8, "tab_sc")
         hit = [tile([PARTS, S], U32, "hit%d" % a) for a in range(PASSES)]
         hit_sc = tile([PARTS, S], U8, "hit_sc")
@@ -60,9 +64,6 @@ def tile_list_hit_segment_energy_kernel(
         last_sc = tile([PARTS, 2 * K_PASS], U8, "last_sc")
         pair_codes = tile([PARTS, K_PASS], U32, "pair_codes")
         pair_sc = tile([PARTS, K_PASS], U8, "pair_sc")
-
-        def place(shape, dtype, name, row):
-            return placed.tile(shape, dtype, name=name, align_bytes=64, offset=int(row * 4 * P))
 
         flat = {}
         grouped = {}
@@ -90,7 +91,10 @@ def tile_list_hit_segment_energy_kernel(
                         grouped[g, a] = place([PARTS, PACK * width], BF16, "grouped10", 14)[:]
                     else:
                         grouped[g, a] = tile([PARTS, PACK * width], BF16, "grouped%d%d" % (g, a))[:]
-                    w1_codes[g, a] = tile([PARTS, width], U32, "w1c%d%d" % (g, a))[:]
+                    if g == 1:
+                        w1_codes[g, a] = place([PARTS, width], U32, "w1c10", 18)[:]
+                    else:
+                        w1_codes[g, a] = tile([PARTS, width], U32, "w1c%d%d" % (g, a))[:]
                     w1_sc[g, a] = tile([PARTS, width], U8, "w1s%d%d" % (g, a))[:]
 
         def rows(ap):
@@ -117,8 +121,8 @@ def tile_list_hit_segment_energy_kernel(
             )
         load_tab(1)
         load_w1(0, 1)
-        load_tab(2)
         load_w1(0, 2)
+        load_tab(2)
         load_w1(1, 0)
         nc.sync.dma_start(pos1_t[:], pos1)
         load_w1(1, 1)
@@ -321,18 +325,16 @@ def tile_list_hit_segment_energy_kernel(
 
         gather_hits(0)
         nc.vector.tensor_copy(hit_sc[:], tab_sc[:].indirect(offs_t[:]))
-        for a in range(PASSES - 1):
-            if a > 0:
+        for a in range(PASSES):
+            if a == 1:
                 gather_hits(a)
             cast_scalar(0, a)
             quantize_w1(0, a)
-            for s in range(2):
-                h_pass(0, s, a)
+            if a < PASSES - 1:
+                for s in range(2):
+                    h_pass(0, s, a)
         for half in range(2):
             gather_hits(PASSES - 1, half * BANK, (half + 1) * BANK)
-            if half == 0:
-                cast_scalar(0, PASSES - 1)
-                quantize_w1(0, PASSES - 1)
             for s in range(2):
                 h_pass(0, s, PASSES - 1, (half,))
         cast_scalar(1, 0)

@@ -27,7 +27,22 @@ BANK = 512
 QUADRANTS = 4
 QUARTERS = P // PARTS
 GROUP = 16
-GROUPS = ((0, K_PASS // 2), (K_PASS // 2, K_PASS // 2), (K_PASS, K_PASS))
+NARROW = K_PASS // 2
+KB = 1024
+SHARE = 24
+
+PLACE = {
+    "codes10": 0, "rounded12": 0, "prod0": 0,
+    "rounded10": 42 * KB, "rounded11": 42 * KB,
+    "h00": 4 * KB, "high01": 4 * KB,
+    "low0": 8 * KB, "pair_codes": 9 * KB, "recip0": 10 * KB,
+    "low12": 14 * KB, "prod1": 14 * KB, "root00": 17 * KB, "high2": 18 * KB,
+    "root01": 20 * KB, "codes_d": 20 * KB,
+    "h10": 22 * KB, "pairs0": 22 * KB,
+    "codes_ab": 26 * KB, "recip1": 26 * KB,
+    "codes_e": 30 * KB, "root2": 30 * KB,
+    "h20": 38 * KB, "pairs10": 38 * KB, "pairs11": 39 * KB,
+}
 
 
 def tile_list_hit_segment_energy_kernel(
@@ -40,162 +55,129 @@ def tile_list_hit_segment_energy_kernel(
         psum = ctx.enter_context(tc.psum_pool(name="psum", bufs=1))
 
         def tile(shape, dtype, name):
+            if name in PLACE:
+                return placed.tile(shape, dtype, name=name, align_bytes=64, offset=PLACE[name])
             return keep.tile(shape, dtype, name=name, align_bytes=64)
 
-        def place(shape, dtype, name, row):
-            return placed.tile(shape, dtype, name=name, align_bytes=64, offset=int(row * 4 * P))
+        def rows(ap):
+            return ap.rearrange("p (r j) -> p r j", j=P)
 
         offs_t = keep.tile([PARTS, S // GROUP], U16, name="offs_t")
         pos1_t = keep.tile([PARTS, P // GROUP], U16, name="pos1_t")
         pos2_t = keep.tile([PARTS, P // GROUP], U16, name="pos2_t")
         knee_half = keep.tile([PARTS, 2, 2], F32, name="knee_half")
         knee_band = keep.tile([PARTS, PACK], F32, name="knee_band")
-        tab = [tile([PARTS, T], I32, "tab%d" % a) for a in range(PASSES - 1)]
-        tab.append(place([PARTS, T], I32, "tab2", 18))
+        tab = [tile([PARTS, T], I32, "tab%d" % a) for a in range(PASSES)]
         tab_sc = tile([PARTS, T], U8, "tab_sc")
         hit = [tile([PARTS, S], U32, "hit%d" % a) for a in range(PASSES)]
         hit_sc = tile([PARTS, S], U8, "hit_sc")
         w2_w = tile([PARTS, BANDS, 2 * N], U8, "w2_w")
         w2_sc = tile([PARTS, BANDS, N], U8, "w2_sc")
 
-        late = tile([PARTS, PACK * P], F32, "late")
-        late_rows = late[:].rearrange("p (r j) -> p r j", j=P)
-        last_codes = tile([PARTS, 2 * K_PASS], U32, "last_codes")
-        last_sc = tile([PARTS, 2 * K_PASS], U8, "last_sc")
-        pair_codes = tile([PARTS, K_PASS], U32, "pair_codes")
-        pair_sc = tile([PARTS, K_PASS], U8, "pair_sc")
-
-        flat = {}
-        grouped = {}
-        w1_codes = {}
-        w1_sc = {}
-        for g, (c0, width) in enumerate(GROUPS):
+        raw = {}
+        for g in range(2):
             for a in range(PASSES):
-                if (g, a) == (2, 2):
-                    flat[g, a] = late[:, 0 : PACK * P]
-                elif (g, a) == (1, 0):
-                    flat[g, a] = place([PARTS, PACK * width], F32, "raw10", 3)[:]
-                elif (g, a) == (2, 0):
-                    flat[g, a] = place([PARTS, PACK * width], F32, "raw20", 7)[:]
-                else:
-                    flat[g, a] = tile([PARTS, PACK * width], F32, "raw%d%d" % (g, a))[:]
-                if g == 1 and a > 0:
-                    w1_codes[g, a] = pair_codes[:, (a - 1) * width : a * width]
-                    w1_sc[g, a] = pair_sc[:, (a - 1) * width : a * width]
-                elif g == 2 and a > 0:
-                    continue
-                else:
-                    if g == 2:
-                        grouped[g, a] = place([PARTS, PACK * width], BF16, "grouped20", 12)[:]
-                    elif g == 1:
-                        grouped[g, a] = place([PARTS, PACK * width], BF16, "grouped10", 14)[:]
-                    else:
-                        grouped[g, a] = tile([PARTS, PACK * width], BF16, "grouped%d%d" % (g, a))[:]
-                    if g == 1:
-                        w1_codes[g, a] = place([PARTS, width], U32, "w1c10", 18)[:]
-                    else:
-                        w1_codes[g, a] = tile([PARTS, width], U32, "w1c%d%d" % (g, a))[:]
-                    w1_sc[g, a] = tile([PARTS, width], U8, "w1s%d%d" % (g, a))[:]
-
-        def rows(ap):
-            return ap.rearrange("p (r j) -> p r j", j=P)
+                raw[g, a] = tile([PARTS, PACK * NARROW], F32, "raw%d%d" % (g, a))[:]
+        raw[2, 0] = tile([PARTS, PACK * K_PASS], F32, "raw20")[:]
+        raw_last = tile([PARTS, 2 * PACK * K_PASS], F32, "raw_last")
+        for a in range(1, PASSES):
+            raw[2, a] = raw_last[:, (a - 1) * PACK * K_PASS : a * PACK * K_PASS]
 
         def load_tab(a):
             nc.sync.dma_start(out=tab[a][:], in_=tab_words[a].rearrange("p t i -> p (t i)").bitcast(I32))
 
         def load_w1(g, a):
-            c0, width = GROUPS[g]
-            src = w1[a * K_PASS : (a + 1) * K_PASS, c0 : c0 + width]
+            width = K_PASS if g == 2 else NARROW
+            src = w1[a * K_PASS : (a + 1) * K_PASS, g * NARROW : g * NARROW + width]
             nc.sync.dma_start(
-                out=flat[g, a].rearrange("p (j c) -> p j c", j=PACK), in_=src.rearrange("(p j) c -> p j c", j=PACK)
+                out=raw[g, a].rearrange("p (j c) -> p j c", j=PACK), in_=src.rearrange("(p j) c -> p j c", j=PACK)
             )
 
         nc.vector.memset(tab_sc[:].bitcast(I32), 0)
+        nc.vector.memset(w2_sc[:].rearrange("p b n -> p (b n)").bitcast(I32), 0)
         load_tab(0)
         nc.sync.dma_start(offs_t[:], offs)
-        load_w1(0, 0)
+        load_tab(1)
         for q in range(QUADRANTS):
             nc.sync.dma_start(
                 out=tab_sc[32 * q : 32 * q + 4 * PASSES, :].bitcast(I32),
                 in_=tab_scales[:, 4 * q : 4 * q + 4, :].bitcast(I32),
             )
-        load_tab(1)
+        load_w1(0, 0)
+        load_tab(2)
         load_w1(0, 1)
         load_w1(0, 2)
-        load_tab(2)
-        load_w1(1, 0)
         nc.sync.dma_start(pos1_t[:], pos1)
-        load_w1(1, 1)
-        load_w1(1, 2)
-        load_w1(2, 0)
-        nc.sync.dma_start(pos2_t[:], pos2)
-        for a in range(1, PASSES):
-            load_w1(2, a)
+        load_w1(1, 0)
         nc.sync.dma_start(out=knee_half[:], in_=knee[0:K_PASS].rearrange("(g q s) -> q g s", g=2, s=2))
+        for a in range(1, PASSES):
+            load_w1(1, a)
+        nc.sync.dma_start(pos2_t[:], pos2)
+        for a in range(PASSES):
+            load_w1(2, a)
         nc.sync.dma_start(out=knee_band[:], in_=knee[K_PASS:].rearrange("(p t) -> p t", t=PACK))
         nc.sync.dma_start(out=w2_w[:].bitcast(I32), in_=w2_words.rearrange("b p n -> p b n").bitcast(I32))
-        nc.vector.memset(w2_sc[:].rearrange("p b n -> p (b n)").bitcast(I32), 0)
         for q in range(QUADRANTS):
             nc.sync.dma_start(
                 out=w2_sc[32 * q : 32 * q + 4, :, :].bitcast(I32),
                 in_=w2_scales[:, 4 * q : 4 * q + 4, :].rearrange("b r n -> r b n").bitcast(I32),
             )
 
-        def gather_hits(a, i0=0, i1=S):
-            nc.vector.tensor_copy(
-                hit[a][:, i0:i1], tab[a][:].bitcast(U32).indirect(offs_t[:, i0 // GROUP : i1 // GROUP])
-            )
+        def gather_hits(a):
+            nc.vector.tensor_copy(hit[a][:], tab[a][:].bitcast(U32).indirect(offs_t[:]))
 
-        def cast_views(g, a, ts=slice(0, PACK)):
-            if g < 2:
-                dst = grouped[g, a].rearrange("p (s m u j) -> p m j u s", s=2, u=2, j=PACK)
-                src = flat[g, a].rearrange("p (j m u s) -> p m j u s", j=PACK, u=2, s=2)
-                return dst, src
-            dst = grouped[g, a, ts.start].rearrange("p t (m j) -> p m j t", j=PACK)
-            src = flat[g, a].rearrange("p (j m t) -> p m j t", j=PACK, t=PACK)
-            return dst, src[:, :, :, ts]
+        def narrow_views(rounded, piece, m0=0, m1=HALF):
+            dst = rounded.rearrange("p (s m u j) -> p m j u s", s=2, u=2, j=PACK)
+            src = piece.rearrange("p (j m u s) -> p m j u s", j=PACK, u=2, s=2)
+            return dst[:, m0:m1], src[:, m0:m1]
 
-        def cast_gpsimd_half(g, a):
-            dst = grouped[g, a].rearrange("p (s q j) -> p q s j", s=2, j=PACK)
-            src = flat[g, a].rearrange("p (j q s) -> p q s j", j=PACK, s=2)
-            nc.gpsimd.tensor_scalar(dst, src, 1.0, 0.0, MULT, ADD)
+        def narrow_gpsimd(rounded, piece, q0, q1):
+            dst = rounded.rearrange("p (s q j) -> p q s j", s=2, j=PACK)
+            src = piece.rearrange("p (j q s) -> p q s j", j=PACK, s=2)
+            nc.gpsimd.tensor_scalar(dst[:, q0:q1], src[:, q0:q1], 1.0, 0.0, MULT, ADD)
 
-        def cast_gpsimd_band(g, a, ts):
-            dst = grouped[g, a, ts.start].rearrange("p t (m j) -> p m t j", j=PACK)
-            src = flat[g, a].rearrange("p (j m t) -> p m t j", j=PACK, t=PACK)[:, :, ts, :]
-            nc.gpsimd.tensor_scalar(dst, src, 1.0, 0.0, MULT, ADD)
+        def band_scalar(rounded, piece, t0):
+            dst = rounded.rearrange("p (t m j) -> p m j t", t=2, j=PACK)
+            src = piece.rearrange("p (j m t) -> p m j t", j=PACK, t=PACK)
+            nc.scalar.copy(dst, src[:, :, :, t0 : t0 + 2])
 
-        def cast_scalar(g, a, ts=slice(0, PACK)):
-            nc.scalar.copy(*cast_views(g, a, ts))
+        def band_gpsimd(rounded, piece, t0):
+            dst = rounded.rearrange("p (t m j) -> p m t j", t=2, j=PACK)
+            src = piece.rearrange("p (j m t) -> p m t j", j=PACK, t=PACK)
+            nc.gpsimd.tensor_scalar(dst, src[:, :, t0 : t0 + 2, :], 1.0, 0.0, MULT, ADD)
 
         def quantize(codes, scales, rounded):
             nc.vector.quantize_mx(out=codes.bitcast(FP8X4), scales=scales, in_=rounded)
 
-        def quantize_w1(g, a):
-            quantize(w1_codes[g, a], w1_sc[g, a], grouped[g, a])
+        def halves(ap):
+            width = ap.shape[1] // 2
+            return [ap[:, 0:width], ap[:, width:]]
 
-        def quantize_last(u0, u1):
-            cols = slice(u0 * PARTS, u1 * PARTS)
-            rounded = last_bf[u0 // PACK][:, u0 % PACK * K_PASS : ((u1 - 1) % PACK + 1) * K_PASS]
-            quantize(last_codes[:, cols], last_sc[:, cols], rounded)
+        weights = {}
+
+        def quantize_w1(name, parts, units):
+            width = len(units) * PARTS
+            codes = tile([PARTS, width], U32, name)
+            scales = tile([PARTS, width], U8, name + "_sc")
+            step = width // len(parts)
+            for i, part in enumerate(parts):
+                quantize(codes[:, i * step : (i + 1) * step], scales[:, i * step : (i + 1) * step], part)
+            for u, unit in enumerate(units):
+                weights[unit] = (codes[:, u * PARTS : (u + 1) * PARTS], scales[:, u * PARTS : (u + 1) * PARTS])
 
         h_bank = {}
 
-        def h_pass(g, s, a, halves=(0, 1)):
-            pair = (s + 2) % PACK if g == 2 else s
-            for half in halves:
+        def h_pass(g, s, a):
+            first_bank = 2 * (s % 2) + (4 if g == 2 else 0)
+            codes, scales = weights[g, s, a]
+            for half in range(2):
                 if a == 0:
-                    h_bank[g, s, half] = psum.tile([PARTS, BANK], F32, name="bank%d" % (2 * pair + half))
+                    h_bank[g, s, half] = psum.tile([PARTS, BANK], F32, name="bank%d" % (first_bank + half))
                 cols = slice(half * BANK, (half + 1) * BANK)
-                if g == 2 and a > 0:
-                    codes, scales, unit = last_codes, last_sc, 2 * s + a - 1
-                else:
-                    codes, scales, unit = w1_codes[g, a], w1_sc[g, a], s
-                wcols = slice(unit * PARTS, (unit + 1) * PARTS)
                 nc.tensor.matmul_mx(
                     out=h_bank[g, s, half][:],
-                    lhsT=codes[:, wcols].bitcast(FP8X4),
-                    lhsT_scale=scales[:, wcols],
+                    lhsT=codes.bitcast(FP8X4),
+                    lhsT_scale=scales,
                     rhs=hit[a][:, cols].bitcast(FP8X4),
                     rhs_scale=hit_sc[4 * a :, cols],
                     start=(a == 0),
@@ -203,105 +185,87 @@ def tile_list_hit_segment_energy_kernel(
                 )
 
         h_t = {}
-        first = [place([PARTS, 2, P], F32, "first0", 16)[:], tile([PARTS, 2, P], F32, "first1")[:], tile([PARTS, PACK, P], F32, "first2")[:]]
-        prod = [None, late_rows[:, 2:4, :], late_rows]
-        mag2 = tile([PARTS, PACK, P], F32, "mag2")
-        mag = [
-            [rows(flat[0, 2])[:, 0, :], None],
-            [late_rows[:, s, :] for s in range(2)],
-            [mag2[:, t, :] for t in range(PACK)],
-        ]
-        root2 = tile([PARTS, PACK, P], F32, "root2")
-        root_half = [rows(flat[1, 1])[:, s, :] for s in range(2)]
-        root = [[None, root_half[1]], root_half, [root2[:, t, :] for t in range(PACK)]]
-        recip = [rows(flat[0, 0]), rows(flat[0, 1]), tile([PARTS, PACK, P], F32, "recip2")[:]]
+        first = [tile([PARTS, 2 if g < 2 else PACK, P], F32, "first%d" % g)[:] for g in range(3)]
+        prod = {2: tile([PARTS, PACK, P], F32, "prod2")[:]}
+        mag = {}
+        for s in range(2):
+            mag[0, s] = rows(raw[1, 2])[:, s, :]
+            mag[1, s] = rows(raw[0, 1])[:, s, :]
+            mag[2, s] = prod[2][:, 2 + s, :]
+            mag[2, 2 + s] = rows(raw[0, 2])[:, s, :]
+        root = {(1, s): prod[2][:, s, :] for s in range(2)}
+        recip = {2: rows(raw[2, 0])}
         z_words = [tile([PARTS, 2, P], BF16, "z_words%d" % half) for half in range(2)]
         z_bf = [tile([PARTS, P, PACK], BF16, "z_bf%d" % b) for b in range(BANDS)]
         z_codes = [tile([PARTS, P], U32, "z_codes%d" % b) for b in range(BANDS)]
         z_sc = [tile([PARTS, P], U8, "z_sc%d" % b) for b in range(BANDS)]
 
         def evacuate(g, s):
-            if (g, s) == (2, 0):
-                h_t[g, s] = place([PARTS, S], F32, "h20", 0)
-            elif g < 2:
-                h_t[g, s] = place([PARTS, S], F32, "h%d%d" % (g, s), 2 + 2 * s if g == 0 else 10 - 2 * s)
-            else:
-                h_t[g, s] = tile([PARTS, S], F32, "h%d%d" % (g, s))
+            h_t[g, s] = tile([PARTS, S], F32, "h%d%d" % (g, s))
             for half in range(2):
                 nc.scalar.copy(h_t[g, s][:, half * BANK : (half + 1) * BANK], h_bank[g, s, half][:])
 
-        def gather_first(g, s):
+        def pick_first(g, s):
             nc.vector.tensor_copy(first[g][:, s, :], h_t[g, s][:].indirect(pos1_t[:]))
 
-        def gather_second(g, s):
+        def pick_second(g, s):
             nc.vector.tensor_tensor(prod[g][:, s, :], h_t[g, s][:].indirect(pos2_t[:]), first[g][:, s, :], MULT)
 
         def magnitude(g, s):
-            nc.scalar.activation(mag[g][s], first[g][:, s, :], ACT.Abs)
+            nc.scalar.activation(mag[g, s], first[g][:, s, :], ACT.Abs)
 
-        def inverse_root(g, s, j0=0, j1=P):
+        def inverse_root(g, s):
             bias = knee_half[:, g, s : s + 1] if g < 2 else knee_band[:, s : s + 1]
-            nc.scalar.activation(root[g][s][:, j0:j1], mag[g][s][:, j0:j1], ACT.Abs_reciprocal_sqrt, bias=bias)
+            nc.scalar.activation(root[g, s], mag[g, s], ACT.Abs_reciprocal_sqrt, bias=bias)
 
-        def reciprocal(g, j0, j1):
-            nc.scalar.activation(recip[g][:, :, j0:j1], root2[:, :, j0:j1], ACT.Square)
-
-        def reciprocal_half(g):
+        def reciprocal_narrow(g):
+            recip[g] = tile([PARTS, 2, P], F32, "recip%d" % g)[:]
             for s in range(2):
-                nc.scalar.activation(recip[g][:, s, :], root[g][s], ACT.Square)
+                nc.scalar.activation(recip[g][:, s, :], root[g, s], ACT.Square)
 
-        def form_z_half(g):
-            width = P if g == 0 else P // 2
-            for half in range(2):
-                if half * (P // 2) % width == 0:
-                    part = slice(half * (P // 2), half * (P // 2) + width)
-                    pairs = place([PARTS, width, 2], BF16, "pairs%d%d" % (g, half), 11.5 if g == 0 else half)
-                    nc.gpsimd.tensor_tensor(
-                        pairs[:].rearrange("p (c i) s -> p c s i", i=4),
-                        prod[g][:, :, part].rearrange("p s (c i) -> p c s i", i=4),
-                        recip[g][:, :, part].rearrange("p s (c i) -> p c s i", i=4),
-                        MULT,
-                    )
-                cols = slice(half * (P // 2) % width, half * (P // 2) % width + P // 2)
+        def form_pairs(g, name, j0, j1):
+            pairs = tile([PARTS, j1 - j0, 2], BF16, name)
+            nc.gpsimd.tensor_tensor(
+                pairs[:].rearrange("p (c i) s -> p c s i", i=4),
+                prod[g][:, :, j0:j1].rearrange("p s (c i) -> p c s i", i=4),
+                recip[g][:, :, j0:j1].rearrange("p s (c i) -> p c s i", i=4),
+                MULT,
+            )
+            for c0 in range(j0, j1, P // 2):
                 for u in range(2):
                     nc.sync.dma_start(
-                        out=z_words[half][g * HALF : (g + 1) * HALF, u, :],
-                        in_=pairs[u:PARTS:2, cols, :].rearrange("p j s -> p (j s)"),
+                        out=z_words[c0 // (P // 2)][g * HALF : (g + 1) * HALF, u, :],
+                        in_=pairs[u:PARTS:2, c0 - j0 : c0 - j0 + P // 2, :].rearrange("p j s -> p (j s)"),
                     )
 
         def weave_z(half):
             woven = z_bf[0][:, half * (P // 2) : (half + 1) * (P // 2), :].rearrange("p j t -> p (j t)")
-            nc.vector.tensor_copy(
-                woven.bitcast(I32).rearrange("p (c i u) -> p c u i", i=2, u=2),
-                z_words[half][:].bitcast(I32).rearrange("p u (c i) -> p c u i", i=2),
+            nc.scalar.copy(
+                woven.bitcast(U32).rearrange("p (c i u) -> p c u i", i=2, u=2),
+                z_words[half][:].bitcast(U32).rearrange("p u (c i) -> p c u i", i=2),
             )
 
-        def form_z(j0, j1):
+        def form_z(c):
+            cols = slice(c * PARTS, (c + 1) * PARTS)
             nc.vector.tensor_tensor(
-                z_bf[1][:, j0:j1, :].rearrange("p (c i) t -> p c t i", i=4),
-                prod[2][:, :, j0:j1].rearrange("p t (c i) -> p c t i", i=4),
-                recip[2][:, :, j0:j1].rearrange("p t (c i) -> p c t i", i=4),
+                z_bf[1][:, cols, :].rearrange("p (c i) t -> p c t i", i=4),
+                prod[2][:, :, cols].rearrange("p t (c i) -> p c t i", i=4),
+                recip[2][:, :, cols].rearrange("p t (c i) -> p c t i", i=4),
                 MULT,
             )
 
         def quantize_z(b, j0, j1):
-            nc.vector.quantize_mx(
-                out=z_codes[b][:, j0:j1].bitcast(FP8X4),
-                scales=z_sc[b][:, j0:j1],
-                in_=z_bf[b][:, j0:j1, :].rearrange("p j t -> p (j t)"),
-            )
+            quantize(z_codes[b][:, j0:j1], z_sc[b][:, j0:j1], z_bf[b][:, j0:j1, :].rearrange("p j t -> p (j t)"))
 
         y_bank = {}
-        y_banks = ((4, 5), (6, 7), (0, 1), (2, 3))
 
         def y_pass(b, c):
             cols = slice(c * PARTS, (c + 1) * PARTS)
-            per = QUARTERS // len(y_banks[c])
-            for u, bank in enumerate(y_banks[c]):
+            for u in range(2):
                 if b == 0:
-                    y_bank[c, u] = psum.tile([PARTS, per, PARTS], F32, name="bank%d" % bank)
-                for v in range(per):
-                    n = per * u + v
+                    y_bank[c, u] = psum.tile([PARTS, 2, PARTS], F32, name="bank%d" % (2 * c + u))
+                for v in range(2):
+                    n = 2 * u + v
                     nc.tensor.matmul_mx(
                         out=y_bank[c, u][:, v, :],
                         lhsT=w2_w[:, b, 2 * n * PARTS : 2 * (n + 1) * PARTS].bitcast(FP4X4),
@@ -309,133 +273,156 @@ def tile_list_hit_segment_energy_kernel(
                         rhs=z_codes[b][:, cols].bitcast(FP8X4),
                         rhs_scale=z_sc[b][:, cols],
                         start=(b == 0 and v == 0),
-                        stop=(b == BANDS - 1 and v == per - 1),
+                        stop=(b == BANDS - 1 and v == 1),
                     )
 
         def store(c):
-            per = QUARTERS // len(y_banks[c])
-            for u in range(len(y_banks[c])):
-                energy = tile([PARTS, per, PARTS], F32, "energy%d%d" % (c, u))
-                nc.scalar.activation(energy[:], y_bank[c, u][:], ACT.Square)
-                dst = out[per * u * PARTS : per * (u + 1) * PARTS, c * PARTS : (c + 1) * PARTS]
-                nc.sync.dma_start(out=dst.rearrange("(n p) j -> p n j", p=PARTS), in_=energy[:])
+            for u in range(2):
+                e0 = (2 * c + u) * 2 * PARTS
+                energy = raw_last[:, e0 : e0 + 2 * PARTS].rearrange("p (v j) -> p v j", v=2)
+                nc.scalar.activation(energy, y_bank[c, u][:], ACT.Square)
+                dst = out[2 * u * PARTS : 2 * (u + 1) * PARTS, c * PARTS : (c + 1) * PARTS]
+                nc.sync.dma_start(out=dst.rearrange("(n p) j -> p n j", p=PARTS), in_=energy)
 
-        unused = keep.tile([PARTS, 1], F32, name="unused")
-        nc.scalar.activation(unused[:], flat[0, 0][:, 0:1], ACT.Abs_reciprocal_sqrt, scale=0.0, bias=1.0)
+        unused = keep.tile([PARTS, 2], F32, name="unused")
+        nc.gpsimd.memset(unused[:, 0:1], 1.0)
+        nc.scalar.activation(unused[:, 1:2], unused[:, 0:1], ACT.Abs_reciprocal_sqrt)
 
         gather_hits(0)
+        gather_hits(1)
         nc.vector.tensor_copy(hit_sc[:], tab_sc[:].indirect(offs_t[:]))
+        rounded = {}
         for a in range(PASSES):
-            if a == 1:
-                gather_hits(a)
-            cast_scalar(0, a)
-            quantize_w1(0, a)
+            rounded[0, a] = tile([PARTS, PACK * NARROW], BF16, "rounded0%d" % a)[:]
             if a < PASSES - 1:
+                nc.scalar.copy(*narrow_views(rounded[0, a], raw[0, a]))
+            else:
+                nc.scalar.copy(*narrow_views(rounded[0, a], raw[0, a], 0, HALF // 2))
+                nc.vector.tensor_copy(*narrow_views(rounded[0, a], raw[0, a], HALF // 2, HALF))
+            parts = halves(rounded[0, a]) if a == PASSES - 1 else [rounded[0, a]]
+            quantize_w1("codes0%d" % a, parts, [(0, 0, a), (0, 1, a)])
+            if a == 0:
+                gather_hits(2)
                 for s in range(2):
-                    h_pass(0, s, a)
-        for half in range(2):
-            gather_hits(PASSES - 1, half * BANK, (half + 1) * BANK)
-            for s in range(2):
-                h_pass(0, s, PASSES - 1, (half,))
-        cast_scalar(1, 0)
-        quantize_w1(1, 0)
+                    h_pass(0, s, 0)
+        for s in range(2):
+            for a in range(1, PASSES):
+                h_pass(0, s, a)
+        rounded[1, 0] = tile([PARTS, PACK * NARROW], BF16, "rounded10")[:]
+        nc.vector.tensor_copy(*narrow_views(rounded[1, 0], raw[1, 0]))
+        quantize_w1("codes10", [rounded[1, 0]], [(1, 0, 0), (1, 1, 0)])
         for s in range(2):
             evacuate(0, s)
             h_pass(1, s, 0)
-            gather_first(0, s)
-        pair_bf = place([PARTS, PACK * K_PASS], BF16, "pair_bf", 14)
+            pick_first(0, s)
+
         for a in range(1, PASSES):
-            grouped[1, a] = pair_bf[:, (a - 1) * 2 * P : a * 2 * P]
-            cast_gpsimd_half(1, a)
-        quantize(pair_codes[:], pair_sc[:], pair_bf[:])
-        prod[0] = place([PARTS, 2, P], F32, "prod0", 14)[:]
-        for s in range(2):
-            for a in range(1, PASSES):
+            rounded[1, a] = tile([PARTS, PACK * NARROW], BF16, "rounded1%d" % a)[:]
+        narrow_gpsimd(rounded[1, 1], raw[1, 1], 0, PARTS)
+        narrow_gpsimd(rounded[1, 2], raw[1, 2], 0, 2 * SHARE)
+        nc.scalar.copy(*narrow_views(rounded[1, 2], raw[1, 2], SHARE, HALF))
+        quantize_w1("pair_codes", [rounded[1, 1], rounded[1, 2]], [(1, s, a) for a in range(1, PASSES) for s in range(2)])
+        for a in range(1, PASSES):
+            for s in range(2):
                 h_pass(1, s, a)
+        prod[0] = tile([PARTS, 2, P], F32, "prod0")[:]
         for s in range(2):
-            gather_second(0, s)
-        magnitude(0, 0)
-        whole = grouped[2, 0]
-        grouped[2, 0, 0] = whole.rearrange("p (t c) -> p t c", t=PACK)
-        cast_scalar(2, 0)
-        quantize(w1_codes[2, 0], w1_sc[2, 0], whole)
+            pick_second(0, s)
         for s in range(2):
-            h_pass(2, s, 0)
+            magnitude(0, s)
+        for s in range(2):
+            root[0, s] = tile([PARTS, P], F32, "root0%d" % s)[:]
+            inverse_root(0, s)
         for s in range(2):
             evacuate(1, s)
-            h_pass(2, s + 2, 0)
-            gather_first(1, s)
-        stage = place([PARTS, 2, P], F32, "stage", 6)
-        mag[0][1] = stage[:, 0, :]
-        root[0][0] = stage[:, 1, :]
-        magnitude(0, 1)
-        last_bf = [place([PARTS, PACK * K_PASS], BF16, "low_bf", 16), place([PARTS, PACK * K_PASS], BF16, "high_bf", 12)]
-        for a in range(1, PASSES):
-            for pair in range(2):
-                grouped[2, a, 2 * pair] = last_bf[pair][:].rearrange("p (t a c) -> p a t c", t=2, a=2)[:, a - 1]
-        cast_gpsimd_band(2, 1, slice(2, PACK))
-        for a in range(1, PASSES):
-            nc.vector.tensor_copy(*cast_views(2, a, slice(0, 2)))
-        quantize_last(0, 1)
-        h_pass(2, 0, 1)
-        cast_scalar(2, 2, slice(2, PACK))
+            pick_first(1, s)
+
+        high01 = tile([PARTS, 2 * K_PASS * 2], BF16, "high01")
+        for a in range(2):
+            band_gpsimd(high01[:, a * 2 * K_PASS : (a + 1) * 2 * K_PASS], raw[2, a], 2)
+        low0 = tile([PARTS, 2 * K_PASS], BF16, "low0")
+        band_scalar(low0[:], raw[2, 0], 0)
+        reciprocal_narrow(0)
+        high2 = tile([PARTS, 2 * K_PASS], BF16, "high2")
+        band_scalar(high2[:], raw[2, 2], 2)
+        quantize_w1("codes20", [low0[:]], [(2, 0, 0), (2, 1, 0)])
         for s in range(2):
-            inverse_root(0, s)
-        reciprocal_half(0)
-        quantize_last(1, 2)
-        h_pass(2, 0, 2)
-        quantize_last(2, 4)
+            h_pass(2, s, 0)
+        low12 = tile([PARTS, 2 * K_PASS * 2], BF16, "low12")
+        nc.vector.tensor_copy(
+            low12[:].rearrange("p (a t m j) -> p a m j t", a=2, t=2, j=PACK),
+            raw_last[:].rearrange("p (a j m t) -> p a m j t", a=2, j=PACK, t=PACK)[:, :, :, :, 0:2],
+        )
+        quantize_w1("codes_d", [high01[:]], [(2, s, a) for a in range(2) for s in range(2, PACK)])
+        quantize_w1("codes_ab", halves(low12[:]), [(2, s, a) for a in range(1, PASSES) for s in range(2)])
         for a in range(1, PASSES):
-            h_pass(2, 1, a)
-        gather_second(1, 0)
-        quantize_last(4, 8)
-        for s in range(2, PACK):
-            for a in range(1, PASSES):
+            for s in range(2):
                 h_pass(2, s, a)
-        gather_second(1, 1)
-        form_z_half(0)
-        magnitude(1, 0)
+        quantize_w1("codes_e", [high2[:]], [(2, s, 2) for s in range(2, PACK)])
+        prod[1] = tile([PARTS, 2, P], F32, "prod1")[:]
         for s in range(2):
-            evacuate(2, s)
-            gather_first(2, s)
-        magnitude(1, 1)
+            pick_second(1, s)
+        for s in range(2):
+            magnitude(1, s)
         for s in range(2):
             inverse_root(1, s)
-            gather_second(2, s)
-        evacuate(2, 2)
-        reciprocal_half(1)
-        form_z_half(1)
-        gather_first(2, 2)
-        evacuate(2, 3)
-        gather_first(2, 3)
+        form_pairs(0, "pairs0", 0, P)
+
+        for s in range(2):
+            evacuate(2, s)
+            for a in range(PASSES - 1):
+                h_pass(2, s + 2, a)
+            pick_first(2, s)
         for s in range(2, PACK):
-            gather_second(2, s)
+            h_pass(2, s, PASSES - 1)
+        reciprocal_narrow(1)
+        for s in range(2):
+            pick_second(2, s)
+        for half in range(2):
+            form_pairs(1, "pairs1%d" % half, half * (P // 2), (half + 1) * (P // 2))
+        for s in range(2):
+            magnitude(2, s)
+        for s in range(2, PACK):
+            evacuate(2, s)
+            pick_first(2, s)
+        root2 = tile([PARTS, PACK, P], F32, "root2")
+        for s in range(PACK):
+            root[2, s] = root2[:, s, :]
+        for s in range(2):
+            inverse_root(2, s)
+        for s in range(2, PACK):
+            pick_second(2, s)
+        for s in range(2, PACK):
+            magnitude(2, s)
+        for s in range(2, PACK):
+            inverse_root(2, s)
+
+        def reciprocal(c):
+            cols = slice(c * PARTS, (c + 1) * PARTS)
+            nc.scalar.activation(recip[2][:, :, cols], root2[:, :, cols], ACT.Square)
+
+        def finish(c):
+            quantize_z(1, c * PARTS, (c + 1) * PARTS)
+            y_pass(1, c)
+            store(c)
+
         weave_z(0)
+        reciprocal(0)
+        reciprocal(1)
         quantize_z(0, 0, P // 2)
         for c in range(2):
             y_pass(0, c)
-        for t in range(2):
-            magnitude(2, t)
-        for t in range(2):
-            inverse_root(2, t)
-        for t in range(2, PACK):
-            magnitude(2, t)
-        for t in range(2, PACK):
-            inverse_root(2, t, 0, P // 2)
-        for c in range(QUARTERS):
-            if c < 2:
-                inverse_root(2, 2 + c, P // 2, P)
-            reciprocal(2, c * PARTS, (c + 1) * PARTS)
-        for c in range(QUARTERS + 1):
-            if c < QUARTERS:
-                form_z(c * PARTS, (c + 1) * PARTS)
-            if c > 0:
-                quantize_z(1, (c - 1) * PARTS, c * PARTS)
-                y_pass(1, c - 1)
-                store(c - 1)
-            if c == 0:
-                weave_z(1)
-            if c == 1:
-                quantize_z(0, P // 2, P)
-                for d in range(2, QUARTERS):
-                    y_pass(0, d)
+        form_z(0)
+        weave_z(1)
+        reciprocal(2)
+        reciprocal(3)
+        form_z(1)
+        finish(0)
+        quantize_z(0, P // 2, P)
+        for c in range(2, QUARTERS):
+            y_pass(0, c)
+        form_z(2)
+        finish(1)
+        finish(2)
+        form_z(3)
+        finish(3)

@@ -33,15 +33,16 @@ SHARE = 24
 
 PLACE = {
     "codes10": 0, "rounded12": 0, "prod0": 0,
-    "rounded10": 42 * KB, "rounded11": 42 * KB,
-    "h00": 4 * KB, "high01": 4 * KB,
-    "low0": 8 * KB, "pair_codes": 9 * KB, "recip0": 10 * KB,
-    "low12": 14 * KB, "prod1": 14 * KB, "root00": 17 * KB, "high2": 18 * KB,
-    "root01": 20 * KB, "codes_d": 20 * KB,
-    "h10": 22 * KB, "pairs0": 22 * KB,
-    "codes_ab": 26 * KB, "recip1": 26 * KB,
-    "codes_e": 30 * KB, "root2": 30 * KB,
-    "h20": 38 * KB, "pairs10": 38 * KB, "pairs11": 39 * KB,
+    "h00": 4 * KB, "whole0": 4 * KB,
+    "high1": 45 * KB, "pair_codes": 46 * KB, "recip0": 47 * KB,
+    "low1": 13 * KB + 512, "root00": 15 * KB, "codes_c": 15 * KB + 512, "codes20": 16 * KB + 512,
+    "root01": 18 * KB, "high2": 18 * KB,
+    "low2": 20 * KB, "mag10": 21 * KB, "codes_d": 22 * KB,
+    "h11": 23 * KB, "pairs0": 23 * KB,
+    "codes_b": 27 * KB, "recip1": 27 * KB,
+    "codes_e": 31 * KB, "root2": 31 * KB,
+    "h20": 39 * KB, "pairs10": 39 * KB, "pairs11": 40 * KB,
+    "rounded02": 43 * KB, "rounded10": 43 * KB, "rounded11": 43 * KB,
 }
 
 
@@ -141,10 +142,10 @@ def tile_list_hit_segment_energy_kernel(
             src = piece.rearrange("p (j m t) -> p m j t", j=PACK, t=PACK)
             nc.scalar.copy(dst, src[:, :, :, t0 : t0 + 2])
 
-        def band_gpsimd(rounded, piece, t0):
-            dst = rounded.rearrange("p (t m j) -> p m t j", t=2, j=PACK)
-            src = piece.rearrange("p (j m t) -> p m t j", j=PACK, t=PACK)
-            nc.gpsimd.tensor_scalar(dst, src[:, :, t0 : t0 + 2, :], 1.0, 0.0, MULT, ADD)
+        def band_vector(rounded, piece):
+            dst = rounded.rearrange("p (t m j) -> p m j t", t=2, j=PACK)
+            src = piece.rearrange("p (j m t) -> p m j t", j=PACK, t=PACK)
+            nc.vector.tensor_copy(dst, src[:, :, :, 0:2])
 
         def quantize(codes, scales, rounded):
             nc.vector.quantize_mx(out=codes.bitcast(FP8X4), scales=scales, in_=rounded)
@@ -337,35 +338,39 @@ def tile_list_hit_segment_energy_kernel(
             evacuate(1, s)
             pick_first(1, s)
 
-        high01 = tile([PARTS, 2 * K_PASS * 2], BF16, "high01")
-        for a in range(2):
-            band_gpsimd(high01[:, a * 2 * K_PASS : (a + 1) * 2 * K_PASS], raw[2, a], 2)
-        low0 = tile([PARTS, 2 * K_PASS], BF16, "low0")
-        band_scalar(low0[:], raw[2, 0], 0)
-        reciprocal_narrow(0)
-        high2 = tile([PARTS, 2 * K_PASS], BF16, "high2")
-        band_scalar(high2[:], raw[2, 2], 2)
-        quantize_w1("codes20", [low0[:]], [(2, 0, 0), (2, 1, 0)])
-        for s in range(2):
-            h_pass(2, s, 0)
-        low12 = tile([PARTS, 2 * K_PASS * 2], BF16, "low12")
-        nc.vector.tensor_copy(
-            low12[:].rearrange("p (a t m j) -> p a m j t", a=2, t=2, j=PACK),
-            raw_last[:].rearrange("p (a j m t) -> p a m j t", a=2, j=PACK, t=PACK)[:, :, :, :, 0:2],
+        whole0 = tile([PARTS, PACK * K_PASS], BF16, "whole0")
+        nc.gpsimd.tensor_scalar(
+            whole0[:].rearrange("p (t m j) -> p m t j", t=PACK, j=PACK),
+            raw[2, 0].rearrange("p (j m t) -> p m t j", j=PACK, t=PACK),
+            1.0, 0.0, MULT, ADD,
         )
-        quantize_w1("codes_d", [high01[:]], [(2, s, a) for a in range(2) for s in range(2, PACK)])
-        quantize_w1("codes_ab", halves(low12[:]), [(2, s, a) for a in range(1, PASSES) for s in range(2)])
-        for a in range(1, PASSES):
-            for s in range(2):
-                h_pass(2, s, a)
-        quantize_w1("codes_e", [high2[:]], [(2, s, 2) for s in range(2, PACK)])
-        prod[1] = tile([PARTS, 2, P], F32, "prod1")[:]
-        for s in range(2):
-            pick_second(1, s)
+        reciprocal_narrow(0)
+        high = {a: tile([PARTS, 2 * K_PASS], BF16, "high%d" % a) for a in range(1, PASSES)}
+        low = {a: tile([PARTS, 2 * K_PASS], BF16, "low%d" % a) for a in range(1, PASSES)}
+        band_scalar(high[1][:], raw[2, 1], 2)
+        mag[1, 0] = tile([PARTS, P], F32, "mag10")[:]
         for s in range(2):
             magnitude(1, s)
+        inverse_root(1, 0)
+        band_scalar(high[2][:], raw[2, 2], 2)
+        inverse_root(1, 1)
+        quantize_w1("codes20", halves(whole0[:])[:1], [(2, s, 0) for s in range(2)])
         for s in range(2):
-            inverse_root(1, s)
+            h_pass(2, s, 0)
+        band_vector(low[1][:], raw[2, 1])
+        quantize_w1("codes_c", halves(whole0[:])[1:], [(2, s, 0) for s in range(2, PACK)])
+        quantize_w1("codes_a", [low[1][:]], [(2, s, 1) for s in range(2)])
+        for s in range(2):
+            h_pass(2, s, 1)
+        prod[1] = rows(raw_last[:, PACK * K_PASS - P : PACK * K_PASS + P])
+        pick_second(1, 0)
+        band_vector(low[2][:], raw[2, 2])
+        quantize_w1("codes_d", [high[1][:]], [(2, s, 1) for s in range(2, PACK)])
+        quantize_w1("codes_b", [low[2][:]], [(2, s, 2) for s in range(2)])
+        for s in range(2):
+            h_pass(2, s, 2)
+        pick_second(1, 1)
+        quantize_w1("codes_e", [high[2][:]], [(2, s, 2) for s in range(2, PACK)])
         form_pairs(0, "pairs0", 0, P)
 
         for s in range(2):

@@ -32,8 +32,8 @@ KB = 1024
 SHARE = 24
 
 PLACE = {
-    "codes10": 0, "rounded12": 0, "prod0": 0,
-    "h00": 4 * KB, "whole0": 4 * KB,
+    "prod0": 0, "rounded12": 2 * KB, "codes10": 3 * KB + 512, "mag00": 4 * KB, "h10": 4 * KB,
+    "h00": 8 * KB, "whole0": 8 * KB,
     "high1": 45 * KB, "pair_codes": 46 * KB, "recip0": 47 * KB,
     "low1": 13 * KB + 512, "root00": 15 * KB, "codes_c": 15 * KB + 512, "codes20": 16 * KB + 512,
     "root01": 18 * KB, "high2": 18 * KB,
@@ -42,7 +42,7 @@ PLACE = {
     "codes_b": 27 * KB, "recip1": 27 * KB,
     "codes_e": 31 * KB, "root2": 31 * KB,
     "h20": 39 * KB, "pairs10": 39 * KB, "pairs11": 40 * KB,
-    "rounded02": 43 * KB, "rounded10": 43 * KB, "rounded11": 43 * KB,
+    "rounded02": 51 * KB, "rounded10": 51 * KB, "rounded11": 51 * KB,
 }
 
 
@@ -98,21 +98,19 @@ def tile_list_hit_segment_energy_kernel(
         nc.vector.memset(w2_sc[:].rearrange("p b n -> p (b n)").bitcast(I32), 0)
         load_tab(0)
         nc.sync.dma_start(offs_t[:], offs)
-        load_tab(1)
+        load_w1(0, 0)
         for q in range(QUADRANTS):
             nc.sync.dma_start(
                 out=tab_sc[32 * q : 32 * q + 4 * PASSES, :].bitcast(I32),
                 in_=tab_scales[:, 4 * q : 4 * q + 4, :].bitcast(I32),
             )
-        load_w1(0, 0)
-        load_tab(2)
-        load_w1(0, 1)
-        load_w1(0, 2)
-        nc.sync.dma_start(pos1_t[:], pos1)
-        load_w1(1, 0)
-        nc.sync.dma_start(out=knee_half[:], in_=knee[0:K_PASS].rearrange("(g q s) -> q g s", g=2, s=2))
         for a in range(1, PASSES):
+            load_tab(a)
+            load_w1(0, a)
+        nc.sync.dma_start(pos1_t[:], pos1)
+        for a in range(PASSES):
             load_w1(1, a)
+        nc.sync.dma_start(out=knee_half[:], in_=knee[0:K_PASS].rearrange("(g q s) -> q g s", g=2, s=2))
         nc.sync.dma_start(pos2_t[:], pos2)
         for a in range(PASSES):
             load_w1(2, a)
@@ -190,7 +188,7 @@ def tile_list_hit_segment_energy_kernel(
         prod = {2: tile([PARTS, PACK, P], F32, "prod2")[:]}
         mag = {}
         for s in range(2):
-            mag[0, s] = rows(raw[1, 2])[:, s, :]
+            mag[0, s] = rows(raw[0, 0])[:, s, :]
             mag[1, s] = rows(raw[0, 1])[:, s, :]
             mag[2, s] = prod[2][:, 2 + s, :]
             mag[2, 2 + s] = rows(raw[0, 2])[:, s, :]
@@ -290,24 +288,20 @@ def tile_list_hit_segment_energy_kernel(
         nc.scalar.activation(unused[:, 1:2], unused[:, 0:1], ACT.Abs_reciprocal_sqrt)
 
         gather_hits(0)
-        gather_hits(1)
         nc.vector.tensor_copy(hit_sc[:], tab_sc[:].indirect(offs_t[:]))
         rounded = {}
         for a in range(PASSES):
+            if a > 0:
+                gather_hits(a)
             rounded[0, a] = tile([PARTS, PACK * NARROW], BF16, "rounded0%d" % a)[:]
             if a < PASSES - 1:
                 nc.scalar.copy(*narrow_views(rounded[0, a], raw[0, a]))
             else:
-                nc.scalar.copy(*narrow_views(rounded[0, a], raw[0, a], 0, HALF // 2))
-                nc.vector.tensor_copy(*narrow_views(rounded[0, a], raw[0, a], HALF // 2, HALF))
+                narrow_gpsimd(rounded[0, a], raw[0, a], 0, 2 * SHARE)
+                nc.scalar.copy(*narrow_views(rounded[0, a], raw[0, a], SHARE, HALF))
             parts = halves(rounded[0, a]) if a == PASSES - 1 else [rounded[0, a]]
             quantize_w1("codes0%d" % a, parts, [(0, 0, a), (0, 1, a)])
-            if a == 0:
-                gather_hits(2)
-                for s in range(2):
-                    h_pass(0, s, 0)
-        for s in range(2):
-            for a in range(1, PASSES):
+            for s in range(2):
                 h_pass(0, s, a)
         rounded[1, 0] = tile([PARTS, PACK * NARROW], BF16, "rounded10")[:]
         nc.vector.tensor_copy(*narrow_views(rounded[1, 0], raw[1, 0]))
@@ -329,6 +323,7 @@ def tile_list_hit_segment_energy_kernel(
         prod[0] = tile([PARTS, 2, P], F32, "prod0")[:]
         for s in range(2):
             pick_second(0, s)
+        mag[0, 0] = tile([PARTS, P], F32, "mag00")[:]
         for s in range(2):
             magnitude(0, s)
         for s in range(2):

@@ -262,7 +262,7 @@ def tile_list_hit_segment_energy_kernel(
             cols = slice(c * PARTS, (c + 1) * PARTS)
             for u in range(2):
                 if b == 0:
-                    y_bank[c, u] = psum.tile([PARTS, 2, PARTS], F32, name="bank%d" % (2 * c + u))
+                    y_bank[c, u] = psum.tile([PARTS, 2, PARTS], F32, name="bank%d" % (2 * (c % (QUARTERS - 1)) + u))
                 for v in range(2):
                     n = 2 * u + v
                     nc.tensor.matmul_mx(
@@ -281,7 +281,8 @@ def tile_list_hit_segment_energy_kernel(
                 energy = raw_last[:, e0 : e0 + 2 * PARTS].rearrange("p (v j) -> p v j", v=2)
                 nc.scalar.activation(energy, y_bank[c, u][:], ACT.Square)
                 dst = out[2 * u * PARTS : 2 * (u + 1) * PARTS, c * PARTS : (c + 1) * PARTS]
-                nc.sync.dma_start(out=dst.rearrange("(n p) j -> p n j", p=PARTS), in_=energy)
+                queue = nc.scalar if (c, u) == (QUARTERS - 1, 1) else nc.sync
+                queue.dma_start(out=dst.rearrange("(n p) j -> p n j", p=PARTS), in_=energy)
 
         unused = keep.tile([PARTS, 2], F32, name="unused")
         nc.gpsimd.memset(unused[:, 0:1], 1.0)

@@ -30,9 +30,10 @@ GROUP = 16
 NARROW = K_PASS // 2
 KB = 1024
 SHARE = 24
+WIDE_SHARE = 108
 
 PLACE = {
-    "prod0": 0, "rounded12": 2 * KB, "codes10": 3 * KB + 512, "mag00": 4 * KB, "h10": 4 * KB,
+    "prod0": 0, "rounded12": KB + 512, "codes100": 3 * KB, "codes101": 4 * KB, "mag00": 4 * KB, "h10": 4 * KB,
     "h00": 8 * KB, "whole0": 8 * KB,
     "high1": 45 * KB, "pair_codes": 46 * KB, "recip0": 47 * KB,
     "low1": 13 * KB + 512, "root00": 15 * KB, "codes_c": 15 * KB + 512, "codes20": 16 * KB + 512,
@@ -281,8 +282,7 @@ def tile_list_hit_segment_energy_kernel(
                 energy = raw_last[:, e0 : e0 + 2 * PARTS].rearrange("p (v j) -> p v j", v=2)
                 nc.scalar.activation(energy, y_bank[c, u][:], ACT.Square)
                 dst = out[2 * u * PARTS : 2 * (u + 1) * PARTS, c * PARTS : (c + 1) * PARTS]
-                queue = nc.scalar if (c, u) == (QUARTERS - 1, 1) else nc.sync
-                queue.dma_start(out=dst.rearrange("(n p) j -> p n j", p=PARTS), in_=energy)
+                nc.sync.dma_start(out=dst.rearrange("(n p) j -> p n j", p=PARTS), in_=energy)
 
         unused = keep.tile([PARTS, 2], F32, name="unused")
         nc.gpsimd.memset(unused[:, 0:1], 1.0)
@@ -306,7 +306,8 @@ def tile_list_hit_segment_energy_kernel(
                 h_pass(0, s, a)
         rounded[1, 0] = tile([PARTS, PACK * NARROW], BF16, "rounded10")[:]
         nc.vector.tensor_copy(*narrow_views(rounded[1, 0], raw[1, 0]))
-        quantize_w1("codes10", [rounded[1, 0]], [(1, 0, 0), (1, 1, 0)])
+        for s in range(2):
+            quantize_w1("codes10%d" % s, [halves(rounded[1, 0])[s]], [(1, s, 0)])
         for s in range(2):
             evacuate(0, s)
             h_pass(1, s, 0)
@@ -318,8 +319,8 @@ def tile_list_hit_segment_energy_kernel(
         narrow_gpsimd(rounded[1, 2], raw[1, 2], 0, 2 * SHARE)
         nc.scalar.copy(*narrow_views(rounded[1, 2], raw[1, 2], SHARE, HALF))
         quantize_w1("pair_codes", [rounded[1, 1], rounded[1, 2]], [(1, s, a) for a in range(1, PASSES) for s in range(2)])
-        for a in range(1, PASSES):
-            for s in range(2):
+        for s in range(2):
+            for a in range(1, PASSES):
                 h_pass(1, s, a)
         prod[0] = tile([PARTS, 2, P], F32, "prod0")[:]
         for s in range(2):
@@ -336,9 +337,13 @@ def tile_list_hit_segment_energy_kernel(
 
         whole0 = tile([PARTS, PACK * K_PASS], BF16, "whole0")
         nc.gpsimd.tensor_scalar(
-            whole0[:].rearrange("p (t m j) -> p m t j", t=PACK, j=PACK),
-            raw[2, 0].rearrange("p (j m t) -> p m t j", j=PACK, t=PACK),
+            whole0[:].rearrange("p (t m j) -> p m t j", t=PACK, j=PACK)[:, 0:WIDE_SHARE],
+            raw[2, 0].rearrange("p (j m t) -> p m t j", j=PACK, t=PACK)[:, 0:WIDE_SHARE],
             1.0, 0.0, MULT, ADD,
+        )
+        nc.scalar.copy(
+            whole0[:].rearrange("p (t m j) -> p m j t", t=PACK, j=PACK)[:, WIDE_SHARE:],
+            raw[2, 0].rearrange("p (j m t) -> p m j t", j=PACK, t=PACK)[:, WIDE_SHARE:],
         )
         reciprocal_narrow(0)
         high = {a: tile([PARTS, 2 * K_PASS], BF16, "high%d" % a) for a in range(1, PASSES)}
@@ -362,7 +367,7 @@ def tile_list_hit_segment_energy_kernel(
         pick_second(1, 0)
         band_vector(low[2][:], raw[2, 2])
         quantize_w1("codes_d", [high[1][:]], [(2, s, 1) for s in range(2, PACK)])
-        quantize_w1("codes_b", [low[2][:]], [(2, s, 2) for s in range(2)])
+        quantize_w1("codes_b", halves(low[2][:]), [(2, s, 2) for s in range(2)])
         for s in range(2):
             h_pass(2, s, 2)
         pick_second(1, 1)

@@ -30,7 +30,7 @@ GROUP = 16
 NARROW = K_PASS // 2
 KB = 1024
 SHARE = 24
-WIDE_SHARE = 108
+WIDE_SHARE = 100
 
 PLACE = {
     "prod0": 0, "rounded12": KB + 512, "codes100": 3 * KB, "codes101": 4 * KB, "mag00": 4 * KB, "h10": 4 * KB,
@@ -419,16 +419,16 @@ def tile_list_hit_segment_energy_kernel(
         for c in range(2):
             y_pass(0, c)
         form_z(0)
-        weave_z(1)
         reciprocal(2)
+        weave_z(1)
         reciprocal(3)
         form_z(1)
         finish(0)
-        quantize_z(0, P // 2, P)
-        for c in range(2, QUARTERS):
-            y_pass(0, c)
-        form_z(2)
         finish(1)
+        form_z(2)
+        quantize_z(0, P // 2, P)
+        y_pass(0, 2)
         finish(2)
+        y_pass(0, 3)
         form_z(3)
         finish(3)

@@ -61,6 +61,9 @@ def tile_list_hit_segment_energy_kernel(
                 return placed.tile(shape, dtype, name=name, align_bytes=64, offset=PLACE[name])
             return keep.tile(shape, dtype, name=name, align_bytes=64)
 
+        def banks(name, first_bank, shape):
+            return psum.tile(shape, F32, name=name, offset=first_bank * 2 * KB)
+
         def rows(ap):
             return ap.rearrange("p (r j) -> p r j", j=P)
 
@@ -170,12 +173,17 @@ def tile_list_hit_segment_energy_kernel(
         def h_pass(g, s, a):
             first_bank = 2 * (s % 2) + (4 if g == 2 else 0)
             codes, scales = weights[g, s, a]
+            if a == 0 and (g, s) == (1, 1):
+                pair = banks("h_banks11", first_bank, [PARTS, 2, BANK])
+                for half in range(2):
+                    h_bank[g, s, half] = pair[:, half, :]
+            elif a == 0:
+                for half in range(2):
+                    h_bank[g, s, half] = banks("h_bank%d%d%d" % (g, s, half), first_bank + half, [PARTS, BANK])[:]
             for half in range(2):
-                if a == 0:
-                    h_bank[g, s, half] = psum.tile([PARTS, BANK], F32, name="bank%d" % (first_bank + half))
                 cols = slice(half * BANK, (half + 1) * BANK)
                 nc.tensor.matmul_mx(
-                    out=h_bank[g, s, half][:],
+                    out=h_bank[g, s, half],
                     lhsT=codes.bitcast(FP8X4),
                     lhsT_scale=scales,
                     rhs=hit[a][:, cols].bitcast(FP8X4),
@@ -203,7 +211,7 @@ def tile_list_hit_segment_energy_kernel(
         def evacuate(g, s):
             h_t[g, s] = tile([PARTS, S], F32, "h%d%d" % (g, s))
             for half in range(2):
-                nc.scalar.copy(h_t[g, s][:, half * BANK : (half + 1) * BANK], h_bank[g, s, half][:])
+                nc.scalar.copy(h_t[g, s][:, half * BANK : (half + 1) * BANK], h_bank[g, s, half])
 
         def pick_first(g, s):
             nc.vector.tensor_copy(first[g][:, s, :], h_t[g, s][:].indirect(pos1_t[:]))
@@ -263,7 +271,7 @@ def tile_list_hit_segment_energy_kernel(
             cols = slice(c * PARTS, (c + 1) * PARTS)
             for u in range(2):
                 if b == 0:
-                    y_bank[c, u] = psum.tile([PARTS, 2, PARTS], F32, name="bank%d" % (2 * (c % (QUARTERS - 1)) + u))
+                    y_bank[c, u] = banks("y_bank%d%d" % (c, u), 2 * (c % (QUARTERS - 1)) + u, [PARTS, 2, PARTS])
                 for v in range(2):
                     n = 2 * u + v
                     nc.tensor.matmul_mx(

from contextlib import ExitStack

import concourse.mybir as mybir

K, T, S, P, H, N = 1536, 2048, 1024, 512, 1024, 512
FLOPS = 2 * K * H * S + 2 * H * N * P

F32 = mybir.dt.float32
BF16 = mybir.dt.bfloat16
I32 = mybir.dt.int32
U32 = mybir.dt.uint32
U16 = mybir.dt.uint16
U8 = mybir.dt.uint8
FP8X4 = mybir.dt.float8_e4m3fn_x4
FP4X4 = mybir.dt.float4_e2m1fn_x4
ACT = mybir.ActivationFunctionType
MULT = mybir.AluOpType.mult
ADD = mybir.AluOpType.add

PARTS = 128
HALF = PARTS // 2
PACK = 4
K_PASS = PARTS * PACK
PASSES = K // K_PASS
BANDS = H // K_PASS
BANK = 512
QUADRANTS = 4
QUARTERS = P // PARTS
GROUP = 16
NARROW = K_PASS // 2
KB = 1024
SHARE = 24
WIDE_SHARE = 100

PLACE = {
    "prod0": 0, "rounded12": KB + 512, "codes100": 3 * KB, "codes101": 4 * KB, "mag00": 4 * KB, "h10": 4 * KB,
    "h00": 8 * KB, "whole0": 8 * KB,
    "high1": 45 * KB, "pair_codes": 46 * KB, "recip0": 47 * KB,
    "low1": 13 * KB + 512, "root00": 15 * KB, "codes_c": 15 * KB + 512, "codes20": 16 * KB + 512,
    "root01": 18 * KB, "high2": 18 * KB,
    "low2": 20 * KB, "mag10": 21 * KB, "codes_d": 22 * KB,
    "h11": 23 * KB, "pairs0": 23 * KB,
    "codes_b": 27 * KB, "recip1": 27 * KB,
    "codes_e": 31 * KB, "root2": 31 * KB,
    "h20": 39 * KB, "pairs10": 39 * KB, "pairs11": 40 * KB,
    "rounded02": 51 * KB, "rounded10": 51 * KB, "rounded11": 51 * KB,
}


def tile_list_hit_segment_energy_kernel(
    tc, tab_words, tab_scales, offs, w1, pos1, pos2, knee, w2_words, w2_scales, out
):
    nc = tc.nc
    with ExitStack() as ctx:
        keep = ctx.enter_context(tc.tile_pool(name="keep", bufs=1))
        placed = ctx.enter_context(tc.tile_pool(name="placed", bufs=1))
        psum = ctx.enter_context(tc.psum_pool(name="psum", bufs=1))

        def tile(shape, dtype, name):
            if name in PLACE:
                return placed.tile(shape, dtype, name=name, align_bytes=64, offset=PLACE[name])
            return keep.tile(shape, dtype, name=name, align_bytes=64)

        def banks(name, first_bank, shape):
            return psum.tile(shape, F32, name=name, offset=first_bank * 2 * KB)

        def rows(ap):
            return ap.rearrange("p (r j) -> p r j", j=P)

        offs_t = keep.tile([PARTS, S // GROUP], U16, name="offs_t")
        pos1_t = keep.tile([PARTS, P // GROUP], U16, name="pos1_t")
        pos2_t = keep.tile([PARTS, P // GROUP], U16, name="pos2_t")
        knee_half = keep.tile([PARTS, 2, 2], F32, name="knee_half")
        knee_band = keep.tile([PARTS, PACK], F32, name="knee_band")
        tab = [tile([PARTS, T], I32, "tab%d" % a) for a in range(PASSES)]
        tab_sc = tile([PARTS, T], U8, "tab_sc")
        hit = [tile([PARTS, S], U32, "hit%d" % a) for a in range(PASSES)]
        hit_sc = tile([PARTS, S], U8, "hit_sc")
        w2_w = tile([PARTS, BANDS, 2 * N], U8, "w2_w")
        w2_sc = tile([PARTS, BANDS, N], U8, "w2_sc")

        raw = {}
        for g in range(2):
            for a in range(PASSES):
                raw[g, a] = tile([PARTS, PACK * NARROW], F32, "raw%d%d" % (g, a))[:]
        raw[2, 0] = tile([PARTS, PACK * K_PASS], F32, "raw20")[:]
        raw_last = tile([PARTS, 2 * PACK * K_PASS], F32, "raw_last")
        for a in range(1, PASSES):
            raw[2, a] = raw_last[:, (a - 1) * PACK * K_PASS : a * PACK * K_PASS]

        def load_tab(a):
            nc.sync.dma_start(out=tab[a][:], in_=tab_words[a].rearrange("p t i -> p (t i)").bitcast(I32))

        def load_w1(g, a):
            width = K_PASS if g == 2 else NARROW
            src = w1[a * K_PASS : (a + 1) * K_PASS, g * NARROW : g * NARROW + width]
            nc.sync.dma_start(
                out=raw[g, a].rearrange("p (j c) -> p j c", j=PACK), in_=src.rearrange("(p j) c -> p j c", j=PACK)
            )

        nc.vector.memset(tab_sc[:].bitcast(I32), 0)
        nc.vector.memset(w2_sc[:].rearrange("p b n -> p (b n)").bitcast(I32), 0)
        load_tab(0)
        nc.sync.dma_start(offs_t[:], offs)
        load_w1(0, 0)
        for q in range(QUADRANTS):
            nc.sync.dma_start(
                out=tab_sc[32 * q : 32 * q + 4 * PASSES, :].bitcast(I32),
                in_=tab_scales[:, 4 * q : 4 * q + 4, :].bitcast(I32),
            )
        for a in range(1, PASSES):
            load_tab(a)
            load_w1(0, a)
        nc.sync.dma_start(pos1_t[:], pos1)
        for a in range(PASSES):
            load_w1(1, a)
        nc.sync.dma_start(out=knee_half[:], in_=knee[0:K_PASS].rearrange("(g q s) -> q g s", g=2, s=2))
        nc.sync.dma_start(pos2_t[:], pos2)
        for a in range(PASSES):
            load_w1(2, a)
        nc.sync.dma_start(out=knee_band[:], in_=knee[K_PASS:].rearrange("(p t) -> p t", t=PACK))
        nc.sync.dma_start(out=w2_w[:].bitcast(I32), in_=w2_words.rearrange("b p n -> p b n").bitcast(I32))
        for q in range(QUADRANTS):
            nc.sync.dma_start(
                out=w2_sc[32 * q : 32 * q + 4, :, :].bitcast(I32),
                in_=w2_scales[:, 4 * q : 4 * q + 4, :].rearrange("b r n -> r b n").bitcast(I32),
            )

        def gather_hits(a):
            nc.vector.tensor_copy(hit[a][:], tab[a][:].bitcast(U32).indirect(offs_t[:]))

        def narrow_views(rounded, piece, m0=0, m1=HALF):
            dst = rounded.rearrange("p (s m u j) -> p m j u s", s=2, u=2, j=PACK)
            src = piece.rearrange("p (j m u s) -> p m j u s", j=PACK, u=2, s=2)
            return dst[:, m0:m1], src[:, m0:m1]

        def narrow_gpsimd(rounded, piece, q0, q1):
            dst = rounded.rearrange("p (s q j) -> p q s j", s=2, j=PACK)
            src = piece.rearrange("p (j q s) -> p q s j", j=PACK, s=2)
            nc.gpsimd.tensor_scalar(dst[:, q0:q1], src[:, q0:q1], 1.0, 0.0, MULT, ADD)

        def band_scalar(rounded, piece, t0):
            dst = rounded.rearrange("p (t m j) -> p m j t", t=2, j=PACK)
            src = piece.rearrange("p (j m t) -> p m j t", j=PACK, t=PACK)
            nc.scalar.copy(dst, src[:, :, :, t0 : t0 + 2])

        def band_vector(rounded, piece):
            dst = rounded.rearrange("p (t m j) -> p m j t", t=2, j=PACK)
            src = piece.rearrange("p (j m t) -> p m j t", j=PACK, t=PACK)
            nc.vector.tensor_copy(dst, src[:, :, :, 0:2])

        def quantize(codes, scales, rounded):
            nc.vector.quantize_mx(out=codes.bitcast(FP8X4), scales=scales, in_=rounded)

        def halves(ap):
            width = ap.shape[1] // 2
            return [ap[:, 0:width], ap[:, width:]]

        weights = {}

        def quantize_w1(name, parts, units):
            width = len(units) * PARTS
            codes = tile([PARTS, width], U32, name)
            scales = tile([PARTS, width], U8, name + "_sc")
            step = width // len(parts)
            for i, part in enumerate(parts):
                quantize(codes[:, i * step : (i + 1) * step], scales[:, i * step : (i + 1) * step], part)
            for u, unit in enumerate(units):
                weights[unit] = (codes[:, u * PARTS : (u + 1) * PARTS], scales[:, u * PARTS : (u + 1) * PARTS])

        h_bank = {}

        def h_pass(g, s, a):
            first_bank = 2 * (s % 2) + (4 if g == 2 else 0)
            codes, scales = weights[g, s, a]
            if a == 0 and (g, s) == (1, 1):
                pair = banks("h_banks11", first_bank, [PARTS, 2, BANK])
                for half in range(2):
                    h_bank[g, s, half] = pair[:, half, :]
            elif a == 0:
                for half in range(2):
                    h_bank[g, s, half] = banks("h_bank%d%d%d" % (g, s, half), first_bank + half, [PARTS, BANK])[:]
            for half in range(2):
                cols = slice(half * BANK, (half + 1) * BANK)
                nc.tensor.matmul_mx(
                    out=h_bank[g, s, half],
                    lhsT=codes.bitcast(FP8X4),
                    lhsT_scale=scales,
                    rhs=hit[a][:, cols].bitcast(FP8X4),
                    rhs_scale=hit_sc[4 * a :, cols],
                    start=(a == 0),
                    stop=(a == PASSES - 1),
                )

        h_t = {}
        first = [tile([PARTS, 2 if g < 2 else PACK, P], F32, "first%d" % g)[:] for g in range(3)]
        prod = {2: tile([PARTS, PACK, P], F32, "prod2")[:]}
        mag = {}
        for s in range(2):
            mag[0, s] = rows(raw[0, 0])[:, s, :]
            mag[1, s] = rows(raw[0, 1])[:, s, :]
            mag[2, s] = prod[2][:, 2 + s, :]
            mag[2, 2 + s] = rows(raw[0, 2])[:, s, :]
        root = {(1, s): prod[2][:, s, :] for s in range(2)}
        recip = {2: rows(raw[2, 0])}
        z_words = [tile([PARTS, 2, P], BF16, "z_words%d" % half) for half in range(2)]
        z_bf = [tile([PARTS, P, PACK], BF16, "z_bf%d" % b) for b in range(BANDS)]
        z_codes = [tile([PARTS, P], U32, "z_codes%d" % b) for b in range(BANDS)]
        z_sc = [tile([PARTS, P], U8, "z_sc%d" % b) for b in range(BANDS)]

        def evacuate(g, s):
            h_t[g, s] = tile([PARTS, S], F32, "h%d%d" % (g, s))
            for half in range(2):
                nc.scalar.copy(h_t[g, s][:, half * BANK : (half + 1) * BANK], h_bank[g, s, half])

        def pick_first(g, s):
            nc.vector.tensor_copy(first[g][:, s, :], h_t[g, s][:].indirect(pos1_t[:]))

        def pick_second(g, s):
            nc.vector.tensor_tensor(prod[g][:, s, :], h_t[g, s][:].indirect(pos2_t[:]), first[g][:, s, :], MULT)

        def magnitude(g, s):
            nc.scalar.activation(mag[g, s], first[g][:, s, :], ACT.Abs)

        def inverse_root(g, s):
            bias = knee_half[:, g, s : s + 1] if g < 2 else knee_band[:, s : s + 1]
            nc.scalar.activation(root[g, s], mag[g, s], ACT.Abs_reciprocal_sqrt, bias=bias)

        def reciprocal_narrow(g):
            recip[g] = tile([PARTS, 2, P], F32, "recip%d" % g)[:]
            for s in range(2):
                nc.scalar.activation(recip[g][:, s, :], root[g, s], ACT.Square)

        def form_pairs(g, name, j0, j1):
            pairs = tile([PARTS, j1 - j0, 2], BF16, name)
            nc.gpsimd.tensor_tensor(
                pairs[:].rearrange("p (c i) s -> p c s i", i=4),
                prod[g][:, :, j0:j1].rearrange("p s (c i) -> p c s i", i=4),
                recip[g][:, :, j0:j1].rearrange("p s (c i) -> p c s i", i=4),
                MULT,
            )
            for c0 in range(j0, j1, P // 2):
                for u in range(2):
                    nc.sync.dma_start(
                        out=z_words[c0 // (P // 2)][g * HALF : (g + 1) * HALF, u, :],
                        in_=pairs[u:PARTS:2, c0 - j0 : c0 - j0 + P // 2, :].rearrange("p j s -> p (j s)"),
                    )

        def weave_z(half):
            woven = z_bf[0][:, half * (P // 2) : (half + 1) * (P // 2), :].rearrange("p j t -> p (j t)")
            nc.scalar.copy(
                woven.bitcast(U32).rearrange("p (c i u) -> p c u i", i=2, u=2),
                z_words[half][:].bitcast(U32).rearrange("p u (c i) -> p c u i", i=2),
            )

        def form_z(c):
            cols = slice(c * PARTS, (c + 1) * PARTS)
            nc.vector.tensor_tensor(
                z_bf[1][:, cols, :].rearrange("p (c i) t -> p c t i", i=4),
                prod[2][:, :, cols].rearrange("p t (c i) -> p c t i", i=4),
                recip[2][:, :, cols].rearrange("p t (c i) -> p c t i", i=4),
                MULT,
            )

        def quantize_z(b, j0, j1):
            quantize(z_codes[b][:, j0:j1], z_sc[b][:, j0:j1], z_bf[b][:, j0:j1, :].rearrange("p j t -> p (j t)"))

        y_bank = {}

        def y_pass(b, c):
            cols = slice(c * PARTS, (c + 1) * PARTS)
            for u in range(2):
                if b == 0:
                    y_bank[c, u] = banks("y_bank%d%d" % (c, u), 2 * (c % (QUARTERS - 1)) + u, [PARTS, 2, PARTS])
                for v in range(2):
                    n = 2 * u + v
                    nc.tensor.matmul_mx(
                        out=y_bank[c, u][:, v, :],
                        lhsT=w2_w[:, b, 2 * n * PARTS : 2 * (n + 1) * PARTS].bitcast(FP4X4),
                        lhsT_scale=w2_sc[:, b, n * PARTS : (n + 1) * PARTS],
                        rhs=z_codes[b][:, cols].bitcast(FP8X4),
                        rhs_scale=z_sc[b][:, cols],
                        start=(b == 0 and v == 0),
                        stop=(b == BANDS - 1 and v == 1),
                    )

        def store(c):
            for u in range(2):
                e0 = (2 * c + u) * 2 * PARTS
                energy = raw_last[:, e0 : e0 + 2 * PARTS].rearrange("p (v j) -> p v j", v=2)
                nc.scalar.activation(energy, y_bank[c, u][:], ACT.Square)
                dst = out[2 * u * PARTS : 2 * (u + 1) * PARTS, c * PARTS : (c + 1) * PARTS]
                nc.sync.dma_start(out=dst.rearrange("(n p) j -> p n j", p=PARTS), in_=energy)

        unused = keep.tile([PARTS, 2], F32, name="unused")
        nc.gpsimd.memset(unused[:, 0:1], 1.0)
        nc.scalar.activation(unused[:, 1:2], unused[:, 0:1], ACT.Abs_reciprocal_sqrt)

        gather_hits(0)
        nc.vector.tensor_copy(hit_sc[:], tab_sc[:].indirect(offs_t[:]))
        rounded = {}
        for a in range(PASSES):
            if a > 0:
                gather_hits(a)
            rounded[0, a] = tile([PARTS, PACK * NARROW], BF16, "rounded0%d" % a)[:]
            if a < PASSES - 1:
                nc.scalar.copy(*narrow_views(rounded[0, a], raw[0, a]))
            else:
                narrow_gpsimd(rounded[0, a], raw[0, a], 0, 2 * SHARE)
                nc.scalar.copy(*narrow_views(rounded[0, a], raw[0, a], SHARE, HALF))
            parts = halves(rounded[0, a]) if a == PASSES - 1 else [rounded[0, a]]
            quantize_w1("codes0%d" % a, parts, [(0, 0, a), (0, 1, a)])
            for s in range(2):
                h_pass(0, s, a)
        rounded[1, 0] = tile([PARTS, PACK * NARROW], BF16, "rounded10")[:]
        nc.vector.tensor_copy(*narrow_views(rounded[1, 0], raw[1, 0]))
        for s in range(2):
            quantize_w1("codes10%d" % s, [halves(rounded[1, 0])[s]], [(1, s, 0)])
        for s in range(2):
            evacuate(0, s)
            h_pass(1, s, 0)
            pick_first(0, s)

        for a in range(1, PASSES):
            rounded[1, a] = tile([PARTS, PACK * NARROW], BF16, "rounded1%d" % a)[:]
        narrow_gpsimd(rounded[1, 1], raw[1, 1], 0, PARTS)
        narrow_gpsimd(rounded[1, 2], raw[1, 2], 0, 2 * SHARE)
        nc.scalar.copy(*narrow_views(rounded[1, 2], raw[1, 2], SHARE, HALF))
        quantize_w1("pair_codes", [rounded[1, 1], rounded[1, 2]], [(1, s, a) for a in range(1, PASSES) for s in range(2)])
        for s in range(2):
            for a in range(1, PASSES):
                h_pass(1, s, a)
        prod[0] = tile([PARTS, 2, P], F32, "prod0")[:]
        for s in range(2):
            pick_second(0, s)
        mag[0, 0] = tile([PARTS, P], F32, "mag00")[:]
        for s in range(2):
            magnitude(0, s)
        for s in range(2):
            root[0, s] = tile([PARTS, P], F32, "root0%d" % s)[:]
            inverse_root(0, s)
        for s in range(2):
            evacuate(1, s)
            pick_first(1, s)

        whole0 = tile([PARTS, PACK * K_PASS], BF16, "whole0")
        nc.gpsimd.tensor_scalar(
            whole0[:].rearrange("p (t m j) -> p m t j", t=PACK, j=PACK)[:, 0:WIDE_SHARE],
            raw[2, 0].rearrange("p (j m t) -> p m t j", j=PACK, t=PACK)[:, 0:WIDE_SHARE],
            1.0, 0.0, MULT, ADD,
        )
        nc.scalar.copy(
            whole0[:].rearrange("p (t m j) -> p m j t", t=PACK, j=PACK)[:, WIDE_SHARE:],
            raw[2, 0].rearrange("p (j m t) -> p m j t", j=PACK, t=PACK)[:, WIDE_SHARE:],
        )
        reciprocal_narrow(0)
        high = {a: tile([PARTS, 2 * K_PASS], BF16, "high%d" % a) for a in range(1, PASSES)}
        low = {a: tile([PARTS, 2 * K_PASS], BF16, "low%d" % a) for a in range(1, PASSES)}
        band_scalar(high[1][:], raw[2, 1], 2)
        mag[1, 0] = tile([PARTS, P], F32, "mag10")[:]
        for s in range(2):
            magnitude(1, s)
        inverse_root(1, 0)
        band_scalar(high[2][:], raw[2, 2], 2)
        inverse_root(1, 1)
        quantize_w1("codes20", halves(whole0[:])[:1], [(2, s, 0) for s in range(2)])
        for s in range(2):
            h_pass(2, s, 0)
        band_vector(low[1][:], raw[2, 1])
        quantize_w1("codes_c", halves(whole0[:])[1:], [(2, s, 0) for s in range(2, PACK)])
        quantize_w1("codes_a", [low[1][:]], [(2, s, 1) for s in range(2)])
        for s in range(2):
            h_pass(2, s, 1)
        prod[1] = rows(raw_last[:, PACK * K_PASS - P : PACK * K_PASS + P])
        pick_second(1, 0)
        band_vector(low[2][:], raw[2, 2])
        quantize_w1("codes_d", [high[1][:]], [(2, s, 1) for s in range(2, PACK)])
        quantize_w1("codes_b", halves(low[2][:]), [(2, s, 2) for s in range(2)])
        for s in range(2):
            h_pass(2, s, 2)
        pick_second(1, 1)
        quantize_w1("codes_e", [high[2][:]], [(2, s, 2) for s in range(2, PACK)])
        form_pairs(0, "pairs0", 0, P)

        for s in range(2):
            evacuate(2, s)
            for a in range(PASSES - 1):
                h_pass(2, s + 2, a)
            pick_first(2, s)
        for s in range(2, PACK):
            h_pass(2, s, PASSES - 1)
        reciprocal_narrow(1)
        for s in range(2):
            pick_second(2, s)
        for half in range(2):
            form_pairs(1, "pairs1%d" % half, half * (P // 2), (half + 1) * (P // 2))
        for s in range(2):
            magnitude(2, s)
        for s in range(2, PACK):
            evacuate(2, s)
            pick_first(2, s)
        root2 = tile([PARTS, PACK, P], F32, "root2")
        for s in range(PACK):
            root[2, s] = root2[:, s, :]
        for s in range(2):
            inverse_root(2, s)
        for s in range(2, PACK):
            pick_second(2, s)
        for s in range(2, PACK):
            magnitude(2, s)
        for s in range(2, PACK):
            inverse_root(2, s)

        def reciprocal(c):
            cols = slice(c * PARTS, (c + 1) * PARTS)
            nc.scalar.activation(recip[2][:, :, cols], root2[:, :, cols], ACT.Square)

        def finish(c):
            quantize_z(1, c * PARTS, (c + 1) * PARTS)
            y_pass(1, c)
            store(c)

        weave_z(0)
        reciprocal(0)
        reciprocal(1)
        quantize_z(0, 0, P // 2)
        for c in range(2):
            y_pass(0, c)
        form_z(0)
        reciprocal(2)
        weave_z(1)
        reciprocal(3)
        form_z(1)
        finish(0)
        finish(1)
        form_z(2)
        quantize_z(0, P // 2, P)
        y_pass(0, 2)
        finish(2)
        y_pass(0, 3)
        form_z(3)
        finish(3)
